import numpy as np, ml_dtypes
CORES = [40,41,42,43,44,45,46,47]
N = 8
BF = ml_dtypes.bfloat16
def gentries(a):
    return np.ascontiguousarray(a.reshape(8, 16, -1).transpose(0, 2, 1)).reshape(8, -1)
def gtable(e):
    e = np.asarray(e); return np.ascontiguousarray(e.reshape(8, -1, 16).transpose(0, 2, 1)).reshape(128, -1).astype(np.int32)
CN, Q0, S, H, RO, EPS, RHO = 3072, 1024, 160, 96, 4, 36, 52
LN = S + H
def pick4(w, ix):
    return np.take_along_axis(w, ix[:, :, None, :], 3)
def noise(rng, m, shape):
    return np.rint((2 * rng.random(shape) - 1) * m).astype(np.int64)
def clip(v):
    return np.minimum(np.maximum(v, 0), 15)
def pos(rng, lo, hi, *shape):
    return (lo + (hi - lo) * rng.random(shape, dtype=np.float32)).astype(BF)
def split(rng, T, m, c):
    r = rng.random(T.shape + (m * c,)); lim = np.take_along_axis(np.sort(r, axis=-1), (T - 1)[..., None], -1)
    return np.moveaxis(np.add.reduce((r <= lim).astype(np.int64).reshape(T.shape + (m, c)), axis=-1), -1, -2)
def parts(rng):
    K = rng.integers(0, 16, (N, 8, 16, Q0)); nb = rng.integers(0, Q0, (N, 8, 16, Q0))
    me = (np.arange(16)[:, None] == rng.integers(0, 16, (N, 8, 1, Q0))) & (rng.random((N, 8, 1, Q0)) < 0.75)
    nb = np.where(me, np.arange(Q0), nb)
    pm = np.argsort(rng.random((N, 8, Q0)), axis=-1); inv = np.argsort(pm, axis=-1)
    home = np.ascontiguousarray(np.tile(pm, (1, 1, CN // Q0 + 1))[..., :CN])
    C = clip(pick4(K, home) + noise(rng, rng.integers(0, 4, (N, 8, 1, CN)), (N, 8, 16, CN)))
    near = inv[:, :, None, :] + Q0 * rng.integers(0, CN // Q0, (N, 8, 16, Q0))
    dl = np.where(rng.random((N, 8, 16, Q0)) < 0.45, near, rng.integers(0, CN, (N, 8, 16, Q0)))
    st = np.take_along_axis(np.argsort(rng.random((N, 8, Q0)), axis=-1), (Q0 * rng.random((N, 8, LN)) ** 2).astype(np.int64), 2)
    j = st[..., :S]; xs = np.zeros((N, 8, 16, RO, S), np.int64); x = None
    for t in range(RO):
        go = np.take_along_axis(pick4(nb, j), rng.integers(0, 16, (N, 8, 1, S)), 2)[:, :, 0]
        stay = (rng.random((N, 8, S)) < 0.5) & (t > 0); j = np.where(stay, j, go)
        z = clip(pick4(K, j) + noise(rng, rng.choice(np.array([1, 3, 5, 8, 12]), (N, 8, 1, S)), (N, 8, 16, S)))
        x = z if x is None else np.where(stay[:, :, None, :], clip(x + noise(rng, 1, x.shape)), z)
        xs[:, :, :, t] = x
    return {"kq": K, "nb": nb, "dl": dl, "cc": C, "aa": pos(rng, 16, 128, N, 8, 16, CN), "xs": xs, "ys": pos(rng, 64, 1024, N, 8, 16, RO, S), "st": st}
def pack(p):
    d = {}
    for k in ("kq", "nb", "dl", "cc", "aa", "xs", "ys"):
        d[k] = np.ascontiguousarray(p[k].reshape(N, 128, -1)).astype(np.int32 if k in ("nb", "dl") else BF)
    d["st"] = np.stack([gtable(a) for a in p["st"]]); return d
def setup_inputs(rng):
    return pack(parts(rng))
def relay(rng, p, pat, g):
    m = H // 3; n = H - 2 * m; X = p["xs"][:, g]
    for a in range(N):
        c = np.zeros((RO, S), np.int64); c[0, :m] = 1; c[1:, :m] = 2; c[:2, m:H] = 4 + a; c[2:, m:H] = 4 + (a - 1) % N
        X[a] = pat[:, c] + rng.integers(-1, 2, (16, RO, S)); X[a, :, 2, :m] = rng.integers(14, 16, (16, m))
    for a in range(N):
        st = rng.permutation(Q0)[:LN]; own, gst = st[:S], st[S:]; p["st"][a, g] = st
        nb = p["nb"][a, g]; nb[:] = np.arange(Q0); nb[1::2][:, own[:H]] = gst
        o = rng.permutation(CN); h = CN // 4; be, b2, b1, b0 = o[:n], o[n:h], o[h:2 * h], o[2 * h:]
        c = p["cc"][a, g]; c[:, b0] = 2 + rng.integers(-1, 2, (16, b0.size)); c[:, b1] = rng.integers(14, 16, (16, b1.size))
        c[:, b2] = pat[:, 2:3] + rng.integers(-1, 2, (16, b2.size))
        x = X[(a - 1) % N, :, 0, 2 * m:H]; z = split(rng, np.full(n, EPS), 16, 4); c[:, be] = np.where(x > 7, x - z, x + z)
        w = np.concatenate([rng.choice(b1, (8, H)), rng.choice(b2, (2, H)), rng.choice(b0, (6, H))]); w[15, 2 * m:] = be
        dl = p["dl"][a, g]; dl[:, own] = rng.choice(b0, (16, S)); dl[:, gst] = rng.permuted(w, axis=0)
        k = p["kq"][a, g]; k[:, own[:m]] = 2; k[:, gst[:m]] = 15
        k[:, own[m:H]] = pat[:, 4 + a][:, None]; k[:, gst[m:]] = pat[:, 4 + (a - 1) % N][:, None]
def far(rng, p, g):
    v = np.exp(-0.015625 * np.arange(EPS + 1, EPS + 9)); far_d = EPS + 1 + int(np.argmax(np.abs(v.astype(BF).astype(np.float64) - v)))
    u = rng.integers(0, 16, (N, 16, 4)); b = np.arange(H) % 4; n = CN // 8
    for a in range(N):
        me, up = u[a], u[(a - 1) % N]
        st = rng.permutation(Q0)[:LN]; own, gst = st[:H], st[S:]; p["st"][a, g] = st
        nb = p["nb"][a, g]; nb[:] = np.arange(Q0); nb[1::2][:, own] = gst
        k = p["kq"][a, g]; k[:, own] = me[:, b]; k[:, gst] = up[:, b]
        X = p["xs"][a, g]; X[:, :2, :H] = me[:, b][:, None, :]; X[:, 2:, :H] = up[:, b][:, None, :]
        Y = p["ys"][a, g]; Y[:, 0, :H] = pos(rng, 1800, 2048, 16, H).astype(np.float32); Y[:, 1:, :H] = pos(rng, 128, 1024, 16, RO - 1, H).astype(np.float32)
        o = rng.permutation(CN)
        for i in range(4):
            c1, c2 = o[2 * i * n:(2 * i + 1) * n], o[(2 * i + 1) * n:(2 * i + 2) * n]
            for x, ix, T, q, lo, hi in ((me[:, i:i + 1], c1, np.full(n, far_d), own[i::4], 124, 128), (up[:, i:i + 1], c2, rng.integers(EPS + 1, 61, n), gst[i::4], 16, 32)):
                z = split(rng, T, 16, 4); p["cc"][a, g][:, ix] = np.where(x > 7, x - z, x + z)
                p["aa"][a, g][:, ix] = pos(rng, lo, hi, 16, n).astype(np.float32)
                p["dl"][a, g][:, q] = rng.choice(ix, (16, q.size))
def setup_inputs_corners(rng):
    p = parts(rng); off = int(rng.integers(0, 8)); vals = (0, 1, 2, 3, H - 1, H, H + 1, S)
    pat = 2 + 10 * np.array([[bin(f & j).count("1") & 1 for j in range(16)] for f in range(16)])
    for a in range(N):
        for g in range(8):
            st = rng.permutation(Q0)[:LN]; own, gst = st[:S], st[S:]; p["st"][a, g] = st
            nb = p["nb"][a, g]; nb[:] = np.arange(Q0); nb[1::2][:, own[:H]] = gst
            o = rng.permutation(CN); h = CN // 2; b0, b1, b2 = o[:h], o[h:h + h // 2], o[h + h // 2:]
            c = p["cc"][a, g]; c[:, b0] = 2 + rng.integers(-1, 2, (16, b0.size)); c[:, b1] = rng.integers(14, 16, (16, b1.size))
            c[:, b2] = pat[:, 1 + np.arange(b2.size) % (RO - 1)] + rng.integers(-1, 2, (16, b2.size))
            dl = p["dl"][a, g]; dl[:, own] = rng.choice(b0, (16, S))
            w = [rng.choice(b1, (8, H))] + [rng.choice(b2[t::RO - 1], (1, H)) for t in range(RO - 1)] + [rng.choice(b0, (9 - RO, H))]
            dl[:, gst] = rng.permuted(np.concatenate(w), axis=0)
            k = p["kq"][a, g]; k[:, own[:H]] = 2; k[:, gst] = 15
            k[:, own[H:]] = pat[:, rng.integers(0, RO, S - H)] + rng.integers(-1, 2, (16, S - H))
            for t in range(RO):
                new = rng.permutation(S) < vals[(a + g + 3 * t + off) % 8]
                x = pat[:, np.where(new & (t < RO - 1), t + 1, 0)] + rng.integers(-1, 2, (16, S))
                if t == RO - 1: x[:, :H] = rng.integers(14, 16, (16, H))
                p["xs"][a, g, :, t] = x
    relay(rng, p, pat, int(rng.integers(0, 8)))
    return pack(p)
def setup_inputs_crowd(rng):
    p = parts(rng)
    for a in range(N):
        for g in range(8):
            o = rng.permutation(Q0); st, nb = p["st"][a, g], p["nb"][a, g]; kind = g // 2
            if (a + g) % 2 == 1:
                st[:] = o[:LN]; nb[:] = np.arange(Q0); p["xs"][a, g] = rng.integers(0, 16, (16, RO, S)); continue
            z = o[:4] if kind == 2 else o[:1]
            nb[:, z] = rng.choice(z, (16, z.size)); st[:] = rng.choice(z, LN)
            if kind == 1 or kind == 3:
                st[LN - 1 if kind == 1 else int(rng.integers(1, S))] = o[5]; nb[:, o[5]] = o[5]
            if kind != 2: p["xs"][a, g][:, :2, 0] = p["cc"][a, g][:, p["dl"][a, g, 0, z[0]]][:, None]
    return pack(p)
def setup_inputs_ends(rng):
    p = parts(rng); sw = (np.arange(N)[:, None] + np.arange(8)) % 2
    hs = 15 * (np.argsort(rng.random((N, 8, 16, 3)), axis=2) < 8)
    pr = np.zeros((N, 8, 16, 8), np.int64); pr[..., 1] = 15; pr[..., 2::2] = hs; pr[..., 3::2] = 15 - hs
    ki = rng.integers(0, 8, (N, 8, Q0)); ci = rng.integers(0, 8, (N, 8, CN)); xi = rng.integers(0, 8, (N, 8, RO, S))
    ci[..., 0] = sw; ci[..., CN - 1] = 1 - sw; ki[..., 0] = 1 - sw; ki[..., Q0 - 1] = sw
    ci[:, 7, 0] = 0; ci[:, 7, CN - 1] = 0; ki[:, 7, 0] = 0; ki[:, 7, Q0 - 1] = 0
    xi[..., 0] = rng.integers(0, 2, (N, 8, RO)); xi[..., S - 1] = rng.integers(0, 2, (N, 8, RO)); xi[:, 7, 0, 0] = 1; xi[:, 7, 0, S - 1] = 1
    p["kq"] = pick4(pr, ki); p["cc"] = pick4(pr, ci); p["xs"] = pick4(pr, xi.reshape(N, 8, RO * S))
    for k, top in (("nb", Q0 - 1), ("dl", CN - 1)):
        v = rng.integers(0, top + 1, (N, 8, 16, Q0)); v[:, :, :6] = 0; v[:, :, 6:11] = top
        v[:, :, :11] = np.where(rng.random((N, 8, 1, Q0)) < 0.5, top - v[:, :, :11], v[:, :, :11])
        v = rng.permuted(v, axis=2)
        for a in range(N):
            for c in (0, Q0 - 1): v[a, 7, :, c] = rng.permutation(np.repeat(np.array([0, top]), 8))
        p[k] = v
    st = np.where(rng.random((N, 8, LN)) < 0.72, (Q0 - 1) * rng.integers(0, 2, (N, 8, LN)), rng.integers(0, Q0, (N, 8, LN)))
    st[..., 0] = 0; st[..., S - 1] = Q0 - 1; st[..., LN - 1] = Q0 - 1; st[:, 7, 0] = Q0 - 1; p["st"] = st
    aa = pos(rng, 64, 128, N, 8, 16, CN).astype(np.float32)
    aa[:, 7, :, CN - 1] = 0.5 * aa[:, 7, :, 0]; p["aa"] = aa
    return pack(p)
def setup_inputs_spread(rng):
    p = parts(rng)
    for k, lo, hi in (("aa", 32, 64), ("ys", 128, 1024)):
        s = (N, 8, 1) + p[k].shape[3:]
        p[k] = pos(rng, lo, hi, *p[k].shape).astype(np.float32) * np.exp2(rng.integers(-1, 2, s))
    far(rng, p, int(rng.integers(0, 8)))
    return pack(p)
def setup_inputs_ties(rng):
    p = parts(rng)
    st = np.argsort(rng.random((N, 4, Q0)), axis=-1)[..., :LN]; p["st"][:, ::2] = st; p["nb"][:, ::2] = np.arange(Q0); p["cc"][:, ::2] = 7
    for t in range(RO):
        h = 8 * ((t // 2) % 2); x = np.full((N, 4, 16, S), 7)
        x[:, :, h:h + 8] += (1 - 2 * (t % 2)) * split(rng, EPS + rng.integers(0, 2, (N, 4, S)), 8, 7)
        p["xs"][:, ::2, :, t] = x
        if t == 0:
            z = split(rng, RHO + rng.integers(0, 2, (N, 4, S)), 16, 8); K = np.where(x > 7, x - z, x + z)
            for a in range(N):
                for g in range(4): p["kq"][a, 2 * g][:, st[a, g, :S]] = K[a, g]
    p["dl"][:, 2, 8:] = p["dl"][:, 2, :8]; p["dl"][:, 6, 8:] = p["dl"][:, 6, :8]
    pr = rng.integers(0, 16, (N, 4, 16, 6)); p["kq"][:, 1::2] = pick4(pr, rng.integers(0, 6, (N, 4, Q0)))
    p["cc"][:, 1::2] = np.where(rng.random((N, 4, 1, CN)) < 0.6, pick4(pr, rng.integers(0, 6, (N, 4, CN))), p["cc"][:, 1::2])
    for t in range(RO):
        m = rng.choice(np.array([0, 0, 1, 4, 9]), (N, 4, 1, S))
        p["xs"][:, 1::2, :, t] = clip(pick4(pr, rng.integers(0, 6, (N, 4, S))) + noise(rng, m, (N, 4, 16, S)))
    return pack(p)
def check_ranges(d):
    bad = []
    for k, hi in (("kq", 15), ("cc", 15), ("xs", 15), ("nb", Q0 - 1), ("dl", CN - 1), ("st", Q0 - 1)):
        v = np.asarray(d[k]).astype(np.float64)
        if not (np.min(v) >= 0 and np.max(v) <= hi): bad.append("range of " + k)
        elif np.any(v != np.floor(v)): bad.append("whole numbers of " + k)
    for k, lo, hi in (("aa", 16, 128), ("ys", 64, 2048)):
        v = np.asarray(d[k]).astype(np.float64)
        if not np.all((v >= lo) & (v <= hi)): bad.append("range of " + k)
    return bad
def pick(w, ix):
    return np.take_along_axis(w, ix[:, None, :], 2)
def entry(v, k):
    return np.take_along_axis(v, k[:, None, :], 1)[:, 0]
def dist(w, ix, x):
    v = pick(w, ix.reshape(8, -1)).reshape(8, 16, 16, -1)
    return np.add.reduce(np.abs(v - x[:, :, None, :]), axis=1)
def reference(kq, nb, dl, cc, aa, xs, ys, st):
    QT, CT = Q0 + LN * (RO - 1), CN + LN * (RO - 1)
    kk = np.zeros((N, 8, 16, QT), np.int32); nn = np.zeros((N, 8, 16, QT), np.int64); ll = np.zeros((N, 8, 16, QT), np.int64)
    ce = np.zeros((N, 8, 16, CT), np.int32); ac = np.zeros((N, 8, 16, CT), np.float64)
    kk[..., :Q0] = kq.astype(np.float32).astype(np.int32).reshape(N, 8, 16, Q0); nn[..., :Q0] = nb.reshape(N, 8, 16, Q0); ll[..., :Q0] = dl.reshape(N, 8, 16, Q0)
    ce[..., :CN] = cc.astype(np.float32).astype(np.int32).reshape(N, 8, 16, CN); ac[..., :CN] = aa.astype(np.float64).reshape(N, 8, 16, CN)
    x0 = xs.astype(np.float32).astype(np.int32).reshape(N, 8, 16, RO, S); y0 = ys.astype(np.float64).reshape(N, 8, 16, RO, S)
    cl = np.stack([gentries(a) for a in st]).astype(np.int64)
    gx = np.zeros((N, 8, 16, H), np.int32); ga = np.zeros((N, 8, 16, H), np.float64); gn = np.zeros((N, 8), np.int64)
    out = np.zeros((N, 8, 16, RO, S), np.float64); lane = np.arange(LN); rows = np.arange(16)[:, None]; before = np.tri(LN, LN, -1, dtype=bool)
    for t in range(RO):
        hx, ha, hn = np.zeros_like(gx), np.zeros_like(ga), np.zeros_like(gn)
        for a in range(N):
            x = np.concatenate([x0[a, :, :, t], gx[a]], axis=2); live = (lane < S) | (lane - S < gn[a][:, None])
            cand = pick(nn[a], cl[a]); d = dist(kk[a], cand, x)
            q = entry(cand, np.argmin(d, axis=1)); dq = np.min(d, axis=1)
            li = pick(ll[a], q); D = dist(ce[a], li, x)
            w = np.exp(-0.015625 * D[:, None, :, :S])
            P = np.add.reduce(w * pick(ac[a], li[:, :, :S].reshape(8, -1)).reshape(8, 16, 16, S), axis=2)
            out[a, :, :, t] = P
            if t == RO - 1: continue
            win = live & ~np.any((q[:, :, None] == q[:, None, :]) & live[:, None, :] & before, axis=2)
            ks, kl = np.argmin(D, axis=1), np.argmax(D, axis=1)
            upd = np.min(D, axis=1) <= EPS; fork = ~upd & (dq > RHO)
            cs = entry(li, ks); lo, ql = CN + LN * t, Q0 + LN * t
            cn = np.where(upd[:, None, :], pick(ce[a], cs), x)
            an = np.concatenate([np.where(upd[:, None, :S], pick(ac[a], cs[:, :S]), 0.0) + 0.25 * (y0[a, :, :, t] - P), ga[a]], axis=2)
            nl = np.where(rows == np.where(upd, ks, kl)[:, None, :], lo + lane, li)
            nq = np.where(rows == t, q[:, None, :], pick(nn[a], q))
            ce[a][:, :, lo:lo + LN] = cn; ac[a][:, :, lo:lo + LN] = an
            b = (a + 1 + t % (N - 1)) % N
            for g in range(8):
                i = np.nonzero(win[g] & ~fork[g])[0]; ll[a, g][:, q[g, i]] = nl[g][:, i]
                i = np.nonzero(win[g] & fork[g])[0]
                ll[a, g][:, ql + i] = nl[g][:, i]; nn[a, g][:, ql + i] = nq[g][:, i]; kk[a, g][:, ql + i] = x[g][:, i]; nn[a, g][8 + t, q[g, i]] = ql + i
                i = np.nonzero(win[g, :S] & ~upd[g, :S])[0][:H]
                hx[b, g][:, :i.size] = x[g][:, i]; ha[b, g][:, :i.size] = an[g][:, i]; hn[b, g] = i.size
            cl[a] = np.where(live, q, cl[a])
        gx, ga, gn = hx, ha, hn
    return {"yp": out.reshape(N, 128, RO * S).astype(np.float32)}

def check_inputs(d):
    bad = list(check_ranges(d))
    if not bad:
        for name, y in reference(**d).items():
            for q in range(N):
                v = np.abs(np.asarray(y[q], np.float64)); s = np.sqrt(np.mean(v * v))
                if v.max() > 5 * s or s < 2.0 ** 7: bad.append('%s of rank %d is uneven or too small' % (name, q))
    return bad

@@ -1,0 +1,847 @@
+import math
+import numpy as np
+from concourse.mybir import AluOpType, ActivationFunctionType
+
+AL = AluOpType
+AF = ActivationFunctionType
+S, H, RO = 160, 96, 4
+HD = 256
+QL = (1024, 1184, 1440, 1696)
+LO = (3328, 3488, 3744, 4000)
+NL = (160, 256, 256, 160)
+MAGIC = 1.5 * 2.0 ** 34
+MX = 255 * 65536 + 30 * 4096 + 4094
+F, B, I, U, HF = "float32", "bfloat16", "int32", "uint16", "float16"
+CFG = {
+    "cut": ((96,), (128,), (128,), (128,)),
+    "actp": (((0,), (128,)), ((128,), (96,)), ((64,), (128,)), ((0, 128), (64, 96, 128))),
+    "relu": ((0, 0), (0, 0), (0, 0), (0, 0)),
+    "scan": (0, 0, 1, 3),
+    "pgrp": 96, "seed": 768, "noise": 200.0, "war": 1, "xe0": 6, "look": 0.3, "iters": 6, "kgrp": 128, "selv": 8,
+    "winact": 1, "gset": 0, "sela": 0, "big": 1, "bigp": 0, "gp": 48, "flagz": 1, "ils": 1000,
+    "early": (0, 1, 1, 1),
+}
+
+SB = {
+    "sti": (16, I), "nbi": (1024, I), "dli": (1024, I), "nn": (2048, F), "ll": (1696, F), "kk": (1696, B),
+    "ce": (4000, B), "ac": (4000, F), "xb": (640, B), "yb": (640, B), "y4": (480, B), "pout": (640, F),
+    "ones": (160, F), "iw": (160, F), "u0": (160, F), "u1": (160, F), "u0b": (160, B), "u1b": (160, B),
+    "ib": (128, B), "nib": (128, B), "iq": (128, F), "bo": (128, B), "bt": (128, B), "w1": (144, B), "w2": (144, B),
+    "w1n": (144, B), "w2d": (144, B), "w2n": (144, B), "nbo": (128, B),
+    "sel": (2048, B), "lt": (128, B), "ew2": (128, B), "ewd": (128, B), "smask": (512, F),
+    "pi": (8, I), "col": (32, F), "pw": (8, B), "rm": (16, F), "nrm": (16, F), "i16": (16, F),
+    "iob": (256, B), "iof": (256, F), "cix": (512, B), "thr": (256, B), "rmin": (128, F), "rmax": (128, F),
+    "lane": (16, F), "jg": (16, F), "pj": (16, F), "own": (96, F), "stf": (16, F), "stu": (16, U), "cl2": (16, U),
+    "candu": (256, U), "candf": (256, F), "nnq": (256, F), "g1": (256, F), "ct": (256, F),
+    "ab1": (4096, B), "ab20": (4096, B), "ab21": (4096, B), "graw": (4096, B), "wt": (2560, F), "prod": (2560, F),
+    "rl1": (2048, B), "rl20": (2048, B), "rl21": (2048, B), "lik": (256, F), "sq": (256, B),
+    "tk": (256, F), "tk2": (256, F), "sc": (256, F), "sc2": (512, F), "hz": (16, F), "qz": (32, HF), "qf": (32, F),
+    "qh": (16, HF), "qr": (256, HF),
+    "eq": (4096, B), "winr": (256, B), "nx": (16, F), "sm": (256, F), "mi": (32, I), "kab": (32, I), "ti": (48, I),
+    "ks": (16, B), "nw": (16, B), "zz": (256, F), "uu": (160, F), "xe": (10240, B), "wg": (16, F), "nz": (16, B),
+    "wr": (432, B), "c16": (160, HF), "fx": (16, U), "dfx": (160, B),
+}
+for _t in range(4):
+    SB["qg%d" % _t] = (16, U)
+    SB["liu%d" % _t] = (256, U)
+for _t in range(3):
+    SB["tu%d" % _t] = (48, U)
+    SB["et%d" % _t] = (32, F)
+for _t in range(2):
+    SB["gx%d" % _t] = (320, B)
+    SB["ga%d" % _t] = (320, F)
+    SB["pos%d" % _t] = (16, U)
+    SB["lb%d" % (_t + 1)] = (112, B)
+SCRATCH = {}
+for _n in SB:
+    SCRATCH[_n] = ("sbuf", [128, SB[_n][0]], SB[_n][1])
+for _t in range(8):
+    SCRATCH["p%d" % _t] = ("psum", [128, 512], F)
+NDMA = 16
+SEMAPHORES = ["sv", "sa", "sp", "sg", "rx0", "rx1", "ra0", "ra1", "sent"] + ["d%d" % _t for _t in range(NDMA)]
+DRAM = ("kq", "cc", "aa", "xs", "ys", "nb", "dl", "st", "yp")
+
+NOM = {"c": 1.04, "g": 1.62, "s": 3.95, "p": 0.52, "x": 90.0, "y": 60.0, "d": 1.0}
+SETS = [NOM, dict(NOM, g=1.2, s=2.2, x=130.0), dict(NOM, g=2.0, s=5.5, p=0.6)]
+
+
+def V(n, a=0, b=None, s=1):
+    if b is None:
+        b = SB[n][0] if n in SB else 512
+    return (n, a, b, s)
+
+
+def C(n, a):
+    return (n, a, a + 1, 1)
+
+
+def X(w, o):
+    return ("ind", w, o)
+
+
+def cnt(v):
+    if v[0] == "ind":
+        return 16 * cnt(v[2])
+    return len(range(v[1], v[2], v[3]))
+
+
+def isview(v):
+    return isinstance(v, tuple)
+
+
+def psum(v):
+    return v[0][0] == "p" and v[0][1:].isdigit()
+
+
+def two(v):
+    return v[0] in SB and SB[v[0]][1] in (B, U, HF)
+
+
+def meet(a, b):
+    if a[0] != b[0] or a[1] >= b[2] or b[1] >= a[2]:
+        return False
+    if a[3] == b[3] and a[3] > 1 and (a[1] - b[1]) % a[3] != 0:
+        return False
+    return True
+
+
+def build(cfg):
+    ops = []
+
+    def add(eng, kind, args, outs, ins, cost, extra=None):
+        rd, wr = [], []
+        for v in ins:
+            if isview(v):
+                rd.extend([v[1], v[2]] if v[0] == "ind" else [v])
+        for v in outs:
+            if v[0] == "ind":
+                wr.append(v[1])
+                rd.append(v[2])
+            else:
+                wr.append(v)
+        ops.append({"e": eng, "k": kind, "a": args, "r": rd, "w": wr, "m": cost, "x": extra or {}})
+        return len(ops) - 1
+
+    def vcost(out, a, f):
+        n = cnt(out)
+        if out[0] == "ind":
+            return (50, n, "s")
+        if a[0] == "ind":
+            return (50, n, "g")
+        return (30, max(64, n * f), "c")
+
+    def cp(out, a):
+        add("v", "cp", (out, a), [out], [a], vcost(out, a, 0.5 if two(out) and two(a) else 1))
+
+    def tt(out, a, b, op):
+        add("v", "tt", (out, a, b, op), [out], [a, b], vcost(out, a, 1 if psum(a) or psum(b) else 2))
+
+    def ts(out, a, s1, o1, s2=None, o2=None):
+        add("v", "ts", (out, a, s1, s2, o1, o2), [out], [a, s1, s2], vcost(out, a, 0.5 if two(out) and two(a) else 1))
+
+    def ms(out, c):
+        add("v", "ms", (out, c), [out], [], vcost(out, out, 0.5 if two(out) else 1))
+
+    def scan(out, d0, d1, o0, o1):
+        add("v", "scan", (out, d0, d1, 0.0, o0, o1), [out], [d0, d1], vcost(out, d0, 1))
+
+    def tr(out, a):
+        add("v", "tr", (out, a), [out], [a], vcost(out, a, 1))
+
+    def act(out, a, f, bias=0.0, scale=1.0, more=0):
+        c = (65, cnt(out), "g") if a[0] == "ind" else (50 + more, max(64, cnt(out)), "c")
+        add("a", "act", (out, a, f, bias, scale), [out], [a, bias, scale], c)
+
+    def mm(out, l, r, st=True, sp=True):
+        add("t", "mm", (out, l, r, st, sp), [out], [l, r], (8, max(64, cnt(r)) * (4 if SB[r[0]][1] == F else 1), "p"))
+
+    def iota(out, pat, base, cm):
+        add("g", "iota", (out, pat, base, cm), [out], [], (0, 156 + 2 * cnt(out), "c"))
+
+    def asel(out, a, pat, op, base, cm, fill=0.0):
+        add("g", "asel", (out, a, pat, op, fill, base, cm), [out], [a], (0, 205 + 2 * cnt(out), "c"))
+
+    def gcp(out, a):
+        asel(out, a, [[0, cnt(out)]], AL.is_ge, 0, 0)
+
+    nd = [0]
+
+    def dma(q, out, a, t, after=None):
+        ins = [a] + ([after] if after else [])
+        add(q, "dma", (out, a), [out], ins, (1000 if q == "g" else 60, 0, "c"), {"sem": "d%d" % nd[0], "lat": t})
+        nd[0] += 1
+
+    def send(dst, src, sem, t):
+        sid = add("g", "send", (dst, src, sem, t), [], [src], (400, 0, "c"), {"lat": 2500})
+        add("r", "recv", (), [dst], [], (0, 0, "c"), {"sem": sem, "from": sid})
+
+    rot = [0]
+
+    def bank():
+        rot[0] += 1
+        return "p%d" % (2 + rot[0] % 2)
+
+    anyrelu = any(any(r) for r in cfg["relu"])
+    dma("a", V("xb"), V("xs", 0, 640), 2200)
+    dma("s", V("sti"), V("st", 0, 16), 2000)
+    dma("s", V("nbi"), V("nb", 0, 1024), 2900)
+    dma("s", V("kk", 0, 1024), V("kq", 0, 1024), 3300)
+    dma("s", V("dli"), V("dl", 0, 1024), 4100)
+    dma("s", V("ce", HD, LO[0]), V("cc", 0, 3072), 5300)
+    dma("s", V("yb"), V("ys", 0, 640), 5600)
+    iota(C("pi", 0), [[0, 1]], 0, 1)
+    ms(V("ones"), 1.0)
+    asel(V("iw"), V("ones"), [[1, 160]], AL.is_equal, -16, -1)
+    asel(V("bt"), V("ones", 0, 128), [[-16, 8], [0, 16]], AL.is_ge, 0, 1)
+    asel(V("bo"), V("bt"), [[16, 8], [0, 16]], AL.is_ge, 15, -1)
+    iota(V("i16"), [[1, 16]], 0, 0)
+    iota(V("cix", 0, 256), [[15, 16], [1, 16]], 0, 0)
+    iota(V("iob"), [[1, 256]], 0, 0)
+    ts(C("pi", 1), C("pi", 0), 15, AL.bitwise_and)
+    ts(C("pi", 2), C("pi", 0), 4, AL.arith_shift_right, 1, AL.bitwise_and)
+    cp(V("col", 0, 2), V("pi", 1, 3))
+    kc, odd, even, b1, b2, k64 = (C("col", j) for j in range(6))
+    act(even, odd, AF.Identity, 1.0, -1.0)
+    act(b1, kc, AF.Identity, -896.0, 2048.0)
+    act(b2, kc, AF.Copy, 0.0, 4096.0)
+    act(k64, kc, AF.Copy, 0.0, -64.0)
+    ts(V("rm"), V("i16"), kc, AL.is_equal)
+    act(V("nrm"), V("rm"), AF.Identity, 1.0, -1.0)
+    act(V("lane"), V("i16"), AF.Identity, kc, 16.0)
+    for w, val in [("w1", 32768.0), ("w2", 65536.0)] + (
+            [("w1n", -32768.0), ("w2d", 131072.0), ("w2n", -65536.0)] if anyrelu else []):
+        if cfg["gset"]:
+            iota(V(w), [[0, 144]], 0, 0)
+        else:
+            ms(V(w), 0.0)
+        act(V(w, 15, 143, 16), V("bo", 0, 128, 16), AF.Copy, 0.0, val)
+    act(V("ib"), V("iw", 16, 144), AF.Copy)
+    act(V("nib"), V("iw", 16, 144), AF.Copy, 0.0, -1.0)
+    act(V("iq"), V("iw", 16, 144), AF.Copy, 0.0, -0.25)
+    act(V("u0b"), V("iw"), AF.Identity, 0.0, even)
+    act(V("u1b"), V("iw"), AF.Identity, 0.0, odd)
+    act(V("u0"), V("iw"), AF.Identity, 0.0, even)
+    act(V("u1"), V("iw"), AF.Identity, 0.0, odd)
+    if cfg["gset"]:
+        iota(V("rmin"), [[0, 128]], 0, 0)
+        asel(V("rmin"), V("rmin"), [[0, 8], [1, 16]], AL.not_equal, 0, 0, 3.0e7)
+        iota(V("rmax"), [[0, 128]], 8192, 0)
+        asel(V("rmax"), V("rmax"), [[0, 8], [1, 16]], AL.not_equal, 0, 0, -3.0e7)
+    else:
+        ms(V("rmin"), 0.0)
+        ms(V("rmin", 0, 128, 16), 3.0e7)
+        ms(V("rmax"), 8192.0)
+        ms(V("rmax", 0, 128, 16), -3.0e7)
+    for r in range(16):
+        if r < cfg["selv"]:
+            ts(V("sel", 128 * r, 128 * r + 128), V("bo"), C("rm", r), AL.mult)
+        elif r < cfg["selv"] + cfg["sela"]:
+            act(V("sel", 128 * r, 128 * r + 128), V("bo"), AF.Identity, 0.0, C("rm", r))
+        else:
+            asel(V("sel", 128 * r, 128 * r + 128), V("ones", 0, 128), [[-16, 8], [0, 16]], AL.is_equal, -r, 1)
+    act(V("thr"), V("cix", 0, 256), AF.Exp, 121 * math.log(2.0), -math.log(2.0), 1600)
+    act(C("pw", 0), kc, AF.Exp, 21 * math.log(2.0), -math.log(2.0))
+    ts(V("ewd"), V("bo"), C("pw", 0), AL.mult)
+    if anyrelu:
+        act(V("ew2"), V("bo"), AF.Copy, 0.0, 2.0)
+        act(V("nbo"), V("bo"), AF.Copy, 0.0, -1.0)
+    asel(V("bt"), V("bo"), [[1, 128]], AL.is_gt, 0, -1)
+    asel(V("lt"), V("bt"), [[1, 128]], AL.not_equal, 0, -1, -512.0)
+    act(V("jg"), V("lane"), AF.Identity, -160.0)
+    act(V("pj"), V("lane"), AF.Identity, 160.0 - 512.0)
+    for t in range(3):
+        act(V("own", 32 * t, 32 * t + 16), V("lane"), AF.Identity, float(QL[t]))
+        act(V("own", 32 * t + 16, 32 * t + 32), V("lane"), AF.Identity, QL[t] - 896.0)
+        act(V("et%d" % t, 16, 32), V("lane"), AF.Identity, float(QL[t] + 256))
+        act(C("col", 8 + t), b2, AF.Identity, float(LO[t]))
+        if cfg["early"][t + 1]:
+            act(V("wr", 144 * t, 144 * t + 144), V("w1"), AF.Identity, 0.0, C("rm", 8 + t))
+        act(C("col", 12 + t), C("rm", 8 + t), AF.Copy, 0.0, float(QL[t]))
+        act(C("col", 16 + t), C("rm", t), AF.Copy, 0.0, 896.0)
+    iota(V("ce", S, HD), [[0, H]], 0, 0)
+    iota(V("nw"), [[0, 16]], 0, 0)
+    for t in range(2):
+        iota(V("gx%d" % t, 0, 112), [[0, 112]], 0, 0)
+        iota(V("ga%d" % t, 0, H), [[0, H]], 0, 0)
+    for k in range(16):
+        if k >= cfg["xe0"]:
+            act(V("xe", k, 2560, 16), V("xb", 0, S), AF.Copy)
+        else:
+            cp(V("xe", k, 2560, 16), V("xb", 0, S))
+    cp(V("stu"), V("sti"))
+    cp(V("qg0", 10, 16), V("sti", 10, 16))
+    cp(V("stf"), V("sti"))
+    cp(V("nn", 0, 1024), V("nbi"))
+    ts(V("ll", 0, 1024), V("dli"), float(HD), AL.add, b2, AL.add)
+    dma("g", V("ac", HD, LO[0]), V("aa", 0, 3072), 5000, V("kk", 0, 1024))
+    iota(V("ac", 0, HD), [[0, HD]], 0, 0)
+    iota(V("iof"), [[1, 256]], 0, 0)
+    iota(V("ll", 1024, 1696), [[0, 672]], 0, 0)
+    act(V("y4"), V("yb", 0, 480), AF.Copy, 0.0, 0.25)
+    if any(cfg["scan"]):
+        iota(V("smask"), [[0, 512]], 1, 0)
+        asel(V("smask"), V("smask"), [[0, 32], [1, 16]], AL.not_equal, 0, 0)
+    for t in (1, 2):
+        for k in range(16):
+            gcp(V("xe", 2560 * t + k, 2560 * (2 * t), 16), V("xb", S * t, S * 2 * t))
+    i32 = V("iw", 16, 144)
+
+    def dist(t, st, c, c0, c1, table, offs, ab, rl):
+        relu = cfg["relu"][t][st] and c == 0
+        e1, skip = min(c1, S), []
+        for a in range(c0, e1, 32):
+            if a in skip:
+                continue
+            onact = a in cfg["actp"][t][st] and not relu
+            b = a + 32
+            if cfg["big"] and not onact and a + 64 + 32 * (cfg["big"] - 1) <= e1 and (relu or b not in cfg["actp"][t][st]):
+                skip.append(b)
+                b += 32
+            d, xe = V(ab, 16 * a, 16 * b), V("xe", 2560 * t + 16 * a, 2560 * t + 16 * b)
+            if onact:
+                gr = V("graw", 16 * a, 16 * a + 512)
+                act(gr, X(table, V(offs, a, a + 32)), AF.Copy)
+                p = bank()
+                mm(V(p), V("ib"), gr, True, False)
+                mm(V(p), V("nib"), xe, False, True)
+                act(d, V(p), AF.Abs)
+            else:
+                tt(d, X(table, V(offs, a, b)), xe, AL.subtract)
+                if relu:
+                    ts(V(rl, 16 * a, 16 * b), d, 0.0, AL.max)
+                else:
+                    act(d, d, AF.Abs)
+        if c1 > S:
+            gp = cfg["gp"]
+            for a in range(S, c1, gp):
+                act(V("graw", 16 * a, 16 * (a + gp)), X(table, V(offs, a, a + gp)), AF.Copy)
+            for k0, k1 in ((0, 4), (4, 8), (8, 12), (12, 16)):
+                p = bank()
+                for k in range(k0, k1):
+                    o = V(p, (k - k0) * H, (k - k0 + 1) * H)
+                    mm(o, V("ib"), V("graw", 16 * S + k, 4096, 16), True, False)
+                    mm(o, V("nib"), V("lb%d" % t, 0, H), False, True)
+                act(V(ab, 16 * S + k0 * H, 16 * S + k1 * H), V(p, 0, (k1 - k0) * H), AF.Abs)
+        return relu
+
+    def key(p, c0, c1, relu, ab, rl, w, num, fix=-1):
+        e1 = min(c1, S)
+        todo = []
+        for a in range(c0, e1, cfg["kgrp"]):
+            b = min(a + cfg["kgrp"], e1)
+            for k in range(16):
+                o = V(p, a - c0, b - c0)
+                if k == fix:
+                    continue
+                if relu:
+                    todo.append((o, {"w1": "w2", "w2": "w2d"}[w], k, V(rl, 16 * a + k, 16 * b, 16)))
+                    todo.append((o, w + "n", k, V(ab, 16 * a + k, 16 * b, 16)))
+                else:
+                    todo.append((o, w, k, V(ab, 16 * a + k, 16 * b, 16)))
+        if fix >= 0 and e1 > c0:
+            todo.append((V(p, 0, e1 - c0), w, fix, V("dfx", c0, e1)))
+        if c1 > S:
+            for k in range(16):
+                todo.append((V(p, S - c0, c1 - c0), w, k, V(ab, 16 * S + k * H, 16 * S + (k + 1) * H)))
+        mm(V(p, 0, c1 - c0), i32, V(num, c0, c1), True, False)
+        for j in range(len(todo)):
+            o, wn, k, r = todo[j]
+            mm(o, V(wn, 15 - k, 143 - k), r, False, j == len(todo) - 1)
+
+    def swap(out, o0, src, s0, n, step, sfx):
+        for c1 in range(2):
+            u = ("u0", "u1")[c1] + sfx
+            o = V(out, o0 + c1, o0 + n, 2)
+            for s in range(2):
+                off = 16 + 16 * (c1 - s)
+                mm(o, V(u, off, off + 128), V(src, s0 + s * step, s0 + n * step, 2 * step), s == 0, s == 1)
+
+    def pstage(t):
+        ab, rl = "ab2%d" % (t % 2), "rl2%d" % (t % 2)
+        last = t == RO - 1
+        for a in range(0, S, 32):
+            if cfg["relu"][t][1] and a < cfg["cut"][t][0]:
+                mm(V("p4"), V("ew2"), V(rl, 16 * a, 16 * a + 512), True, False)
+                mm(V("p4"), V("nbo"), V(ab, 16 * a, 16 * a + 512), False, True)
+            else:
+                mm(V("p4"), V("bo"), V(ab, 16 * a, 16 * a + 512))
+            act(V("wt", 16 * a, 16 * a + 512), V("p4"), AF.Exp, 0.0, -1.0 / 64)
+            if cfg["bigp"] and a in (0, 64):
+                continue
+            a0 = a - 32 if cfg["bigp"] and a in (32, 96) else a
+            tt(V("prod", 16 * a0, 16 * a + 512), X(V("ac", 0, LO[t]), V("liu%d" % t, a0, a + 32)),
+               V("wt", 16 * a0, 16 * a + 512), AL.mult)
+        pe = S - 32 * cfg["scan"][t]
+        grp = [(0, cfg["pgrp"]), (cfg["pgrp"], pe)] if pe > cfg["pgrp"] else [(0, pe)]
+        for a, b in grp:
+            if b > a:
+                for k in range(16):
+                    mm(V("p6", a, b), V("iq"), V("prod", 16 * a + k, 16 * b, 16), k == 0, k == 15)
+        if pe > 0:
+            act(V("pout", S * t, S * t + pe), V("p6", 0, pe), AF.Copy, 0.0, -4.0)
+        if last and pe < S:
+            dma("s", V("yp", S * t, S * t + pe), V("pout", S * t, S * t + pe), 2000)
+        for a in range(pe, S, 32):
+            scan(V("wt", 16 * a, 16 * a + 512), V("smask"), V("prod", 16 * a, 16 * a + 512), AL.mult, AL.add)
+            cp(V("pout", S * t + a, S * t + a + 32), V("wt", 16 * a + 15, 16 * a + 512, 16))
+        o0 = pe if last and pe < S else 0
+        dma("s", V("yp", S * t + o0, S * t + S), V("pout", S * t + o0, S * t + S), 2000)
+        if last:
+            return
+        tt(V("uu"), X(V("ac", 0, LO[t]), V("tu%d" % t, 32, 42)), V("y4", S * t, S * t + S), AL.add)
+        if pe > 0:
+            tt(V("ac", LO[t], LO[t] + pe), V("uu", 0, pe), V("p6", 0, pe), AL.add)
+        if pe < S:
+            act(V("p6", pe, S), V("pout", S * t + pe, S * t + S), AF.Copy, 0.0, -0.25)
+            tt(V("ac", LO[t] + pe, LO[t] + S), V("uu", pe, S), V("p6", pe, S), AL.add)
+        if t < 2:
+            cp(X(V("ga%d" % t), V("pos%d" % t, 0, 10)), V("ac", LO[t], LO[t] + S))
+            a0 = LO[t + 1] + S
+            send(V("ac", a0, a0 + H), V("ga%d" % t, 0, H), "ra%d" % t, t)
+
+    for t in range(RO):
+        n, nb = NL[t], NL[t] // 16
+        last = t == RO - 1
+        cuts = (0,) + cfg["cut"][t] + (n,)
+        chunks = [(cuts[c], cuts[c + 1]) for c in range(len(cuts) - 1)]
+        qg, liu, ab2, rl2 = "qg%d" % t, "liu%d" % t, "ab2%d" % (t % 2), "rl2%d" % (t % 2)
+        nnw, llw = V("nn", 0, QL[t]), V("ll", 0, QL[t])
+        xt = V("xb", S * t, S * t + S)
+        if not last:
+            gcp(V("ce", 0, S), xt)
+            gcp(V("kk", QL[t], QL[t] + S), xt)
+            if n > S:
+                gcp(V("ce", S, HD), V("lb%d" % t, 0, H))
+                gcp(V("kk", QL[t] + S, QL[t] + n), V("lb%d" % t, 0, H))
+        early = t > 0 and cfg["early"][t]
+        if early:
+            cp(V("c16"), X(nnw, V("qg%d" % (t - 1), 0, 10)))
+            for r in range(16):
+                mm(V("p7", 192, 202), V("wr", 144 * t - 129 - r, 144 * t - 1 - r), V("c16", r, S, 16), r == 0, r == 15)
+            ts(V("fx", 0, 10), V("p7", 192, 202), 2.0 ** -15, AL.mult)
+            tt(V("dfx"), X(V("kk", 0, QL[t]), V("fx", 0, 10)), xt, AL.subtract)
+            act(V("dfx"), V("dfx"), AF.Abs)
+        for c in range(len(chunks)):
+            c0, c1 = chunks[c]
+            b0, bn = c0 // 16, (c1 - c0) // 16
+            if t == 0:
+                cl = "stu"
+            elif t == 2 and c1 > S:
+                cl = "cl2"
+            else:
+                cl = "qg%d" % (t - 1)
+            d0 = max(c0, S) if early else c0
+            if c1 > d0:
+                cp(V("candu", d0, c1), X(V("nbi") if t == 0 else nnw, V(cl, d0 // 16, c1 // 16)))
+                dist(t, 0, c, d0, c1, V("kk", 0, QL[t]), "candu", "ab1", "rl1")
+            act(V("candf", c0, c1), X(nnw, V(cl, b0, b0 + bn)), AF.Identity, b1)
+            relu = cfg["relu"][t][0] and c == 0
+            p = "p%d" % (c % 2)
+            key(p, c0, c1, relu, "ab1", "rl1", "w1", "candf", 7 + t if early else -1)
+            tr(V("tk", c0, c1), V(p, 0, c1 - c0))
+            scan(V("sc", c0, c1), V("rmin", 0, c1 - c0), V("tk", c0, c1), AL.add, AL.min)
+            mn = V("sc", c0 + 15, c1, 16)
+            ts(V("hz", b0, b0 + bn), mn, MAGIC, AL.add, MAGIC, AL.subtract)
+            tt(V("qz", b0, b0 + bn), mn, V("hz", b0, b0 + bn), AL.subtract)
+            swap("p7", b0, "qz", b0, bn, 1, "b")
+            ts(V(qg, b0, b0 + bn), V("p7", b0, b0 + bn), 896.0, AL.add)
+        if not last:
+            cp(V("qh", 0, nb), V("p7", 0, nb))
+            ts(V("qz", 16, 16 + nb), V("sc", 15, n, 16), 53 * 32768.0 - 1024, AL.is_ge)
+            swap("p7", nb, "qz", 16, nb, 1, "b")
+            cp(V("qf", 0, 2 * nb), V("p7", 0, 2 * nb))
+        for c in range(len(chunks)):
+            c0, c1 = chunks[c]
+            b0, bn = c0 // 16, (c1 - c0) // 16
+            ts(V(liu, c0, c1), X(llw, V(qg, b0, b0 + bn)), b2, AL.subtract)
+            if not last:
+                act(V("lik", c0, c1), X(llw, V(qg, b0, b0 + bn)), AF.Copy)
+            relu = dist(t, 1, c, c0, c1, V("ce", 0, LO[t]), liu, ab2, rl2)
+            if last:
+                continue
+            p = "p%d" % ((c + len(chunks)) % 2)
+            key(p, c0, c1, relu, ab2, rl2, "w2", "lik")
+            tr(V("tk2", c0, c1), V(p, 0, c1 - c0))
+            scan(V("sc2", c0, c1), V("rmin", 0, c1 - c0), V("tk2", c0, c1), AL.add, AL.min)
+            scan(V("sc2", n + c0, n + c1), V("rmax", 0, c1 - c0), V("tk2", c0, c1), AL.add, AL.max)
+        if last:
+            pstage(t)
+            continue
+        if cfg["early"][t + 1]:
+            cp(V("candu", 0, S), X(nnw, V(qg, 0, 10)))
+            c1 = cfg["cut"][t + 1][0]
+            dist(t + 1, 0, 0, 0, c1, V("kk", 0, QL[t]), "candu", "ab1", "rl1")
+            dist(t + 1, 0, 1, c1, S, V("kk", 0, QL[t]), "candu", "ab1", "rl1")
+
+        def sm(j, w=1):
+            return V("sm", 16 * j, 16 * j + (nb if w == 1 else 32))
+        for r in range(16):
+            mm(V("p5", r, n, 16), V("sel", 128 * r, 128 * r + 128), V("qh", 0, nb))
+        cp(V("qr", 0, n), V("p5", 0, n))
+        act(V("p5", 256, 256 + n), V("p5", 0, n), AF.Identity, C("col", 16 + t), C("rm", t))
+        act(V("nnq", 0, n), X(nnw, V(qg, 0, nb)), AF.Copy)
+        act(V("g1", 0, n), V("nnq", 0, n), AF.Identity, 0.0, C("nrm", t))
+        act(V("ct", 0, n), V("iof", 0, n), AF.Identity, C("col", 12 + t), C("rm", 8 + t))
+        tt(V("nn", QL[t], QL[t] + n), V("g1", 0, n), V("p5", 256, 256 + n), AL.add)
+        mm(V("p5", 256, 256 + n), V("nib"), V("thr", 0, n), True, False)
+        for b in range(nb):
+            e0 = 256 * b
+            ts(V("eq", e0, e0 + n - 16 * b), V("qr", 16 * b, n), C("qf", b), AL.is_equal, 2.0 ** (99 - 15 * b), AL.mult)
+            mm(V("p5", 256 + 16 * b, 256 + n), V("ewd"), V("eq", e0, e0 + n - 16 * b), False, b == nb - 1)
+        if cfg["winact"]:
+            act(V("winr", 0, n), V("p5", 256, 256 + n), AF.Sign, 0.0, -1.0)
+        else:
+            ts(V("winr", 0, n), V("p5", 256, 256 + n), 0.0, AL.is_lt)
+        for r in range(16):
+            mm(V("p5", 0, nb), V("w1", 15 - r, 143 - r), V("winr", r, n, 16), r == 0, r == 15)
+        own, ownm = V("own", 32 * t, 32 * t + nb), V("own", 32 * t + 16, 32 * t + 16 + nb)
+        qf, far = V("qf", 0, nb), V("qf", nb, 2 * nb)
+        wl, ndq, wf0 = sm(0), sm(1), sm(2)
+        if t == 0:
+            act(wl, V("p5", 0, nb), AF.Relu, 0.0, 2.0 ** -19)
+        else:
+            ts(sm(3), V("jg", 0, nb), C("lb%d" % t, H), AL.is_lt, 2.0 ** -19, AL.mult)
+            if cfg["winact"]:
+                act(V("wg", 0, nb), V("p5", 0, nb), AF.Relu)
+            tt(wl, V("wg" if cfg["winact"] else "p5", 0, nb), sm(3), AL.mult)
+        if t == 1:
+            tt(sm(4), qf, V("stf"), AL.subtract)
+            ts(sm(4), sm(4), 896.0, AL.add, 2.0 ** 19, AL.mult)
+            tt(sm(4), sm(4), sm(3), AL.mult)
+            tt(sm(4), sm(4), V("stf"), AL.add)
+            cp(V("cl2"), sm(4))
+        tt(ndq, ownm, qf, AL.subtract)
+        act(sm(5), ndq, AF.Identity, -256.0, -1.0)
+        tt(wf0, wl, far, AL.mult)
+        tt(sm(6), wl, ndq, AL.mult)
+        tt(V("et%d" % t, 0, nb), own, sm(6), AL.subtract)
+        tt(sm(8), ndq, wf0, AL.mult)
+        tt(sm(9), sm(5), wf0, AL.mult)
+        tu = "tu%d" % t
+        mn = V("p7", 64, 64 + nb)
+        th = 37 * 65536.0
+        if cfg["flagz"]:
+            ts(V("nz", 0, nb), V("sc2", 15, n, 16), th, AL.is_ge)
+            swap("p7", 128, "nz", 0, nb, 1, "b")
+            swap("p7", 144, "nz", 0, nb, 1, "b")
+            nu = ("p7", 128)
+        else:
+            swap("p7", 64, "sc2", 15, 2 * nb, 16, "")
+            ts(sm(11), mn, th, AL.is_ge)
+            ts(sm(10), mn, th, AL.is_ge)
+            nu = ("sm", 160)
+        if nb == 16:
+            tt(sm(12, 2), sm(8, 2), V(nu[0], nu[1], nu[1] + 32), AL.mult)
+            tt(V("ti", 0, 32), sm(12, 2), V("et%d" % t), AL.add)
+            cp(V(tu, 0, 32), V("ti", 0, 32))
+        else:
+            for j in (1, 0):
+                tt(sm(12 + j), sm(8 + j), V(nu[0], nu[1], nu[1] + nb), AL.mult)
+                tt(V("ti", 16 * j, 16 * j + nb), sm(12 + j), V("et%d" % t, 16 * j, 16 * j + nb), AL.add)
+                cp(V(tu, 16 * j, 16 * j + nb), V("ti", 16 * j, 16 * j + nb))
+        tt(X(V("nn", 0, QL[t] + 512), V(tu, 16, 16 + nb)), V("nnq", 0, n), V("ct", 0, n), AL.max)
+        if t < 2:
+            tt(V("nw", 0, 10), V("sm", 0, 10), V(nu[0], nu[1], nu[1] + 10), AL.mult)
+        if cfg["flagz"]:
+            swap("p7", 64, "sc2", 15, 2 * nb, 16, "")
+        ts(sm(7), mn, th, AL.is_lt)
+        tt(sm(7), mn, sm(7), AL.mult)
+        if cfg["flagz"]:
+            ts(sm(11), V("p7", 64 + nb, 64 + 2 * nb), -1.0, AL.mult, float(MX), AL.add)
+            tt(V("mi", 16, 16 + nb), sm(11), V("p7", 128, 128 + nb), AL.mult)
+        else:
+            act(V("nx", 0, nb), V("p7", 64 + nb, 64 + 2 * nb), AF.Identity, float(MX), -1.0)
+            tt(V("mi", 16, 16 + nb), V("nx", 0, nb), sm(10), AL.mult)
+        if t < 2:
+            mm(V("p7", 160, 171), V("lt"), V("nw", 0, 11), True, False)
+            for s in range(1, 11):
+                mm(V("p7", 160 + s, 171), V("bo"), V("nw", 0, 11 - s), False, s == 10)
+            tt(V("sm", 224, 234), V("p7", 160, 170), V("pj", 0, 10), AL.min)
+            cp(V("sm", 240, 241), C("p7", 170))
+            ts(V("pos%d" % t, 0, 10), V("sm", 224, 234), 512.0, AL.add)
+            gx = "gx%d" % t
+            cp(X(V(gx), V("pos%d" % t, 0, 10)), xt)
+            act(C(gx, H), V("sm", 240, 241), AF.Copy)
+            send(V("lb%d" % (t + 1)), V(gx, 0, 112), "rx%d" % t, t)
+        tt(V("mi", 0, nb), sm(7), V("lane", 0, nb), AL.max)
+        ts(V("ti", 32, 32 + nb), V("mi", 0, nb), 4095, AL.bitwise_and)
+        cp(V(tu, 32, 32 + nb), V("ti", 32, 32 + nb))
+        if nb == 16:
+            ts(V("kab"), V("mi"), 12, AL.arith_shift_right, 15, AL.bitwise_and)
+        else:
+            for j in range(2):
+                ts(V("kab", 16 * j, 16 * j + nb), V("mi", 16 * j, 16 * j + nb), 12, AL.arith_shift_right, 15, AL.bitwise_and)
+        tt(V("ks", 0, nb), V("kab", 0, nb), V("kab", 16, 16 + nb), AL.add)
+        for r in range(16):
+            mm(V("p5", r, n, 16), V("sel", 128 * r, 128 * r + 128), V("ks", 0, nb))
+        act(V("sq", 0, n), V("p5", 0, n), AF.Square, k64, 64.0)
+        mm(V("p5", 256, 256 + n), V("ib"), V("iob", 0, n), True, False)
+        mm(V("p5", 256, 256 + n), V("nib"), V("sq", 0, n), False, True)
+        act(V("zz", 0, n), V("p5", 256, 256 + n), AF.Identity, C("col", 8 + t))
+        tt(X(V("ll", 0, QL[t] + n), V(tu, 0, nb)), V("zz", 0, n), V("lik", 0, n), AL.max)
+        act(V("ce", LO[t], LO[t] + n), X(V("ce", 0, LO[t]), V(tu, 32, 32 + nb)), AF.Copy)
+        pstage(t)
+    return ops
+
+
+def graph(cfg):
+    ops = build(cfg)
+    n = len(ops)
+    seen = {}
+    before = {}
+    for i in range(n):
+        o = ops[i]
+        deps = {}
+        soft = {}
+        acc = [(v, False) for v in o["r"] if v[0] not in DRAM] + [(v, True) for v in o["w"] if v[0] not in DRAM]
+        for v, w in acc:
+            lst = seen.setdefault(v[0], [])
+            if psum(v):
+                if lst and ops[lst[0][0]]["e"] != o["e"]:
+                    before[v[0]] = [e[0] for e in lst]
+                    lst[:] = []
+                for j in before.get(v[0], ()):
+                    deps[j] = True
+            for j, u, uw in lst:
+                if (w or uw) and meet(u, v):
+                    if w and not uw and not cfg["war"] and ops[j]["e"] == o["e"] and o["e"] in "va" and ops[j]["k"] != "dma":
+                        soft[j] = True
+                    else:
+                        deps[j] = True
+        for v, w in acc:
+            lst = seen[v[0]]
+            if w and v[3] == 1 and not psum(v):
+                lst[:] = [e for e in lst if not (e[1][1] >= v[1] and e[1][2] <= v[2])]
+            lst.append((i, v, w))
+        deps.pop(i, None)
+        soft.pop(i, None)
+        o["d"] = sorted(deps)
+        o["s"] = list(o["d"]) + sorted(soft) + ([o["x"]["from"]] if o["k"] == "recv" else [])
+    lastmm = {}
+    for i in range(n):
+        o = ops[i]
+        if o["k"] == "mm":
+            b = o["w"][0][0]
+            if b in lastmm:
+                o["s"].append(lastmm[b])
+            lastmm[b] = i
+        o["s"] = sorted(set(o["s"]))
+        o["h"] = set(o["d"])
+    return ops
+
+
+def cost(o, m):
+    return o["m"][0] + o["m"][1] * m[o["m"][2]]
+
+
+def gap(o, q, i, m):
+    if q["e"] == o["e"]:
+        return 0.0 if o["e"] == "t" or i not in q["h"] else m["y"]
+    return m["x"]
+
+
+def schedule(ops, cfg, m):
+    n = len(ops)
+    succ = [[] for _ in range(n)]
+    for i in range(n):
+        for j in ops[i]["s"]:
+            succ[j].append(i)
+    cs = [cost(o, m) for o in ops]
+    tl = [o["x"].get("lat", 0.0) * m["d"] for o in ops]
+    pr = [0.0] * n
+    for i in range(n - 1, -1, -1):
+        pr[i] = cs[i] + tl[i] + max([m["x"] + pr[j] for j in succ[i]] + [0.0])
+    fw = [[(j, tl[i] + gap(ops[i], ops[j], i, m)) for j in succ[i]] for i in range(n)]
+    bw = [[(j, tl[j] + gap(ops[j], ops[i], j, m)) for j in ops[i]["s"]] for i in range(n)]
+    eng = [o["e"] for o in ops]
+
+    def sweep(pri, nxt, prv, first):
+        left = [len(x) for x in prv]
+        ready = list(first)
+        pool = {}
+        for i in range(n):
+            if left[i] == 0:
+                pool.setdefault(eng[i], []).append(i)
+        free, seq, st = {}, [], [0.0] * n
+        for _ in range(n):
+            best = None
+            for e in pool:
+                if pool[e]:
+                    t0 = max(free.get(e, 0.0), min([ready[i] for i in pool[e]]))
+                    if best is None or t0 < best[0]:
+                        best = (t0, e)
+            t0, e = best
+            top = i = -1
+            for j in pool[e]:
+                if top < 0 or pri[j] > pri[top]:
+                    top = j
+                if ready[j] <= t0 + 1e-6 and (i < 0 or pri[j] > pri[i]):
+                    i = j
+            if top != i and ready[top] - t0 < cfg["look"] * cs[i]:
+                i = top
+            st[i] = max(free.get(e, 0.0), ready[i])
+            pool[e].remove(i)
+            free[e] = st[i] + cs[i]
+            seq.append(i)
+            for j, lat in nxt[i]:
+                ready[j] = max(ready[j], free[e] + lat)
+                left[j] -= 1
+                if left[j] == 0:
+                    pool.setdefault(eng[j], []).append(j)
+        return seq, st
+
+    rs = np.random.RandomState(cfg["seed"])
+    best = None
+    for _ in range(cfg["iters"] + 1):
+        seq, st = sweep(pr, fw, bw, [0.0] * n)
+        end = max(st[i] + cs[i] + tl[i] for i in range(n))
+        if best is None or end < best[0]:
+            best = (end, seq, st)
+        z = rs.standard_normal(n) * cfg["noise"]
+        back = sweep([st[i] + cs[i] + float(z[i]) for i in range(n)], bw, fw, tl)[1]
+        pr = [back[i] + cs[i] for i in range(n)]
+    if cfg["ils"]:
+        best = (sum(replay(ops, best[1], q) for q in SETS), best[1], best[2])
+    for _ in range(cfg["ils"]):
+        t0, wd, sg = rs.uniform(0, 100000), rs.uniform(3000, 15000), (200.0, 600.0, 1500.0)[rs.randint(3)]
+        z = rs.standard_normal(n) * sg
+        keep = rs.uniform(size=n) < rs.uniform(0.1, 1.0)
+        pri = [-best[2][i] + (float(z[i]) if keep[i] and t0 <= best[2][i] < t0 + wd else 0.0) for i in range(n)]
+        seq, st = sweep(pri, fw, bw, [0.0] * n)
+        if rs.uniform() < 0.3:
+            back = sweep([st[i] + cs[i] for i in range(n)], bw, fw, tl)[1]
+            seq, st = sweep([back[i] + cs[i] for i in range(n)], fw, bw, [0.0] * n)
+        val = sum(replay(ops, seq, q) for q in SETS)
+        if val <= best[0]:
+            best = (val, seq, st)
+    for i in range(n):
+        ops[i]["t"] = best[2][i]
+    return best[1]
+
+
+def replay(ops, seq, m):
+    free, fin, end = {}, {}, 0.0
+    for i in seq:
+        o = ops[i]
+        s = free.get(o["e"], 0.0)
+        for j in o["s"]:
+            s = max(s, fin[j] + gap(ops[j], o, j, m))
+        free[o["e"]] = s + cost(o, m)
+        fin[i] = free[o["e"]] + o["x"].get("lat", 0.0) * m["d"]
+        end = max(end, fin[i])
+    return end
+
+
+def plan(cfg):
+    ops = graph(cfg)
+    order = {}
+    for i in schedule(ops, cfg, NOM):
+        order.setdefault(ops[i]["e"], []).append(i)
+    place = {}
+    for e in order:
+        for k in range(len(order[e])):
+            place[order[e][k]] = k
+    marked = {}
+    for e in order:
+        got = {}
+        for i in order[e]:
+            o = ops[i]
+            need = {}
+            own = []
+            for j in o["d"]:
+                q = ops[j]
+                if "sem" in q["x"]:
+                    if ("x", j) not in got:
+                        got[("x", j)] = True
+                        own.append(j)
+                elif not (e == "t" and q["e"] == "t"):
+                    need[q["e"]] = max(need.get(q["e"], -1), place[j])
+            o["wo"] = own
+            o["wq"] = []
+            for f in need:
+                if need[f] > got.get(f, -1):
+                    got[f] = need[f]
+                    j = order[f][need[f]]
+                    marked[j] = True
+                    o["wq"].append(j)
+    for e in order:
+        c = 0
+        for i in order[e]:
+            if i in marked:
+                c += 1
+                ops[i]["n"] = c
+    return ops, order
+
+
+PLAN = []
+ENG = 4
+QSEM = {"v": "sv", "a": "sa", "t": "sp", "g": "sg"}
+
+
+def rank_program(g, core, T, topo):
+    rank = T.rank_of(core)
+    if rank is None:
+        return
+    if not PLAN:
+        PLAN.append(plan(CFG))
+    ops, order = PLAN[0]
+    nr = len(T.cores)
+    qs = {"v": g.vector, "a": g.scalar, "t": g.tensor, "g": g, "s": g.sync}
+
+    def ap(v):
+        if not isview(v):
+            return v
+        if v[0] == "ind":
+            return ap(v[1]).indirect(ap(v[2]))
+        if v[3] == 1:
+            return T[v[0]][:, v[1]:v[2]]
+        return T[v[0]][:, v[1]:v[1] + (cnt(v) - 1) * v[3] + 1:v[3]]
+
+    for e in ("s", "g", "v", "a", "t"):
+        q = qs[e]
+        for i in order[e]:
+            o = ops[i]
+            for j in o["wo"]:
+                q.wait_ge(T.sem[ops[j]["x"]["sem"]], ENG if ops[j]["k"] == "recv" else 16)
+            for j in o["wq"]:
+                q.wait_ge(T.sem[QSEM[ops[j]["e"]]], ops[j]["n"])
+            k = o["k"]
+            if k == "send":
+                dst = T.cores[(rank + 1 + o["a"][3] % (nr - 1)) % nr]
+                rid, pid, _ = topo.addr(dst)
+                mask = sum(1 << x for x in topo.engines(core, dst)[:ENG])
+                g.remote_dma(ap(o["a"][0]), ap(o["a"][1]), T.sem[o["a"][2]], T.sem.sent, pid, rid, mask)
+                continue
+            a = [ap(v) for v in o["a"]]
+            if k == "dma":
+                q.dma_start(a[0], a[1]).then_inc(T.sem[o["x"]["sem"]], 16)
+                continue
+            if k == "cp":
+                ins = q.tensor_copy(a[0], a[1])
+            elif k == "tt":
+                ins = q.tensor_tensor(a[0], a[1], a[2], a[3])
+            elif k == "ts":
+                ins = q.tensor_scalar(a[0], a[1], a[2], None, a[4]) if a[5] is None else q.tensor_scalar(*a)
+            elif k == "ms":
+                ins = q.memset(a[0], a[1])
+            elif k == "scan":
+                ins = q.tensor_tensor_scan(*a)
+            elif k == "tr":
+                ins = q.transpose(a[0], a[1])
+            elif k == "act":
+                ins = q.activation(a[0], a[1], a[2], bias=a[3], scale=a[4])
+            elif k == "mm":
+                ins = q.matmul(*a)
+            elif k == "iota":
+                if SB[o["a"][0][0]][1] == I:
+                    ins = q.iota(*a)
+                else:
+                    ins = q.iota(*a, allow_small_or_imprecise_dtypes=True)
+            else:
+                ins = q.affine_select(*a)
+            if "n" in o:
+                ins.then_inc(T.sem[QSEM[e]], 1)
+    g.wait_ge(T.sem.sent, 4 * ENG)
+    for o in ops:
+        if o["k"] == "dma" and o["a"][0][0] == "yp":
+            g.sync.wait_ge(T.sem[o["x"]["sem"]], 16)

@@ -10,59 +10,70 @@ QL = (1024, 1184, 1440, 1696)
 LO = (3328, 3488, 3744, 4000)
 NL = (160, 256, 256, 160)
 MAGIC = 1.5 * 2.0 ** 34
-MX = 255 * 65536 + 30 * 4096 + 4094
+MAGIC2 = 1.5 * 2.0 ** 39
 F, B, I, U, HF = "float32", "bfloat16", "int32", "uint16", "float16"
 CFG = {
     "cut": ((96,), (128,), (128,), (128,)),
-    "actp": (((0,), (128,)), ((128,), (96,)), ((64,), (128,)), ((0, 128), (64, 96, 128))),
-    "relu": ((0, 0), (0, 0), (0, 0), (0, 0)),
-    "scan": (0, 0, 1, 3),
-    "pgrp": 96, "seed": 768, "noise": 200.0, "war": 1, "xe0": 6, "look": 0.3, "iters": 6, "kgrp": 128, "selv": 8,
-    "winact": 1, "gset": 0, "sela": 0, "big": 1, "bigp": 0, "gp": 48, "flagz": 1, "ils": 1000,
-    "early": (0, 1, 1, 1),
+    "pc": (("a32 v64 v64", "v64 v32 v32 a32"), ("v64 v64 a32 k96", "v64 v32 a32 v32 k96"),
+           ("v64 a32 v64 k96", "v64 v64 a32 k96"), ("a32 v64 v32 a32", "v64 a32 a32 a32")),
+    "pm": "ddee", "ch": (4, 4, 1, 1), "lev": (0, 0, 0, 0), "pp": 4, "wdep": 1, "acm": "t", "ctm": "d", "cfrom": 1,
+    "scan": (0, 0, 0, 3),
+    "pgrp": 160, "seed": 768, "noise": 200.0, "xe0": 6, "look": 0.3, "iters": 6, "selv": 8, "sela": 0,
+    "bigp": 0, "gp": 48, "ils": 1000, "ug": 4, "ig": 0, "xeg": 0, "fixr": 0, "zv": 0, "seld": 0, "tmax": 1200,
+    "boost": {}, "ptag": 0.3, "sa": 0, "temp": 300.0,
 }
 
+CFG.update({
+    "cut": (((96,), (96,)), ((160,), (160,)), ((160,), (160,)), ((128,), (128,))), "eg": 1, "fixt": 1, "wd": 1,
+    "kv": ((0, 0), (0, 0), (0, 0), (0, 0)), "eng": (0, 16, 2), "fsplit": (0, 1, 1, 0), "pm": "ddde", "ch": (2, 2, 1, 1), "wdep": 0, "xe0": 11, "acm": "v", "seld": 1,
+    "zv": 1, "pgrp": 96, "ils": 600, "ptag": 0.5, "sa": 8000, "temp": 200.0, "seed": 2,
+    "pc": (("a32 v64 v32 a32", "v64 a32 v32 a32"), ("v64 v32 a32 a32 k96", "v64 a32 a32 v32 k96"),
+           ("v64 a32 v64 k96", "v64 a32 a32 a32 k96"), ("a32 v64 a32 a32", "v32 a32 a32 a32 a32")),
+})
+
 SB = {
-    "sti": (16, I), "nbi": (1024, I), "dli": (1024, I), "nn": (2048, F), "ll": (1696, F), "kk": (1696, B),
-    "ce": (4000, B), "ac": (4000, F), "xb": (640, B), "yb": (640, B), "y4": (480, B), "pout": (640, F),
+    "sti": (16, I), "nbi": (1024, I), "dli": (1024, I), "nn": (HD + 1696, F), "ll": (1696, F), "kk": (1856, B),
+    "ce": (4000, B), "ac": (4000, F), "yb": (640, B), "y4": (480, B), "pout": (640, F),
     "ones": (160, F), "iw": (160, F), "u0": (160, F), "u1": (160, F), "u0b": (160, B), "u1b": (160, B),
-    "ib": (128, B), "nib": (128, B), "iq": (128, F), "bo": (128, B), "bt": (128, B), "w1": (144, B), "w2": (144, B),
-    "w1n": (144, B), "w2d": (144, B), "w2n": (144, B), "nbo": (128, B),
-    "sel": (2048, B), "lt": (128, B), "ew2": (128, B), "ewd": (128, B), "smask": (512, F),
-    "pi": (8, I), "col": (32, F), "pw": (8, B), "rm": (16, F), "nrm": (16, F), "i16": (16, F),
-    "iob": (256, B), "iof": (256, F), "cix": (512, B), "thr": (256, B), "rmin": (128, F), "rmax": (128, F),
-    "lane": (16, F), "jg": (16, F), "pj": (16, F), "own": (96, F), "stf": (16, F), "stu": (16, U), "cl2": (16, U),
-    "candu": (256, U), "candf": (256, F), "nnq": (256, F), "g1": (256, F), "ct": (256, F),
+    "ib": (128, B), "nib": (128, B), "iq": (128, F), "iy": (128, B), "bo": (128, B), "bt": (128, B), "w0": (144, B),
+    "wn1": (144, B), "wn2": (144, B), "nbo": (128, B),
+    "sel": (2048, B), "lt": (128, B), "ewd": (128, B), "smask": (512, F),
+    "pi": (8, I), "col": (32, F), "pw": (8, B), "rm": (16, F), "i16": (16, F),
+    "iob": (256, B), "iof": (768, F), "cix": (256, B), "thr": (256, B), "rm1": (256, F), "rm2": (256, F), "rmx": (256, F),
+    "lc": (112, F), "lx": (32, F), "stm": (16, F), "stu": (16, U), "cst": (16, B), "zb": (256, B), "cz": (256, HF),
+    "candu": (256, U), "c16": (256, HF), "lih": (256, HF), "qrf": (256, F), "ct": (768, F),
     "ab1": (4096, B), "ab20": (4096, B), "ab21": (4096, B), "graw": (4096, B), "wt": (2560, F), "prod": (2560, F),
-    "rl1": (2048, B), "rl20": (2048, B), "rl21": (2048, B), "lik": (256, F), "sq": (256, B),
-    "tk": (256, F), "tk2": (256, F), "sc": (256, F), "sc2": (512, F), "hz": (16, F), "qz": (32, HF), "qf": (32, F),
-    "qh": (16, HF), "qr": (256, HF),
-    "eq": (4096, B), "winr": (256, B), "nx": (16, F), "sm": (256, F), "mi": (32, I), "kab": (32, I), "ti": (48, I),
-    "ks": (16, B), "nw": (16, B), "zz": (256, F), "uu": (160, F), "xe": (10240, B), "wg": (16, F), "nz": (16, B),
-    "wr": (432, B), "c16": (160, HF), "fx": (16, U), "dfx": (160, B),
+    "rl1": (2560, B), "rl20": (2560, B), "rl21": (2560, B), "lik": (256, F), "sq": (256, B),
+    "tk": (256, F), "tk2": (256, F), "sc": (256, F), "sc2": (512, F), "hz": (16, F), "qz": (32, HF), "qf": (48, F),
+    "qh": (16, HF), "qr": (256, HF), "vd": (96, B), "wq": (160, F), "wc": (160, F), "lz": (160, HF), "lk": (160, U),
+    "eq": (4096, B), "winr": (256, B), "sm": (256, F), "mi": (32, I), "kab": (32, I), "ti": (16, I), "rr": (16, F),
+    "ks": (16, B), "nw": (32, B), "zz": (256, F), "uu": (160, F), "xe": (10240, B), "nz": (16, B),
+    "wr": (432, B), "fx": (16, U), "dfx": (256, B), "rfx": (256, B),
 }
 for _t in range(4):
     SB["qg%d" % _t] = (16, U)
     SB["liu%d" % _t] = (256, U)
 for _t in range(3):
     SB["tu%d" % _t] = (48, U)
-    SB["et%d" % _t] = (32, F)
 for _t in range(2):
     SB["gx%d" % _t] = (320, B)
     SB["ga%d" % _t] = (320, F)
     SB["pos%d" % _t] = (16, U)
-    SB["lb%d" % (_t + 1)] = (112, B)
 SCRATCH = {}
 for _n in SB:
     SCRATCH[_n] = ("sbuf", [128, SB[_n][0]], SB[_n][1])
 for _t in range(8):
     SCRATCH["p%d" % _t] = ("psum", [128, 512], F)
-NDMA = 16
-SEMAPHORES = ["sv", "sa", "sp", "sg", "rx0", "rx1", "ra0", "ra1", "sent"] + ["d%d" % _t for _t in range(NDMA)]
+SCRATCH["wd"] = ("dram", [8, 4, 2560], F)
+NDMA = 48
+SEMAPHORES = (["sv", "sa", "sp", "sg", "rx0", "rx1", "ra0", "ra1", "tx0", "tx1", "ta0", "ta1", "wz", "ws"]
+              + ["w%s%d" % (_a, _t) for _a in "ab" for _t in range(3)] + ["d%d" % _t for _t in range(NDMA)])
 DRAM = ("kq", "cc", "aa", "xs", "ys", "nb", "dl", "st", "yp")
+ENG = len(range(*CFG["eng"]))
 
-NOM = {"c": 1.04, "g": 1.62, "s": 3.95, "p": 0.52, "x": 90.0, "y": 60.0, "d": 1.0}
-SETS = [NOM, dict(NOM, g=1.2, s=2.2, x=130.0), dict(NOM, g=2.0, s=5.5, p=0.6)]
+NOM = {"c": 0.95, "g": 1.48, "s": 3.6, "p": 0.48, "x": 130.0, "y": 90.0, "d": 1.2, "i": 150.0}
+SETS = [NOM, {"c": 0.85, "g": 1.0, "s": 2.0, "p": 0.43, "x": 150.0, "y": 100.0, "d": 1.4, "i": 250.0},
+        {"c": 1.15, "g": 2.2, "s": 5.5, "p": 0.6, "x": 120.0, "y": 80.0, "d": 1.1, "i": 100.0}]
 
 
 def V(n, a=0, b=None, s=1):
@@ -73,6 +84,10 @@ def V(n, a=0, b=None, s=1):
 
 def C(n, a):
     return (n, a, a + 1, 1)
+
+
+def P(v, r, step=16):
+    return v + ((r, 128, step),)
 
 
 def X(w, o):
@@ -102,11 +117,22 @@ def meet(a, b):
         return False
     if a[3] == b[3] and a[3] > 1 and (a[1] - b[1]) % a[3] != 0:
         return False
+    if len(a) > 4 and len(b) > 4 and a[4] != b[4]:
+        return False
     return True
+
+
+def pieces(text):
+    out, a = [], 0
+    for w in text.split():
+        out.append((a, a + int(w[1:]), w[0]))
+        a += int(w[1:])
+    return out
 
 
 def build(cfg):
     ops = []
+    tag = [""]
 
     def add(eng, kind, args, outs, ins, cost, extra=None):
         rd, wr = [], []
@@ -119,7 +145,8 @@ def build(cfg):
                 rd.append(v[2])
             else:
                 wr.append(v)
-        ops.append({"e": eng, "k": kind, "a": args, "r": rd, "w": wr, "m": cost, "x": extra or {}})
+        ops.append({"e": eng, "k": kind, "a": args, "r": rd, "w": wr, "m": cost, "x": extra or {},
+                    "g": tag[0] or (wr[0][0] + str(wr[0][1] // 2560) if wr else "")})
         return len(ops) - 1
 
     def vcost(out, a, f):
@@ -146,7 +173,7 @@ def build(cfg):
         add("v", "scan", (out, d0, d1, 0.0, o0, o1), [out], [d0, d1], vcost(out, d0, 1))
 
     def tr(out, a):
-        add("v", "tr", (out, a), [out], [a], vcost(out, a, 1))
+        add("v", "tr", (out, a), [out], [a], vcost(out, a, 0.5 if two(out) else 1))
 
     def act(out, a, f, bias=0.0, scale=1.0, more=0):
         c = (65, cnt(out), "g") if a[0] == "ind" else (50 + more, max(64, cnt(out)), "c")
@@ -166,14 +193,17 @@ def build(cfg):
 
     nd = [0]
 
-    def dma(q, out, a, t, after=None):
-        ins = [a] + ([after] if after else [])
-        add(q, "dma", (out, a), [out], ins, (1000 if q == "g" else 60, 0, "c"), {"sem": "d%d" % nd[0], "lat": t})
-        nd[0] += 1
+    def dma(q, out, a, t, after=None, acc=False, sem=None):
+        ins = [a] + ([after] if after else []) + ([out] if acc else [])
+        if sem is None:
+            sem = ("d%d" % nd[0], 16)
+            nd[0] += 1
+        add(q, "dma", (out, a, acc), [out], ins, (1000, 0, "c") if q == "g" else (0, 1, "i"), {"sem": sem[0], "val": sem[1], "lat": t})
 
-    def send(dst, src, sem, t):
-        sid = add("g", "send", (dst, src, sem, t), [], [src], (400, 0, "c"), {"lat": 2500})
-        add("r", "recv", (), [dst], [], (0, 0, "c"), {"sem": sem, "from": sid})
+    def send(dst, src, sem, gone, t):
+        sid = add("g", "send", (dst, src, sem, t, gone), [], [src], (400, 0, "c"), {"lat": 2500})
+        add("r", "recv", (), [dst], [], (0, 0, "c"), {"sem": sem, "val": ENG, "from": sid})
+        add("r", "recv", (), [(gone, 0, 1, 1)], [], (0, 0, "c"), {"sem": gone, "val": ENG, "from": sid})
 
     rot = [0]
 
@@ -181,169 +211,227 @@ def build(cfg):
         rot[0] += 1
         return "p%d" % (2 + rot[0] % 2)
 
-    anyrelu = any(any(r) for r in cfg["relu"])
-    dma("a", V("xb"), V("xs", 0, 640), 2200)
+    pcs = [[pieces(x) for x in y] for y in cfg["pc"]]
+    relu = [any(p[2] == "r" for t in range(RO) for p in pcs[t][st]) for st in range(2)]
+    relue = any(p[2] == "r" for t in range(RO) for p in pcs[t][1] if cfg["pm"][t] == "e")
+    xen = [max([p[1] for st in range(2) for p in pcs[t][st] if p[2] != "k"] + [0]) for t in range(RO)]
+
+    def chunks(t, st):
+        cuts = (0,) + tuple(cfg["cut"][t][st]) + (NL[t],)
+        return [(cuts[c], cuts[c + 1]) for c in range(len(cuts) - 1)]
+
+    def xl(t, a, b, s=1):
+        return V("kk", QL[t] + a, QL[t] + b, s)
+    dma("a", xl(0, 0, 2 * S), V("xs", 0, 2 * S), 2100)
     dma("s", V("sti"), V("st", 0, 16), 2000)
     dma("s", V("nbi"), V("nb", 0, 1024), 2900)
     dma("s", V("kk", 0, 1024), V("kq", 0, 1024), 3300)
     dma("s", V("dli"), V("dl", 0, 1024), 4100)
     dma("s", V("ce", HD, LO[0]), V("cc", 0, 3072), 5300)
     dma("s", V("yb"), V("ys", 0, 640), 5600)
+    dma("s", xl(2, 0, S), V("xs", 2 * S, 3 * S), 5800)
+    dma("s", xl(3, 0, S), V("xs", 3 * S, 4 * S), 5900)
+    for o in ops:
+        o["x"]["load"] = True
     iota(C("pi", 0), [[0, 1]], 0, 1)
     ms(V("ones"), 1.0)
     asel(V("iw"), V("ones"), [[1, 160]], AL.is_equal, -16, -1)
     asel(V("bt"), V("ones", 0, 128), [[-16, 8], [0, 16]], AL.is_ge, 0, 1)
     asel(V("bo"), V("bt"), [[16, 8], [0, 16]], AL.is_ge, 15, -1)
     iota(V("i16"), [[1, 16]], 0, 0)
-    iota(V("cix", 0, 256), [[15, 16], [1, 16]], 0, 0)
+    iota(V("cix"), [[15, 16], [1, 16]], 0, 0)
     iota(V("iob"), [[1, 256]], 0, 0)
     ts(C("pi", 1), C("pi", 0), 15, AL.bitwise_and)
-    ts(C("pi", 2), C("pi", 0), 4, AL.arith_shift_right, 1, AL.bitwise_and)
-    cp(V("col", 0, 2), V("pi", 1, 3))
-    kc, odd, even, b1, b2, k64 = (C("col", j) for j in range(6))
-    act(even, odd, AF.Identity, 1.0, -1.0)
-    act(b1, kc, AF.Identity, -896.0, 2048.0)
-    act(b2, kc, AF.Copy, 0.0, 4096.0)
-    act(k64, kc, AF.Copy, 0.0, -64.0)
-    ts(V("rm"), V("i16"), kc, AL.is_equal)
-    act(V("nrm"), V("rm"), AF.Identity, 1.0, -1.0)
-    act(V("lane"), V("i16"), AF.Identity, kc, 16.0)
-    for w, val in [("w1", 32768.0), ("w2", 65536.0)] + (
-            [("w1n", -32768.0), ("w2d", 131072.0), ("w2n", -65536.0)] if anyrelu else []):
-        if cfg["gset"]:
-            iota(V(w), [[0, 144]], 0, 0)
-        else:
-            ms(V(w), 0.0)
-        act(V(w, 15, 143, 16), V("bo", 0, 128, 16), AF.Copy, 0.0, val)
-    act(V("ib"), V("iw", 16, 144), AF.Copy)
-    act(V("nib"), V("iw", 16, 144), AF.Copy, 0.0, -1.0)
-    act(V("iq"), V("iw", 16, 144), AF.Copy, 0.0, -0.25)
-    act(V("u0b"), V("iw"), AF.Identity, 0.0, even)
-    act(V("u1b"), V("iw"), AF.Identity, 0.0, odd)
-    act(V("u0"), V("iw"), AF.Identity, 0.0, even)
-    act(V("u1"), V("iw"), AF.Identity, 0.0, odd)
-    if cfg["gset"]:
-        iota(V("rmin"), [[0, 128]], 0, 0)
-        asel(V("rmin"), V("rmin"), [[0, 8], [1, 16]], AL.not_equal, 0, 0, 3.0e7)
-        iota(V("rmax"), [[0, 128]], 8192, 0)
-        asel(V("rmax"), V("rmax"), [[0, 8], [1, 16]], AL.not_equal, 0, 0, -3.0e7)
+    kc, odd, even, k64 = (C("col", j) for j in range(4))
+    if cfg["ug"] < 4:
+        ts(C("pi", 2), C("pi", 0), 4, AL.arith_shift_right, 1, AL.bitwise_and)
+        cp(V("col", 0, 2), V("pi", 1, 3))
+        act(even, odd, AF.Identity, 1.0, -1.0)
     else:
-        ms(V("rmin"), 0.0)
-        ms(V("rmin", 0, 128, 16), 3.0e7)
-        ms(V("rmax"), 8192.0)
-        ms(V("rmax", 0, 128, 16), -3.0e7)
+        cp(kc, C("pi", 1))
+    act(k64, kc, AF.Identity, -960.0, 64.0)
+    ts(V("rm"), V("i16"), kc, AL.is_equal)
+    ms(V("w0"), 0.0)
+    act(V("w0", 15, 143, 16), V("bo", 0, 128, 16), AF.Copy)
+    if relu[0] or cfg["fixr"]:
+        ts(V("wn1"), V("w0"), -32768.0, AL.mult)
+    if relu[1]:
+        ts(V("wn2"), V("w0"), -65536.0, AL.mult)
+    if relue:
+        ts(V("nbo"), V("bo"), -65536.0, AL.mult)
+    i32 = V("iw", 16, 144)
+    for j, (w, val) in enumerate((("iy", 0.25), ("iq", -0.25), ("nib", -1.0), ("ib", 1.0))):
+        if w == "iy" and cfg["acm"] != "t":
+            continue
+        if j < cfg["ig"]:
+            asel(V(w), V("bt"), [[1, 128]], AL.is_gt, -200, 0)
+            asel(V(w), V(w), [[1, 128]], AL.not_equal, 0, -1, val)
+        else:
+            act(V(w), i32, AF.Copy, 0.0, val)
+    for j, (w, par) in enumerate((("u0", 1), ("u1", 0), ("u0b", 1), ("u1b", 0))):
+        if j < cfg["ug"]:
+            asel(V(w), V("iw"), [[0, 5], [1, 2], [0, 16]], AL.is_equal, -par, 0)
+        else:
+            act(V(w), V("iw"), AF.Identity, 0.0, even if par else odd)
+    for w, val, first in (("rm1", -2048.0, 3.0e7), ("rm2", -4096.0, 3.0e7), ("rmx", 4096.0, -3.0e7)):
+        st = 0 if w == "rm1" else 1
+        wid = max(b - a for t in range(RO - st) for a, b in chunks(t, st))
+        ms(V(w, 0, wid), val)
+        ms(V(w, 0, wid, 16), first)
+    if cfg["eg"]:
+        iota(V("zb"), [[0, 256]], 0, 0)
+    zero = V("ac", 0, HD)
+    if cfg["zv"]:
+        ms(zero, 0.0)
+    else:
+        iota(zero, [[0, HD]], 0, 0)
+    if cfg["seld"]:
+        ms(V("eq", 0, 512), 0.0)
+        for j in range(4):
+            dma("s", V("sel", 512 * j, 512 * j + 512), V("eq", 0, 512), 2300, None, False, ("wz", 64))
     for r in range(16):
-        if r < cfg["selv"]:
+        if cfg["seld"]:
+            dma("s", P(V("sel", 128 * r, 128 * r + 128), r), P(V("bo"), r), 2000, None, False, ("ws", 256))
+        elif r < cfg["selv"]:
             ts(V("sel", 128 * r, 128 * r + 128), V("bo"), C("rm", r), AL.mult)
         elif r < cfg["selv"] + cfg["sela"]:
             act(V("sel", 128 * r, 128 * r + 128), V("bo"), AF.Identity, 0.0, C("rm", r))
         else:
             asel(V("sel", 128 * r, 128 * r + 128), V("ones", 0, 128), [[-16, 8], [0, 16]], AL.is_equal, -r, 1)
-    act(V("thr"), V("cix", 0, 256), AF.Exp, 121 * math.log(2.0), -math.log(2.0), 1600)
-    act(C("pw", 0), kc, AF.Exp, 21 * math.log(2.0), -math.log(2.0))
+    act(C("pw", 0), kc, AF.Exp, 21 * math.log(2.0), -math.log(2.0), 1600)
+    act(V("thr"), V("cix"), AF.Exp, 121 * math.log(2.0), -math.log(2.0))
+    ops[-1]["x"]["from"] = len(ops) - 2
     ts(V("ewd"), V("bo"), C("pw", 0), AL.mult)
-    if anyrelu:
-        act(V("ew2"), V("bo"), AF.Copy, 0.0, 2.0)
-        act(V("nbo"), V("bo"), AF.Copy, 0.0, -1.0)
-    asel(V("bt"), V("bo"), [[1, 128]], AL.is_gt, 0, -1)
-    asel(V("lt"), V("bt"), [[1, 128]], AL.not_equal, 0, -1, -512.0)
-    act(V("jg"), V("lane"), AF.Identity, -160.0)
-    act(V("pj"), V("lane"), AF.Identity, 160.0 - 512.0)
+    asel(V("lt"), V("bo"), [[1, 128]], AL.is_gt, 0, -1)
+    ET = (16, 36, 68)
+    iota(V("lc", 0, 16), [[16, 16]], 1, 0)
     for t in range(3):
-        act(V("own", 32 * t, 32 * t + 16), V("lane"), AF.Identity, float(QL[t]))
-        act(V("own", 32 * t + 16, 32 * t + 32), V("lane"), AF.Identity, QL[t] - 896.0)
-        act(V("et%d" % t, 16, 32), V("lane"), AF.Identity, float(QL[t] + 256))
-        act(C("col", 8 + t), b2, AF.Identity, float(LO[t]))
-        if cfg["early"][t + 1]:
-            act(V("wr", 144 * t, 144 * t + 144), V("w1"), AF.Identity, 0.0, C("rm", 8 + t))
-        act(C("col", 12 + t), C("rm", 8 + t), AF.Copy, 0.0, float(QL[t]))
-        act(C("col", 16 + t), C("rm", t), AF.Copy, 0.0, 896.0)
-    iota(V("ce", S, HD), [[0, H]], 0, 0)
-    iota(V("nw"), [[0, 16]], 0, 0)
-    for t in range(2):
-        iota(V("gx%d" % t, 0, 112), [[0, 112]], 0, 0)
-        iota(V("ga%d" % t, 0, H), [[0, H]], 0, 0)
-    for k in range(16):
-        if k >= cfg["xe0"]:
-            act(V("xe", k, 2560, 16), V("xb", 0, S), AF.Copy)
+        nb = NL[t] // 16
+        iota(V("lc", ET[t], ET[t] + 2 * nb), [[-QL[t], 2], [16, nb]], QL[t] - 896, 0)
+    act(V("lc", 0, 100), V("lc", 0, 100), AF.Identity, kc)
+    act(V("lx", 16, 32), V("lc", 0, 16), AF.Identity, 4096.0, -1.0)
+    act(V("cst", 0, 10), V("lc", 0, 10), AF.Identity, 160.0, -1.0)
+    for t in range(3):
+        if not cfg["fixt"]:
+            asel(V("wr", 144 * t, 144 * t + 144), V("w0"), [[-1, 144]], AL.is_equal, 7 - t, 1)
+        iota(V("iof", 256 * t, 256 * t + NL[t]), [[1, NL[t]]], QL[t], 0)
+        ctv = V("ct", 256 * t, 256 * t + NL[t])
+        if cfg["ctm"] == "d":
+            dma("s", ctv, V("ac", 0, NL[t]), 2300)
+            dma("s", P(ctv, 8 + t), P(V("iof", 256 * t, 256 * t + NL[t]), 8 + t), 2200)
         else:
-            cp(V("xe", k, 2560, 16), V("xb", 0, S))
+            act(ctv, V("iof", 256 * t, 256 * t + NL[t]), AF.Identity, 0.0, C("rm", 8 + t))
+    iota(V("ce", S, HD), [[0, H]], 0, 0)
+    for t in range(2):
+        iota(V("gx%d" % t, S, HD), [[0, H]], 16, 0)
+        dma("s", V("ga%d" % t, S, HD), V("ac", 0, H), 2200)
+    for a in range(1024, QL[3], HD):
+        dma("s", V("ll", a, min(a + HD, QL[3])), V("ac", 0, min(HD, QL[3] - a)), 2300)
+    for k in range(16):
+        o, a = V("xe", k, 16 * xen[0], 16), xl(0, 0, xen[0])
+        if k >= 16 - cfg["xeg"]:
+            gcp(o, a)
+        elif k >= cfg["xe0"]:
+            act(o, a, AF.Copy)
+        else:
+            cp(o, a)
     cp(V("stu"), V("sti"))
     cp(V("qg0", 10, 16), V("sti", 10, 16))
-    cp(V("stf"), V("sti"))
-    cp(V("nn", 0, 1024), V("nbi"))
-    ts(V("ll", 0, 1024), V("dli"), float(HD), AL.add, b2, AL.add)
+    ts(V("stm"), V("sti"), -896.0, AL.add)
+    cp(V("nn", HD, HD + 1024), V("nbi"))
+    cp(V("ll", 0, 1024), V("dli"))
     dma("g", V("ac", HD, LO[0]), V("aa", 0, 3072), 5000, V("kk", 0, 1024))
-    iota(V("ac", 0, HD), [[0, HD]], 0, 0)
-    iota(V("iof"), [[1, 256]], 0, 0)
-    iota(V("ll", 1024, 1696), [[0, 672]], 0, 0)
-    act(V("y4"), V("yb", 0, 480), AF.Copy, 0.0, 0.25)
+    ops[-1]["x"]["load"] = True
+    if cfg["acm"] != "t":
+        act(V("y4"), V("yb", 0, 480), AF.Copy, 0.0, 0.25)
     if any(cfg["scan"]):
         iota(V("smask"), [[0, 512]], 1, 0)
         asel(V("smask"), V("smask"), [[0, 32], [1, 16]], AL.not_equal, 0, 0)
-    for t in (1, 2):
-        for k in range(16):
-            gcp(V("xe", 2560 * t + k, 2560 * (2 * t), 16), V("xb", S * t, S * 2 * t))
-    i32 = V("iw", 16, 144)
+    for t in (1, 2, 3):
+        for k in range(16 if xen[t] else 0):
+            gcp(V("xe", 2560 * t + k, 2560 * t + 16 * xen[t], 16), xl(t, 0, xen[t]))
 
-    def dist(t, st, c, c0, c1, table, offs, ab, rl):
-        relu = cfg["relu"][t][st] and c == 0
-        e1, skip = min(c1, S), []
-        for a in range(c0, e1, 32):
-            if a in skip:
-                continue
-            onact = a in cfg["actp"][t][st] and not relu
-            b = a + 32
-            if cfg["big"] and not onact and a + 64 + 32 * (cfg["big"] - 1) <= e1 and (relu or b not in cfg["actp"][t][st]):
-                skip.append(b)
-                b += 32
-            d, xe = V(ab, 16 * a, 16 * b), V("xe", 2560 * t + 16 * a, 2560 * t + 16 * b)
-            if onact:
-                gr = V("graw", 16 * a, 16 * a + 512)
-                act(gr, X(table, V(offs, a, a + 32)), AF.Copy)
+    def dist(t, st, pc, table, offs, ab, rl):
+        a, b, mode = pc
+        sc = 32768.0 * (st + 1)
+        if mode == "k":
+            m = b - a
+            for a0 in range(a, b, cfg["gp"]):
+                b0 = min(b, a0 + cfg["gp"])
+                if (a0 - a) // cfg["gp"] < cfg["kv"][t][st]:
+                    cp(V("graw", 16 * a0, 16 * b0), X(table, V(offs, a0, b0)))
+                else:
+                    act(V("graw", 16 * a0, 16 * b0), X(table, V(offs, a0, b0)), AF.Copy)
+            kb = min(16, 1 << int(math.log2(512 // m)))
+            for k0 in range(0, 16, kb):
                 p = bank()
-                mm(V(p), V("ib"), gr, True, False)
-                mm(V(p), V("nib"), xe, False, True)
-                act(d, V(p), AF.Abs)
+                for k in range(k0, k0 + kb):
+                    o = V(p, (k - k0) * m, (k - k0 + 1) * m)
+                    mm(o, V("ib"), V("graw", 16 * a + k, 16 * b, 16), True, False)
+                    mm(o, V("nib"), xl(t, a, b), False, True)
+                act(V(ab, 16 * a + k0 * m, 16 * a + (k0 + kb) * m), V(p, 0, kb * m), AF.Abs, 0.0, sc)
+            return
+        d, xe = V(ab, 16 * a, 16 * b), V("xe", 2560 * t + 16 * a, 2560 * t + 16 * b)
+        if mode == "a":
+            gr = V("graw", 16 * a, 16 * b)
+            act(gr, X(table, V(offs, a, b)), AF.Copy)
+            for a0 in range(a, b, 32):
+                p = bank()
+                mm(V(p), V("ib"), V("graw", 16 * a0, 16 * a0 + 512), True, False)
+                mm(V(p), V("nib"), V("xe", 2560 * t + 16 * a0, 2560 * t + 16 * a0 + 512), False, True)
+                act(V(ab, 16 * a0, 16 * a0 + 512), V(p), AF.Abs, 0.0, sc)
+        else:
+            tt(d, X(table, V(offs, a, b)), xe, AL.subtract)
+            if mode == "r":
+                ts(V(rl, 16 * a, 16 * b), d, 0.0, AL.max, 2 * sc, AL.mult)
             else:
-                tt(d, X(table, V(offs, a, b)), xe, AL.subtract)
-                if relu:
-                    ts(V(rl, 16 * a, 16 * b), d, 0.0, AL.max)
-                else:
-                    act(d, d, AF.Abs)
-        if c1 > S:
-            gp = cfg["gp"]
-            for a in range(S, c1, gp):
-                act(V("graw", 16 * a, 16 * (a + gp)), X(table, V(offs, a, a + gp)), AF.Copy)
-            for k0, k1 in ((0, 4), (4, 8), (8, 12), (12, 16)):
-                p = bank()
-                for k in range(k0, k1):
-                    o = V(p, (k - k0) * H, (k - k0 + 1) * H)
-                    mm(o, V("ib"), V("graw", 16 * S + k, 4096, 16), True, False)
-                    mm(o, V("nib"), V("lb%d" % t, 0, H), False, True)
-                act(V(ab, 16 * S + k0 * H, 16 * S + k1 * H), V(p, 0, (k1 - k0) * H), AF.Abs)
-        return relu
+                act(d, d, AF.Abs, 0.0, sc)
 
-    def key(p, c0, c1, relu, ab, rl, w, num, fix=-1):
-        e1 = min(c1, S)
+    def key(p, t, st, c0, c1, ab, rl, num, fix=-1, d0=0):
+        runs = []
+        for a, b, mode in pcs[t][st]:
+            mode = "e" if mode in "va" else mode
+            lo, hi = max(a, c0), min(b, c1)
+            if lo >= hi:
+                continue
+            if runs and mode != "k" and runs[-1][2] == mode and (runs[-1][0] < d0) == (lo < d0):
+                runs[-1] = (runs[-1][0], hi, mode, a, b)
+            else:
+                runs.append((lo, hi, mode, a, b))
         todo = []
-        for a in range(c0, e1, cfg["kgrp"]):
-            b = min(a + cfg["kgrp"], e1)
+        for lo, hi, mode, a, b in runs:
+            o = V(p, lo - c0, hi - c0)
             for k in range(16):
-                o = V(p, a - c0, b - c0)
-                if k == fix:
+                if k == fix and lo < d0:
                     continue
-                if relu:
-                    todo.append((o, {"w1": "w2", "w2": "w2d"}[w], k, V(rl, 16 * a + k, 16 * b, 16)))
-                    todo.append((o, w + "n", k, V(ab, 16 * a + k, 16 * b, 16)))
+                if mode == "k":
+                    e0 = 16 * a + k * (b - a) - a
+                    todo.append((o, "w0", k, V(ab, e0 + lo, e0 + hi)))
+                elif mode == "r":
+                    todo.append((o, "wn%d" % (st + 1), k, V(ab, 16 * lo + k, 16 * hi, 16)))
+                    todo.append((o, "w0", k, V(rl, 16 * lo + k, 16 * hi, 16)))
                 else:
-                    todo.append((o, w, k, V(ab, 16 * a + k, 16 * b, 16)))
-        if fix >= 0 and e1 > c0:
-            todo.append((V(p, 0, e1 - c0), w, fix, V("dfx", c0, e1)))
-        if c1 > S:
-            for k in range(16):
-                todo.append((V(p, S - c0, c1 - c0), w, k, V(ab, 16 * S + k * H, 16 * S + (k + 1) * H)))
-        mm(V(p, 0, c1 - c0), i32, V(num, c0, c1), True, False)
+                    todo.append((o, "w0", k, V(ab, 16 * lo + k, 16 * hi, 16)))
+        if fix >= 0 and min(c1, d0) > c0:
+            e1 = min(c1, d0)
+            if cfg["fixr"]:
+                todo.append((V(p, 0, e1 - c0), "wn1", fix, V("dfx", c0, e1)))
+                todo.append((V(p, 0, e1 - c0), "w0", fix, V("rfx", c0, e1)))
+            else:
+                todo.append((V(p, 0, e1 - c0), "w0", fix, V("dfx", c0, e1)))
+        first = [x for x in todo if x[3][0] in ("ab1", "rl1") and fix >= 0 and x[0][2] + c0 <= d0]
+        if first and c1 <= d0 and (len(runs) == 1 or cfg["eg"]):
+            rest = [x for x in todo if x not in first]
+            if len(runs) > 1:
+                mm(V(p, 0, c1 - c0), V("ib"), V("zb", 0, c1 - c0), True, False)
+            for j in range(len(first)):
+                o, wn, k, r = first[j]
+                mm(o, V(wn, 15 - k, 143 - k), r, j == 0 and len(runs) == 1, False)
+            for o, wn, k, r in rest:
+                mm(o, V(wn, 15 - k, 143 - k), r, False, False)
+            mm(V(p, 0, c1 - c0), V("ib"), V(num, c0, c1), False, True)
+            return
+        mm(V(p, 0, c1 - c0), V("ib"), V(num, c0, c1), True, False)
         for j in range(len(todo)):
             o, wn, k, r = todo[j]
             mm(o, V(wn, 15 - k, 143 - k), r, False, j == len(todo) - 1)
@@ -357,29 +445,66 @@ def build(cfg):
                 mm(o, V(u, off, off + 128), V(src, s0 + s * step, s0 + n * step, 2 * step), s == 0, s == 1)
 
     def pstage(t):
+        tag[0] = "P%d" % t
         ab, rl = "ab2%d" % (t % 2), "rl2%d" % (t % 2)
         last = t == RO - 1
-        for a in range(0, S, 32):
-            if cfg["relu"][t][1] and a < cfg["cut"][t][0]:
-                mm(V("p4"), V("ew2"), V(rl, 16 * a, 16 * a + 512), True, False)
-                mm(V("p4"), V("nbo"), V(ab, 16 * a, 16 * a + 512), False, True)
-            else:
-                mm(V("p4"), V("bo"), V(ab, 16 * a, 16 * a + 512))
-            act(V("wt", 16 * a, 16 * a + 512), V("p4"), AF.Exp, 0.0, -1.0 / 64)
-            if cfg["bigp"] and a in (0, 64):
-                continue
-            a0 = a - 32 if cfg["bigp"] and a in (32, 96) else a
-            tt(V("prod", 16 * a0, 16 * a + 512), X(V("ac", 0, LO[t]), V("liu%d" % t, a0, a + 32)),
-               V("wt", 16 * a0, 16 * a + 512), AL.mult)
-        pe = S - 32 * cfg["scan"][t]
-        grp = [(0, cfg["pgrp"]), (cfg["pgrp"], pe)] if pe > cfg["pgrp"] else [(0, pe)]
-        for a, b in grp:
-            if b > a:
-                for k in range(16):
-                    mm(V("p6", a, b), V("iq"), V("prod", 16 * a + k, 16 * b, 16), k == 0, k == 15)
+        acw = V("ac", HD, LO[t])
+        viat = cfg["acm"] == "t"
+        idm = i32 if viat else V("iq")
+        po = V("pout", S * t, S * t + S)
+        pe = S
+        if cfg["pm"][t] == "d":
+            act(V("wc"), V("wq"), AF.Exp, MAGIC2 * 2.0 ** -22, -2.0 ** -22)
+            if cfg["wd"]:
+                for j in range(4):
+                    dma("s", ("wd", j, j + 1, 1), V("wc"), 2200 + 100 * j, None, False, ("wa%d" % t, 64))
+                for j in range(4):
+                    dma("s", P(V("wt"), j, 4), ("wd", 0, 4, 1), 2400 + 550 * j, None, False, ("wb%d" % t, 64))
+            for j in range(0 if cfg["wd"] else 16):
+                f = 4 * (j % 4) + j // 4
+                dma("s", P(V("wt"), f), V("wc"), 2400 + 600 * j, None, False, ("wb%d" % t, 256))
+            tr(V("lz"), V("lih", 0, S))
+            for bb in range(5):
+                for c1 in range(2):
+                    for s in range(2):
+                        off = 16 + 16 * (c1 - s)
+                        mm(V("p4", 2 * bb + c1, S, 10), V(("u0b", "u1b")[c1], off, off + 128),
+                           V("lz", 32 * bb + 16 * s, 32 * bb + 16 * s + 16), s == 0, s == 1)
+            ts(V("lk"), V("p4", 0, S), 2048.0 - HD, AL.add)
+            ch = cfg["ch"][t]
+            seg = 16 // ch
+            pp = min(cfg["pp"], seg)
+            for k in range(0, 16, pp):
+                tt(V("prod", S * k, S * (k + pp)), X(acw, V("lk", 10 * k, 10 * (k + pp))), V("wt", S * k, S * (k + pp)), AL.mult)
+                if (k + pp) % seg == 0 and k + pp > seg:
+                    dma("g", V("prod", 0, S * seg), V("prod", S * (k + pp - seg), S * (k + pp)), 2200 + 250 * seg, None, True)
+            for _ in range(cfg["lev"][t]):
+                seg //= 2
+                dma("g", V("prod", 0, S * seg), V("prod", S * seg, 2 * S * seg), 2200 + 250 * seg, None, True)
+            for k in range(seg):
+                mm(V("p6", 0, S), idm, V("prod", S * k, S * k + S), k == 0, k == seg - 1)
+        else:
+            for a in range(0, S, 32):
+                if [p for p in pcs[t][1] if p[0] <= a < p[1]][0][2] == "r":
+                    mm(V("p4"), V("nbo"), V(ab, 16 * a, 16 * a + 512), True, False)
+                    mm(V("p4"), V("bo"), V(rl, 16 * a, 16 * a + 512), False, True)
+                else:
+                    mm(V("p4"), V("bo"), V(ab, 16 * a, 16 * a + 512))
+                act(V("wt", 16 * a, 16 * a + 512), V("p4"), AF.Exp, 0.0, -2.0 ** -22)
+                if cfg["bigp"] and a in (0, 64):
+                    continue
+                a0 = a - 32 if cfg["bigp"] and a in (32, 96) else a
+                tt(V("prod", 16 * a0, 16 * a + 512), X(acw, V("liu%d" % t, a0, a + 32)),
+                   V("wt", 16 * a0, 16 * a + 512), AL.mult)
+            pe = S - 32 * cfg["scan"][t]
+            grp = [(0, cfg["pgrp"]), (cfg["pgrp"], pe)] if pe > cfg["pgrp"] else [(0, pe)]
+            for a, b in grp:
+                if b > a:
+                    for k in range(16):
+                        mm(V("p6", a, b), idm, V("prod", 16 * a + k, 16 * b, 16), k == 0, k == 15)
         if pe > 0:
-            act(V("pout", S * t, S * t + pe), V("p6", 0, pe), AF.Copy, 0.0, -4.0)
-        if last and pe < S:
+            act(V("pout", S * t, S * t + pe), V("p6", 0, pe), AF.Copy, 0.0, 1.0 if viat else -4.0)
+        if last and 0 < pe < S:
             dma("s", V("yp", S * t, S * t + pe), V("pout", S * t, S * t + pe), 2000)
         for a in range(pe, S, 32):
             scan(V("wt", 16 * a, 16 * a + 512), V("smask"), V("prod", 16 * a, 16 * a + 512), AL.mult, AL.add)
@@ -388,58 +513,70 @@ def build(cfg):
         dma("s", V("yp", S * t + o0, S * t + S), V("pout", S * t + o0, S * t + S), 2000)
         if last:
             return
-        tt(V("uu"), X(V("ac", 0, LO[t]), V("tu%d" % t, 32, 42)), V("y4", S * t, S * t + S), AL.add)
-        if pe > 0:
-            tt(V("ac", LO[t], LO[t] + pe), V("uu", 0, pe), V("p6", 0, pe), AL.add)
-        if pe < S:
-            act(V("p6", pe, S), V("pout", S * t + pe, S * t + S), AF.Copy, 0.0, -0.25)
-            tt(V("ac", LO[t] + pe, LO[t] + S), V("uu", pe, S), V("p6", pe, S), AL.add)
+        old = X(V("ac", 0, LO[t]), V("tu%d" % t, 2 * (NL[t] // 16), 2 * (NL[t] // 16) + 10))
+        new = V("ac", LO[t], LO[t] + S)
+        if viat:
+            act(V("uu"), old, AF.Copy)
+            mm(V("p6", 256, 256 + S), V("iy"), V("yb", S * t, S * t + S), True, False)
+            mm(V("p6", 256, 256 + S), i32, V("uu"), False, False)
+            mm(V("p6", 256, 256 + S), V("iq"), po, False, True)
+            act(new, V("p6", 256, 256 + S), AF.Copy)
+        else:
+            tt(V("uu"), old, V("y4", S * t, S * t + S), AL.add)
+            tt(new, V("uu"), V("p6", 0, S), AL.add)
         if t < 2:
-            cp(X(V("ga%d" % t), V("pos%d" % t, 0, 10)), V("ac", LO[t], LO[t] + S))
+            cp(X(V("ga%d" % t), V("pos%d" % t, 0, 10)), new)
             a0 = LO[t + 1] + S
-            send(V("ac", a0, a0 + H), V("ga%d" % t, 0, H), "ra%d" % t, t)
+            send(V("ac", a0, a0 + H), V("ga%d" % t, S, HD), "ra%d" % t, "ta%d" % t, t)
+
+    def ahead(t):
+        return (NL[t] if cfg["eg"] else S) if t > 0 else 0
 
     for t in range(RO):
         n, nb = NL[t], NL[t] // 16
         last = t == RO - 1
-        cuts = (0,) + cfg["cut"][t] + (n,)
-        chunks = [(cuts[c], cuts[c + 1]) for c in range(len(cuts) - 1)]
         qg, liu, ab2, rl2 = "qg%d" % t, "liu%d" % t, "ab2%d" % (t % 2), "rl2%d" % (t % 2)
-        nnw, llw = V("nn", 0, QL[t]), V("ll", 0, QL[t])
-        xt = V("xb", S * t, S * t + S)
+        nnw, llw = V("nn", HD, HD + QL[t]), V("ll", 0, QL[t])
+        kkw = V("kk", 0, QL[t])
+        xt = xl(t, 0, S)
         if not last:
-            gcp(V("ce", 0, S), xt)
-            gcp(V("kk", QL[t], QL[t] + S), xt)
+            dma("s", V("ce", 0, S), xt, 2300)
             if n > S:
-                gcp(V("ce", S, HD), V("lb%d" % t, 0, H))
-                gcp(V("kk", QL[t] + S, QL[t] + n), V("lb%d" % t, 0, H))
-        early = t > 0 and cfg["early"][t]
-        if early:
-            cp(V("c16"), X(nnw, V("qg%d" % (t - 1), 0, 10)))
-            for r in range(16):
-                mm(V("p7", 192, 202), V("wr", 144 * t - 129 - r, 144 * t - 1 - r), V("c16", r, S, 16), r == 0, r == 15)
-            ts(V("fx", 0, 10), V("p7", 192, 202), 2.0 ** -15, AL.mult)
-            tt(V("dfx"), X(V("kk", 0, QL[t]), V("fx", 0, 10)), xt, AL.subtract)
-            act(V("dfx"), V("dfx"), AF.Abs)
-        for c in range(len(chunks)):
-            c0, c1 = chunks[c]
+                dma("s", V("ce", S, HD), xl(t, S, n), 2200)
+        d0 = ahead(t)
+        tag[0] = "F%d" % t
+        if d0:
+            ts(V("c16", 0, d0), X(V("nn", HD, HD + QL[t - 1]), V("qg%d" % (t - 1), 0, d0 // 16)), -896.0, AL.add)
+            if cfg["fixt"]:
+                tr(V("cz", 0, d0), V("c16", 0, d0))
+                swap("p7", 192, "cz", 7 + t, d0 // 16, 16, "b")
+            for r in range(0 if cfg["fixt"] else 16):
+                mm(V("p7", 192, 192 + d0 // 16), V("wr", 144 * t - 129 - r, 144 * t - 1 - r), V("c16", r, d0, 16), r == 0, r == 15)
+            ts(V("fx", 0, d0 // 16), V("p7", 192, 192 + d0 // 16), 896.0, AL.add)
+            for a, b in chunks(t, 0) if cfg["fsplit"][t] else [(0, d0)]:
+                b = min(b, d0)
+                if a >= b:
+                    continue
+                tt(V("dfx", a, b), X(kkw, V("fx", a // 16, b // 16)), xl(t, a, b), AL.subtract)
+                if cfg["fixr"]:
+                    ts(V("rfx", a, b), V("dfx", a, b), 0.0, AL.max, 65536.0, AL.mult)
+                else:
+                    act(V("dfx", a, b), V("dfx", a, b), AF.Abs, 0.0, 32768.0)
+        for c, (c0, c1) in enumerate(chunks(t, 0)):
             b0, bn = c0 // 16, (c1 - c0) // 16
-            if t == 0:
-                cl = "stu"
-            elif t == 2 and c1 > S:
-                cl = "cl2"
-            else:
-                cl = "qg%d" % (t - 1)
-            d0 = max(c0, S) if early else c0
-            if c1 > d0:
-                cp(V("candu", d0, c1), X(V("nbi") if t == 0 else nnw, V(cl, d0 // 16, c1 // 16)))
-                dist(t, 0, c, d0, c1, V("kk", 0, QL[t]), "candu", "ab1", "rl1")
-            act(V("candf", c0, c1), X(nnw, V(cl, b0, b0 + bn)), AF.Identity, b1)
-            relu = cfg["relu"][t][0] and c == 0
+            e0 = max(c0, d0)
+            tag[0] = "Q%d%d" % (t, c)
+            if c1 > e0:
+                cl = ("stu", "qg0", "qg1")[t]
+                cp(V("candu", e0, c1), X(V("nbi") if t == 0 else V("nn", HD, HD + QL[t - 1]), V(cl, e0 // 16, c1 // 16)))
+                for pc in pcs[t][0]:
+                    if e0 <= pc[0] < c1:
+                        dist(t, 0, pc, kkw, "candu", "ab1", "rl1")
+                ts(V("c16", e0, c1), V("candu", e0, c1), -896.0, AL.add)
             p = "p%d" % (c % 2)
-            key(p, c0, c1, relu, "ab1", "rl1", "w1", "candf", 7 + t if early else -1)
+            key(p, t, 0, c0, c1, "ab1", "rl1", "c16", 7 + t if d0 else -1, d0)
             tr(V("tk", c0, c1), V(p, 0, c1 - c0))
-            scan(V("sc", c0, c1), V("rmin", 0, c1 - c0), V("tk", c0, c1), AL.add, AL.min)
+            scan(V("sc", c0, c1), V("rm1", 0, c1 - c0), V("tk", c0, c1), AL.add, AL.min)
             mn = V("sc", c0 + 15, c1, 16)
             ts(V("hz", b0, b0 + bn), mn, MAGIC, AL.add, MAGIC, AL.subtract)
             tt(V("qz", b0, b0 + bn), mn, V("hz", b0, b0 + bn), AL.subtract)
@@ -447,139 +584,135 @@ def build(cfg):
             ts(V(qg, b0, b0 + bn), V("p7", b0, b0 + bn), 896.0, AL.add)
         if not last:
             cp(V("qh", 0, nb), V("p7", 0, nb))
-            ts(V("qz", 16, 16 + nb), V("sc", 15, n, 16), 53 * 32768.0 - 1024, AL.is_ge)
+            ts(V("qz", 16, 16 + nb), V("hz", 0, nb), 52 * 32768.0 + 1024, AL.is_ge)
             swap("p7", nb, "qz", 16, nb, 1, "b")
-            cp(V("qf", 0, 2 * nb), V("p7", 0, 2 * nb))
-        for c in range(len(chunks)):
-            c0, c1 = chunks[c]
+            swap("p7", 2 * nb, "qz", 16, nb, 1, "b")
+            act(V("qf", 0, 3 * nb), V("p7", 0, 3 * nb), AF.Copy)
+        for c, (c0, c1) in enumerate(chunks(t, 1)):
             b0, bn = c0 // 16, (c1 - c0) // 16
-            ts(V(liu, c0, c1), X(llw, V(qg, b0, b0 + bn)), b2, AL.subtract)
-            if not last:
-                act(V("lik", c0, c1), X(llw, V(qg, b0, b0 + bn)), AF.Copy)
-            relu = dist(t, 1, c, c0, c1, V("ce", 0, LO[t]), liu, ab2, rl2)
+            tag[0] = "D%d%d" % (t, c)
+            cp(V(liu, c0, c1), X(llw if t else V("dli"), V(qg, b0, b0 + bn)))
+            for pc in pcs[t][1]:
+                if c0 <= pc[0] < c1:
+                    dist(t, 1, pc, V("ce", HD, LO[t]), liu, ab2, rl2)
             if last:
                 continue
-            p = "p%d" % ((c + len(chunks)) % 2)
-            key(p, c0, c1, relu, ab2, rl2, "w2", "lik")
+            ts(V("lih", c0, c1), V(liu, c0, c1), HD - 2048.0, AL.add)
+            p = "p%d" % ((c + len(chunks(t, 0))) % 2)
+            key(p, t, 1, c0, c1, ab2, rl2, "lih")
             tr(V("tk2", c0, c1), V(p, 0, c1 - c0))
-            scan(V("sc2", c0, c1), V("rmin", 0, c1 - c0), V("tk2", c0, c1), AL.add, AL.min)
-            scan(V("sc2", n + c0, n + c1), V("rmax", 0, c1 - c0), V("tk2", c0, c1), AL.add, AL.max)
+            if cfg["pm"][t] == "d" and c0 < S:
+                act(V("wq", c0, min(c1, S)), V(p, 0, min(c1, S) - c0), AF.Identity, MAGIC2)
+            scan(V("sc2", c0, c1), V("rm2", 0, c1 - c0), V("tk2", c0, c1), AL.add, AL.min)
+            scan(V("sc2", n + c0, n + c1), V("rmx", 0, c1 - c0), V("tk2", c0, c1), AL.add, AL.max)
         if last:
             pstage(t)
             continue
-        if cfg["early"][t + 1]:
+        nnq = V("nn", HD + QL[t], HD + QL[t] + n)
+        act(V("lik", 0, n), X(llw, V(qg, 0, nb)), AF.Copy)
+        act(nnq, X(nnw, V(qg, 0, nb)), AF.Copy)
+        d1 = ahead(t + 1)
+        tag[0] = "E%d" % t
+        if cfg["cfrom"]:
+            cp(V("candu", 0, S), V("nn", HD + QL[t], HD + QL[t] + S))
+        else:
             cp(V("candu", 0, S), X(nnw, V(qg, 0, 10)))
-            c1 = cfg["cut"][t + 1][0]
-            dist(t + 1, 0, 0, 0, c1, V("kk", 0, QL[t]), "candu", "ab1", "rl1")
-            dist(t + 1, 0, 1, c1, S, V("kk", 0, QL[t]), "candu", "ab1", "rl1")
+        for pc in pcs[t + 1][0]:
+            if pc[1] <= S:
+                dist(t + 1, 0, pc, kkw, "candu", "ab1", "rl1")
 
         def sm(j, w=1):
-            return V("sm", 16 * j, 16 * j + (nb if w == 1 else 32))
+            return V("sm", 32 * j + 32, 32 * j + 32 + w * nb)
+        tag[0] = "W%d" % t
         for r in range(16):
             mm(V("p5", r, n, 16), V("sel", 128 * r, 128 * r + 128), V("qh", 0, nb))
         cp(V("qr", 0, n), V("p5", 0, n))
-        act(V("p5", 256, 256 + n), V("p5", 0, n), AF.Identity, C("col", 16 + t), C("rm", t))
-        act(V("nnq", 0, n), X(nnw, V(qg, 0, nb)), AF.Copy)
-        act(V("g1", 0, n), V("nnq", 0, n), AF.Identity, 0.0, C("nrm", t))
-        act(V("ct", 0, n), V("iof", 0, n), AF.Identity, C("col", 12 + t), C("rm", 8 + t))
-        tt(V("nn", QL[t], QL[t] + n), V("g1", 0, n), V("p5", 256, 256 + n), AL.add)
+        if t < 2:
+            act(V("qrf", 0, n), V("p5", 0, n), AF.Identity, 896.0)
         mm(V("p5", 256, 256 + n), V("nib"), V("thr", 0, n), True, False)
+        if n > S:
+            act(V("vd"), xl(t, S, n), AF.Relu, -15.0 / 16, 1.0 / 16)
+            mm(V("p5", 256 + S, 256 + n), V("bo"), V("vd"), False, False)
         for b in range(nb):
             e0 = 256 * b
             ts(V("eq", e0, e0 + n - 16 * b), V("qr", 16 * b, n), C("qf", b), AL.is_equal, 2.0 ** (99 - 15 * b), AL.mult)
             mm(V("p5", 256 + 16 * b, 256 + n), V("ewd"), V("eq", e0, e0 + n - 16 * b), False, b == nb - 1)
-        if cfg["winact"]:
-            act(V("winr", 0, n), V("p5", 256, 256 + n), AF.Sign, 0.0, -1.0)
-        else:
-            ts(V("winr", 0, n), V("p5", 256, 256 + n), 0.0, AL.is_lt)
+        act(V("winr", 0, n), V("p5", 256, 256 + n), AF.Sign, 0.0, -1.0)
         for r in range(16):
-            mm(V("p5", 0, nb), V("w1", 15 - r, 143 - r), V("winr", r, n, 16), r == 0, r == 15)
-        own, ownm = V("own", 32 * t, 32 * t + nb), V("own", 32 * t + 16, 32 * t + 16 + nb)
-        qf, far = V("qf", 0, nb), V("qf", nb, 2 * nb)
-        wl, ndq, wf0 = sm(0), sm(1), sm(2)
-        if t == 0:
-            act(wl, V("p5", 0, nb), AF.Relu, 0.0, 2.0 ** -19)
-        else:
-            ts(sm(3), V("jg", 0, nb), C("lb%d" % t, H), AL.is_lt, 2.0 ** -19, AL.mult)
-            if cfg["winact"]:
-                act(V("wg", 0, nb), V("p5", 0, nb), AF.Relu)
-            tt(wl, V("wg" if cfg["winact"] else "p5", 0, nb), sm(3), AL.mult)
+            mm(V("p5", 0, nb), V("w0", 15 - r, 143 - r), V("winr", r, n, 16), r == 0, r == 15)
+        et, et0 = V("lc", ET[t], ET[t] + 2 * nb), V("lc", ET[t], ET[t] + nb)
+        qf = V("qf", 0, nb)
         if t == 1:
-            tt(sm(4), qf, V("stf"), AL.subtract)
-            ts(sm(4), sm(4), 896.0, AL.add, 2.0 ** 19, AL.mult)
-            tt(sm(4), sm(4), sm(3), AL.mult)
-            tt(sm(4), sm(4), V("stf"), AL.add)
-            cp(V("cl2"), sm(4))
-        tt(ndq, ownm, qf, AL.subtract)
-        act(sm(5), ndq, AF.Identity, -256.0, -1.0)
-        tt(wf0, wl, far, AL.mult)
-        tt(sm(6), wl, ndq, AL.mult)
-        tt(V("et%d" % t, 0, nb), own, sm(6), AL.subtract)
-        tt(sm(8), ndq, wf0, AL.mult)
-        tt(sm(9), sm(5), wf0, AL.mult)
-        tu = "tu%d" % t
-        mn = V("p7", 64, 64 + nb)
-        th = 37 * 65536.0
-        if cfg["flagz"]:
-            ts(V("nz", 0, nb), V("sc2", 15, n, 16), th, AL.is_ge)
-            swap("p7", 128, "nz", 0, nb, 1, "b")
-            swap("p7", 144, "nz", 0, nb, 1, "b")
-            nu = ("p7", 128)
-        else:
-            swap("p7", 64, "sc2", 15, 2 * nb, 16, "")
-            ts(sm(11), mn, th, AL.is_ge)
-            ts(sm(10), mn, th, AL.is_ge)
-            nu = ("sm", 160)
-        if nb == 16:
-            tt(sm(12, 2), sm(8, 2), V(nu[0], nu[1], nu[1] + 32), AL.mult)
-            tt(V("ti", 0, 32), sm(12, 2), V("et%d" % t), AL.add)
-            cp(V(tu, 0, 32), V("ti", 0, 32))
-        else:
-            for j in (1, 0):
-                tt(sm(12 + j), sm(8 + j), V(nu[0], nu[1], nu[1] + nb), AL.mult)
-                tt(V("ti", 16 * j, 16 * j + nb), sm(12 + j), V("et%d" % t, 16 * j, 16 * j + nb), AL.add)
-                cp(V(tu, 16 * j, 16 * j + nb), V("ti", 16 * j, 16 * j + nb))
-        tt(X(V("nn", 0, QL[t] + 512), V(tu, 16, 16 + nb)), V("nnq", 0, n), V("ct", 0, n), AL.max)
+            for r in range(16):
+                mm(V("p5", 32, 38), V("w0", 15 - r, 143 - r), V("vd", r, H, 16), r == 0, r == 15)
+        for j in range(2):
+            act(V("sm", 32 + j * nb, 32 + (j + 1) * nb), V("p5", 0, nb), AF.Relu, 0.0, 1.0 / 16)
+        if t == 1:
+            w = V("sm", 240, 246)
+            tt(w, V("qf", 10, 16), V("stm", 10, 16), AL.subtract)
+            tt(w, w, V("p5", 32, 38), AL.mult)
+            tt(w, V("qf", 10, 16), w, AL.subtract)
+            ts(V(qg, 10, 16), w, 896.0, AL.add)
         if t < 2:
-            tt(V("nw", 0, 10), V("sm", 0, 10), V(nu[0], nu[1], nu[1] + 10), AL.mult)
-        if cfg["flagz"]:
-            swap("p7", 64, "sc2", 15, 2 * nb, 16, "")
-        ts(sm(7), mn, th, AL.is_lt)
-        tt(sm(7), mn, sm(7), AL.mult)
-        if cfg["flagz"]:
-            ts(sm(11), V("p7", 64 + nb, 64 + 2 * nb), -1.0, AL.mult, float(MX), AL.add)
-            tt(V("mi", 16, 16 + nb), sm(11), V("p7", 128, 128 + nb), AL.mult)
-        else:
-            act(V("nx", 0, nb), V("p7", 64 + nb, 64 + 2 * nb), AF.Identity, float(MX), -1.0)
-            tt(V("mi", 16, 16 + nb), V("nx", 0, nb), sm(10), AL.mult)
+            tt(V("sm", 22, 32), V("sm", 32, 42), V("lc", 0, 10), AL.mult)
+            if d1 > S:
+                cp(V("candu", S, HD), X(nnw, V(qg, 10, 16)))
+        tt(sm(1), et0, qf, AL.subtract)
+        act(V("sm", 64 + nb, 64 + 2 * nb), sm(1), AF.Identity, float(QL[t] + HD), -1.0)
+        tt(sm(2, 2), sm(1, 2), sm(0, 2), AL.mult)
+        tt(et0, et0, sm(2), AL.subtract)
+        tt(sm(3, 2), sm(2, 2), V("qf", nb, 3 * nb), AL.mult)
+        th = 37 * 65536.0 - 63488.0
         if t < 2:
-            mm(V("p7", 160, 171), V("lt"), V("nw", 0, 11), True, False)
-            for s in range(1, 11):
-                mm(V("p7", 160 + s, 171), V("bo"), V("nw", 0, 11 - s), False, s == 10)
-            tt(V("sm", 224, 234), V("p7", 160, 170), V("pj", 0, 10), AL.min)
-            cp(V("sm", 240, 241), C("p7", 170))
-            ts(V("pos%d" % t, 0, 10), V("sm", 224, 234), 512.0, AL.add)
+            tag[0] = "G%d" % t
+            ts(V("nz", 0, 10), V("sc2", 15, S, 16), th, AL.is_ge)
+            swap("p7", 96, "nz", 0, 10, 1, "b")
+            swap("p7", 106, "nz", 0, 10, 1, "b")
+            tt(V("nw", 0, 20), V("sm", 22, 42), V("p7", 96, 116), AL.mult)
+            mm(V("p7", 176, 186), V("ib"), V("cst", 0, 10), True, False)
+            mm(V("p7", 176, 186), V("ib"), V("nw", 0, 10), False, False)
+            mm(V("p7", 176, 186), V("lt"), V("nw", 10, 20), False, False)
+            for s in range(1, 10):
+                mm(V("p7", 176 + s, 186), V("bo"), V("nw", 10, 20 - s), False, s == 9)
+            ts(V("pos%d" % t, 0, 10), V("p7", 176, 186), 0.0, AL.add)
             gx = "gx%d" % t
             cp(X(V(gx), V("pos%d" % t, 0, 10)), xt)
-            act(C(gx, H), V("sm", 240, 241), AF.Copy)
-            send(V("lb%d" % (t + 1)), V(gx, 0, 112), "rx%d" % t, t)
-        tt(V("mi", 0, nb), sm(7), V("lane", 0, nb), AL.max)
-        ts(V("ti", 32, 32 + nb), V("mi", 0, nb), 4095, AL.bitwise_and)
-        cp(V(tu, 32, 32 + nb), V("ti", 32, 32 + nb))
-        if nb == 16:
-            ts(V("kab"), V("mi"), 12, AL.arith_shift_right, 15, AL.bitwise_and)
-        else:
-            for j in range(2):
-                ts(V("kab", 16 * j, 16 * j + nb), V("mi", 16 * j, 16 * j + nb), 12, AL.arith_shift_right, 15, AL.bitwise_and)
-        tt(V("ks", 0, nb), V("kab", 0, nb), V("kab", 16, 16 + nb), AL.add)
+            send(xl(t + 1, S, HD), V(gx, S, HD), "rx%d" % t, "tx%d" % t, t)
+            tag[0] = "H%d" % t
+            for pc in pcs[t + 1][0]:
+                if S < pc[1] <= d1:
+                    dist(t + 1, 0, pc, kkw, "candu", "ab1", "rl1")
+        tag[0] = "L%d" % t
+        tu = "tu%d" % t
+        z0 = 10 if t < 2 else 0
+        if nb > z0:
+            ts(V("nz", z0, nb), V("sc2", 16 * z0 + 15, n, 16), th, AL.is_ge)
+            swap("p7", 128, "nz", 0, nb, 1, "b")
+            swap("p7", 128 + nb, "nz", 0, nb, 1, "b")
+        nu = V("p7", 128, 128 + 2 * nb) if nb > z0 else V("p7", 96, 116)
+        tt(sm(4, 2), sm(3, 2), nu, AL.mult)
+        tt(sm(4, 2), sm(4, 2), et, AL.add)
+        ts(V(tu, 0, 2 * nb), sm(4, 2), 896.0, AL.add)
+        tt(X(V("nn", 0, HD + QL[t]), V(tu, nb, 2 * nb)), nnq, V("ct", 256 * t, 256 * t + n), AL.max)
+        if t < 2:
+            dma("s", P(nnq, t), P(V("qrf", 0, n), t), 2200)
+        swap("p5", 0, "sc2", 15, 2 * nb, 16, "")
+        act(V("rr", 0, nb), V("p5", 0, nb), AF.Relu, th - 1.0, -1.0)
+        act(V("lx", 16 - nb, 16), V("p5", nb, 2 * nb), AF.Identity, 2048.0)
+        tt(V("mi", 0, 2 * nb), V("lx", 16 - nb, 16 + nb), nu, AL.mult)
+        tt(V("mi", nb, 2 * nb), V("mi", nb, 2 * nb), V("rr", 0, nb), AL.add)
+        ts(V("ti", 0, nb), V("mi", nb, 2 * nb), 4095, AL.bitwise_and)
+        ts(V(tu, 2 * nb, 3 * nb), V("ti", 0, nb), -1.0, AL.mult, 4095.0, AL.add)
+        ts(V("kab", 0, 2 * nb), V("mi", 0, 2 * nb), 12, AL.arith_shift_right, 15, AL.bitwise_and)
+        tt(V("ks", 0, nb), V("kab", 0, nb), V("kab", nb, 2 * nb), AL.add)
         for r in range(16):
             mm(V("p5", r, n, 16), V("sel", 128 * r, 128 * r + 128), V("ks", 0, nb))
         act(V("sq", 0, n), V("p5", 0, n), AF.Square, k64, 64.0)
         mm(V("p5", 256, 256 + n), V("ib"), V("iob", 0, n), True, False)
         mm(V("p5", 256, 256 + n), V("nib"), V("sq", 0, n), False, True)
-        act(V("zz", 0, n), V("p5", 256, 256 + n), AF.Identity, C("col", 8 + t))
+        act(V("zz", 0, n), V("p5", 256, 256 + n), AF.Identity, float(LO[t] - HD))
         tt(X(V("ll", 0, QL[t] + n), V(tu, 0, nb)), V("zz", 0, n), V("lik", 0, n), AL.max)
-        act(V("ce", LO[t], LO[t] + n), X(V("ce", 0, LO[t]), V(tu, 32, 32 + nb)), AF.Copy)
+        act(V("ce", LO[t], LO[t] + n), X(V("ce", 0, LO[t]), V(tu, 2 * nb, 3 * nb)), AF.Copy)
         pstage(t)
     return ops
 
@@ -592,7 +725,6 @@ def graph(cfg):
     for i in range(n):
         o = ops[i]
         deps = {}
-        soft = {}
         acc = [(v, False) for v in o["r"] if v[0] not in DRAM] + [(v, True) for v in o["w"] if v[0] not in DRAM]
         for v, w in acc:
             lst = seen.setdefault(v[0], [])
@@ -604,19 +736,15 @@ def graph(cfg):
                     deps[j] = True
             for j, u, uw in lst:
                 if (w or uw) and meet(u, v):
-                    if w and not uw and not cfg["war"] and ops[j]["e"] == o["e"] and o["e"] in "va" and ops[j]["k"] != "dma":
-                        soft[j] = True
-                    else:
-                        deps[j] = True
+                    deps[j] = True
         for v, w in acc:
             lst = seen[v[0]]
-            if w and v[3] == 1 and not psum(v):
+            if w and v[3] == 1 and len(v) == 4 and not psum(v):
                 lst[:] = [e for e in lst if not (e[1][1] >= v[1] and e[1][2] <= v[2])]
             lst.append((i, v, w))
         deps.pop(i, None)
-        soft.pop(i, None)
         o["d"] = sorted(deps)
-        o["s"] = list(o["d"]) + sorted(soft) + ([o["x"]["from"]] if o["k"] == "recv" else [])
+        o["s"] = list(o["d"]) + ([o["x"]["from"]] if "from" in o["x"] else [])
     lastmm = {}
     for i in range(n):
         o = ops[i]
@@ -640,8 +768,36 @@ def gap(o, q, i, m):
     return m["x"]
 
 
-def schedule(ops, cfg, m):
+def schedule(full, cfg, m):
+    ops, of, last = [], [], {}
+    for i in range(len(full)):
+        o = full[i]
+        if o["k"] == "mm":
+            b = o["w"][0][0]
+            ext = set(j for j in o["s"] if full[j]["e"] != "t")
+            z = last.get(b)
+            if (z is not None and full[i - 1]["k"] == "mm" and of[i - 1] == z and ext <= ops[z]["ext"]
+                    and ops[z]["m"][1] < cfg["tmax"]):
+                q = ops[z]
+                q["m"] = (q["m"][0] + o["m"][0], q["m"][1] + o["m"][1], "p")
+                q["sub"].append(i)
+                q["s"] = sorted(set(q["s"]) | set(of[j] for j in o["s"] if of[j] != z))
+                of.append(z)
+                continue
+            last[b] = len(ops)
+        of.append(len(ops))
+        ops.append({"e": o["e"], "k": o["k"], "m": o["m"], "x": o["x"], "g": o["g"], "sub": [i], "s": sorted(set(of[j] for j in o["s"])),
+                    "h": set(of[j] for j in o["h"]), "ext": set(j for j in o["s"] if full[j]["e"] != "t")})
     n = len(ops)
+    anc = []
+    for i in range(n):
+        far = 0
+        for j in ops[i]["s"]:
+            far |= anc[j]
+        ops[i]["s"] = [j for j in ops[i]["s"] if not far >> j & 1]
+        for j in ops[i]["s"]:
+            far |= 1 << j
+        anc.append(far)
     succ = [[] for _ in range(n)]
     for i in range(n):
         for j in ops[i]["s"]:
@@ -654,10 +810,30 @@ def schedule(ops, cfg, m):
     fw = [[(j, tl[i] + gap(ops[i], ops[j], i, m)) for j in succ[i]] for i in range(n)]
     bw = [[(j, tl[j] + gap(ops[j], ops[i], j, m)) for j in ops[i]["s"]] for i in range(n)]
     eng = [o["e"] for o in ops]
+    tabs = [([cost(o, q) for o in ops], [o["x"].get("lat", 0.0) * q["d"] for o in ops],
+             [[(j, gap(ops[j], ops[i], j, q)) for j in ops[i]["s"]] for i in range(n)]) for q in SETS]
+
+    def value(seq):
+        tot = 0.0
+        for c, lat, pre in tabs:
+            free, fin, end = {}, [0.0] * n, 0.0
+            for i in seq:
+                s = free.get(eng[i], 0.0)
+                for j, w in pre[i]:
+                    if fin[j] + w > s:
+                        s = fin[j] + w
+                free[eng[i]] = s + c[i]
+                fin[i] = s + c[i] + lat[i]
+                if fin[i] > end:
+                    end = fin[i]
+            tot += end
+        return tot
 
     def sweep(pri, nxt, prv, first):
         left = [len(x) for x in prv]
         ready = list(first)
+        if nxt is fw:
+            pri = [1e9 - i if "load" in ops[i]["x"] else pri[i] for i in range(n)]
         pool = {}
         for i in range(n):
             if left[i] == 0:
@@ -690,33 +866,107 @@ def schedule(ops, cfg, m):
                     pool.setdefault(eng[j], []).append(j)
         return seq, st
 
+    def timing(seq, tab):
+        c, lat, pre = tab
+        free, last, fin, par, end, top = {}, {}, [0.0] * n, [-1] * n, 0.0, -1
+        for i in seq:
+            e = eng[i]
+            s, p = free.get(e, 0.0), last.get(e, -1)
+            for j, w in pre[i]:
+                if fin[j] + w > s:
+                    s, p = fin[j] + w, j
+            free[e], last[e], par[i] = s + c[i], i, p
+            fin[i] = s + c[i] + lat[i]
+            if fin[i] > end:
+                end, top = fin[i], i
+        return end, par, top
+
+    def polish(seq):
+        prs = [set(o["s"]) for o in ops]
+        res = [timing(seq, tab) for tab in tabs]
+        val = sum(r[0] for r in res)
+        keep = (val, seq)
+        for it in range(cfg["sa"]):
+            temp = cfg["temp"] * (1.0 - it / cfg["sa"])
+            _, par, i = res[rs.randint(len(res))]
+            cand = []
+            while i >= 0:
+                p = par[i]
+                if p >= 0 and eng[p] == eng[i] and p not in prs[i] and "load" not in ops[p]["x"]:
+                    cand.append((p, i))
+                i = p
+            if not cand:
+                break
+            p, i = cand[rs.randint(len(cand))]
+            a, b = seq.index(p), seq.index(i)
+            e = eng[i]
+            hop = rs.randint(4)
+            if rs.uniform() < 0.5:
+                while hop and a > 0 and "load" not in ops[seq[a - 1]]["x"]:
+                    a -= 1
+                    hop -= eng[seq[a]] == e
+                mark, engs, move = set(prs[i]), set(), [i]
+                for k in range(b - 1, a - 1, -1):
+                    j = seq[k]
+                    if j in mark or eng[j] in engs:
+                        move.append(j)
+                        mark |= prs[j]
+                        engs.add(eng[j])
+                ms = set(move)
+                new = seq[:a] + move[::-1] + [j for j in seq[a:b + 1] if j not in ms] + seq[b + 1:]
+            else:
+                while hop and b < n - 1:
+                    b += 1
+                    hop -= eng[seq[b]] == e
+                ms, engs, move = {p}, set(), [p]
+                for k in range(a + 1, b + 1):
+                    j = seq[k]
+                    if eng[j] in engs or not ms.isdisjoint(prs[j]):
+                        move.append(j)
+                        ms.add(j)
+                        engs.add(eng[j])
+                new = seq[:a] + [j for j in seq[a:b + 1] if j not in ms] + move + seq[b + 1:]
+            if new == seq:
+                continue
+            r2 = [timing(new, tab) for tab in tabs]
+            v2 = sum(r[0] for r in r2)
+            if v2 <= val - temp * math.log(1.0 - rs.uniform()):
+                seq, res, val = new, r2, v2
+                if val < keep[0]:
+                    keep = (val, seq)
+        return keep[1]
+
+    tags = sorted(set(o["g"] for o in ops))
     rs = np.random.RandomState(cfg["seed"])
     best = None
     for _ in range(cfg["iters"] + 1):
         seq, st = sweep(pr, fw, bw, [0.0] * n)
-        end = max(st[i] + cs[i] + tl[i] for i in range(n))
-        if best is None or end < best[0]:
-            best = (end, seq, st)
+        val = value(seq)
+        if best is None or val < best[0]:
+            best = (val, seq, st)
         z = rs.standard_normal(n) * cfg["noise"]
         back = sweep([st[i] + cs[i] + float(z[i]) for i in range(n)], bw, fw, tl)[1]
         pr = [back[i] + cs[i] for i in range(n)]
-    if cfg["ils"]:
-        best = (sum(replay(ops, best[1], q) for q in SETS), best[1], best[2])
+    if cfg["boost"]:
+        seq, st = sweep([-best[2][i] + cfg["boost"].get(ops[i]["g"], 0.0) for i in range(n)], fw, bw, [0.0] * n)
+        best = (value(seq), seq, st)
     for _ in range(cfg["ils"]):
-        t0, wd, sg = rs.uniform(0, 100000), rs.uniform(3000, 15000), (200.0, 600.0, 1500.0)[rs.randint(3)]
+        t0, wd, sg = rs.uniform(0, 85000), rs.uniform(3000, 15000), (200.0, 600.0, 1500.0)[rs.randint(3)]
         z = rs.standard_normal(n) * sg
         keep = rs.uniform(size=n) < rs.uniform(0.1, 1.0)
         pri = [-best[2][i] + (float(z[i]) if keep[i] and t0 <= best[2][i] < t0 + wd else 0.0) for i in range(n)]
+        if rs.uniform() < cfg["ptag"]:
+            mv = {tags[rs.randint(len(tags))]: float(rs.standard_normal()) * 5000.0 for _ in range(1 + rs.randint(2))}
+            pri = [-best[2][i] + mv.get(ops[i]["g"], 0.0) for i in range(n)]
         seq, st = sweep(pri, fw, bw, [0.0] * n)
         if rs.uniform() < 0.3:
             back = sweep([st[i] + cs[i] for i in range(n)], bw, fw, tl)[1]
             seq, st = sweep([back[i] + cs[i] for i in range(n)], fw, bw, [0.0] * n)
-        val = sum(replay(ops, seq, q) for q in SETS)
+        val = value(seq)
         if val <= best[0]:
             best = (val, seq, st)
-    for i in range(n):
-        ops[i]["t"] = best[2][i]
-    return best[1]
+    seq = polish(best[1]) if cfg["sa"] else best[1]
+    return [j for i in seq for j in ops[i]["sub"]]
 
 
 def replay(ops, seq, m):
@@ -751,8 +1001,8 @@ def plan(cfg):
             for j in o["d"]:
                 q = ops[j]
                 if "sem" in q["x"]:
-                    if ("x", j) not in got:
-                        got[("x", j)] = True
+                    if ("x", q["x"]["sem"]) not in got:
+                        got[("x", q["x"]["sem"])] = True
                         own.append(j)
                 elif not (e == "t" and q["e"] == "t"):
                     need[q["e"]] = max(need.get(q["e"], -1), place[j])
@@ -774,7 +1024,6 @@ def plan(cfg):
 
 
 PLAN = []
-ENG = 4
 QSEM = {"v": "sv", "a": "sa", "t": "sp", "g": "sg"}
 
 
@@ -793,6 +1042,10 @@ def rank_program(g, core, T, topo):
             return v
         if v[0] == "ind":
             return ap(v[1]).indirect(ap(v[2]))
+        if v[0] == "wd":
+            return T.wd[:, v[1], :] if v[2] - v[1] == 1 else T.wd[:]
+        if len(v) > 4:
+            return T[v[0]][v[4][0]:v[4][1]:v[4][2], v[1]:v[2]]
         if v[3] == 1:
             return T[v[0]][:, v[1]:v[2]]
         return T[v[0]][:, v[1]:v[1] + (cnt(v) - 1) * v[3] + 1:v[3]]
@@ -802,19 +1055,20 @@ def rank_program(g, core, T, topo):
         for i in order[e]:
             o = ops[i]
             for j in o["wo"]:
-                q.wait_ge(T.sem[ops[j]["x"]["sem"]], ENG if ops[j]["k"] == "recv" else 16)
+                q.wait_ge(T.sem[ops[j]["x"]["sem"]], ops[j]["x"]["val"])
             for j in o["wq"]:
                 q.wait_ge(T.sem[QSEM[ops[j]["e"]]], ops[j]["n"])
             k = o["k"]
             if k == "send":
                 dst = T.cores[(rank + 1 + o["a"][3] % (nr - 1)) % nr]
                 rid, pid, _ = topo.addr(dst)
-                mask = sum(1 << x for x in topo.engines(core, dst)[:ENG])
-                g.remote_dma(ap(o["a"][0]), ap(o["a"][1]), T.sem[o["a"][2]], T.sem.sent, pid, rid, mask)
+                mask = sum(1 << x for x in topo.engines(core, dst)[slice(*CFG["eng"])])
+                g.remote_dma(ap(o["a"][0]), ap(o["a"][1]), T.sem[o["a"][2]], T.sem[o["a"][4]], pid, rid, mask)
                 continue
             a = [ap(v) for v in o["a"]]
             if k == "dma":
-                q.dma_start(a[0], a[1]).then_inc(T.sem[o["x"]["sem"]], 16)
+                ins = q.dma_start(a[0], a[1], accum_op=AL.add) if a[2] else q.dma_start(a[0], a[1])
+                ins.then_inc(T.sem[o["x"]["sem"]], 16)
                 continue
             if k == "cp":
                 ins = q.tensor_copy(a[0], a[1])
@@ -841,7 +1095,8 @@ def rank_program(g, core, T, topo):
                 ins = q.affine_select(*a)
             if "n" in o:
                 ins.then_inc(T.sem[QSEM[e]], 1)
-    g.wait_ge(T.sem.sent, 4 * ENG)
     for o in ops:
+        if o["k"] == "send":
+            g.wait_ge(T.sem[o["a"][4]], ENG)
         if o["k"] == "dma" and o["a"][0][0] == "yp":
             g.sync.wait_ge(T.sem[o["x"]["sem"]], 16)

@@ -1,5 +1,6 @@
 import math
 import numpy as np
+from concourse.bass import DstId, RemoteDMATransfer
 from concourse.mybir import AluOpType, ActivationFunctionType
 
 AL = AluOpType
@@ -9,6 +10,7 @@ HD = 256
 QL = (1024, 1184, 1440, 1696)
 LO = (3328, 3488, 3744, 4000)
 NL = (160, 256, 256, 160)
+XO = (0, 2560, 6656, 10752)
 MAGIC = 1.5 * 2.0 ** 34
 MAGIC2 = 1.5 * 2.0 ** 39
 F, B, I, U, HF = "float32", "bfloat16", "int32", "uint16", "float16"
@@ -20,15 +22,24 @@ CFG = {
     "scan": (0, 0, 0, 3),
     "pgrp": 160, "seed": 768, "noise": 200.0, "xe0": 6, "look": 0.3, "iters": 6, "selv": 8, "sela": 0,
     "bigp": 0, "gp": 48, "ils": 1000, "ug": 4, "ig": 0, "xeg": 0, "fixr": 0, "zv": 0, "seld": 0, "tmax": 1200,
-    "boost": {}, "ptag": 0.3, "sa": 0, "temp": 300.0,
+    "sa2": 0, "temp2": 50.0, "phs": 0, "ptemp": 500.0, "wmean": 0.0, "pany": 0.0, "slack": 150.0, "boost": {}, "ptag": 0.3, "sa": 0, "temp": 300.0,
 }
 
 CFG.update({
     "cut": (((96,), (96,)), ((160,), (160,)), ((160,), (160,)), ((128,), (128,))), "eg": 1, "fixt": 1, "wd": 1,
-    "kv": ((0, 0), (0, 0), (0, 0), (0, 0)), "eng": (0, 16, 2), "fsplit": (0, 1, 1, 0), "pm": "ddde", "ch": (2, 2, 1, 1), "wdep": 0, "xe0": 11, "acm": "v", "seld": 1,
+    "kv": ((0, 0), (0, 0), (0, 0), (0, 0)), "eng": (0, 16, 2), "bk": "23", "bk3": "23", "bke": "45", "prune": 1, "x23": 0, "fixa": (0, 0, 0, 0), "pouta": 1, "pk": (5, 5, 4, 2),
+    "feng": (0, 16, 1), "fmax": 96, "flat": 14.0, "fsplit": (0, 1, 1, 0), "pm": "ddde", "ch": (2, 2, 1, 1), "wdep": 0, "xe0": 11, "acm": "v", "seld": 1,
     "zv": 1, "pgrp": 96, "ils": 600, "ptag": 0.5, "sa": 8000, "temp": 200.0, "seed": 2,
     "pc": (("a32 v64 v32 a32", "v64 a32 v32 a32"), ("v64 v32 a32 a32 k96", "v64 a32 a32 v32 k96"),
            ("v64 a32 v64 k96", "v64 a32 a32 a32 k96"), ("a32 v64 a32 a32", "v32 a32 a32 a32 a32")),
+})
+
+CFG.update({
+    "zv": 0, "fsplit": (0, 1, 0, 1), "ils": 60, "sa": 1500, "temp": 60.0, "seed": 127, "noise": 600.0, "iters": 12,
+    "sa2": 30000, "temp2": 60.0,
+    "ug": 2, "fixa": (0, 0, 0, 1), "gp": 32, "fsplit": (0, 1, 1, 0), "seed": 214, "sa2": 25000,
+    "pc": (("a32 v64 v32 a32", "v32 v32 a32 v32 a32"), ("v64 v32 a32 v32 k96", "v64 a32 a32 v32 k96"),
+           ("v64 m64 v32 k96", "v64 m64 a32 k96"), ("v64 m96", "v32 a32 a32 a32 a32")),
 })
 
 SB = {
@@ -40,14 +51,14 @@ SB = {
     "sel": (2048, B), "lt": (128, B), "ewd": (128, B), "smask": (512, F),
     "pi": (8, I), "col": (32, F), "pw": (8, B), "rm": (16, F), "i16": (16, F),
     "iob": (256, B), "iof": (768, F), "cix": (256, B), "thr": (256, B), "rm1": (256, F), "rm2": (256, F), "rmx": (256, F),
-    "lc": (112, F), "lx": (32, F), "stm": (16, F), "stu": (16, U), "cst": (16, B), "zb": (256, B), "cz": (256, HF),
+    "lc": (184, F), "lx": (32, F), "stm": (16, F), "stu": (16, U), "cst": (16, B), "zb": (512, B), "xb": (320, B), "cz": (256, HF),
     "candu": (256, U), "c16": (256, HF), "lih": (256, HF), "qrf": (256, F), "ct": (768, F),
     "ab1": (4096, B), "ab20": (4096, B), "ab21": (4096, B), "graw": (4096, B), "wt": (2560, F), "prod": (2560, F),
-    "rl1": (2560, B), "rl20": (2560, B), "rl21": (2560, B), "lik": (256, F), "sq": (256, B),
+    "rl1": (4096, B), "rl20": (4096, B), "rl21": (4096, B), "lik": (256, F), "sq": (256, B),
     "tk": (256, F), "tk2": (256, F), "sc": (256, F), "sc2": (512, F), "hz": (16, F), "qz": (32, HF), "qf": (48, F),
     "qh": (16, HF), "qr": (256, HF), "vd": (96, B), "wq": (160, F), "wc": (160, F), "lz": (160, HF), "lk": (160, U),
     "eq": (4096, B), "winr": (256, B), "sm": (256, F), "mi": (32, I), "kab": (32, I), "ti": (16, I), "rr": (16, F),
-    "ks": (16, B), "nw": (32, B), "zz": (256, F), "uu": (160, F), "xe": (10240, B), "nz": (16, B),
+    "ks": (16, B), "nw": (32, B), "zz": (256, F), "uu": (160, F), "xe": (13312, B), "nz": (16, B),
     "wr": (432, B), "fx": (16, U), "dfx": (256, B), "rfx": (256, B),
 }
 for _t in range(4):
@@ -67,13 +78,15 @@ for _t in range(8):
 SCRATCH["wd"] = ("dram", [8, 4, 2560], F)
 NDMA = 48
 SEMAPHORES = (["sv", "sa", "sp", "sg", "rx0", "rx1", "ra0", "ra1", "tx0", "tx1", "ta0", "ta1", "wz", "ws"]
-              + ["w%s%d" % (_a, _t) for _a in "ab" for _t in range(3)] + ["d%d" % _t for _t in range(NDMA)])
+              + ["w%s%d" % (_a, _t) for _a in "abc" for _t in range(3)] + ["d%d" % _t for _t in range(NDMA)])
 DRAM = ("kq", "cc", "aa", "xs", "ys", "nb", "dl", "st", "yp")
+SEMAPHORES += ["f%s%d%d" % (_a, _t, _j) for _a in "abcd" for _t in (1, 2, 3) for _j in range(3)]
 ENG = len(range(*CFG["eng"]))
+FENG = len(range(*CFG["feng"]))
 
-NOM = {"c": 0.95, "g": 1.48, "s": 3.6, "p": 0.48, "x": 130.0, "y": 90.0, "d": 1.2, "i": 150.0}
-SETS = [NOM, {"c": 0.85, "g": 1.0, "s": 2.0, "p": 0.43, "x": 150.0, "y": 100.0, "d": 1.4, "i": 250.0},
-        {"c": 1.15, "g": 2.2, "s": 5.5, "p": 0.6, "x": 120.0, "y": 80.0, "d": 1.1, "i": 100.0}]
+NOM = {"c": 0.86, "g": 1.34, "s": 3.2, "p": 0.43, "x": 165.0, "y": 140.0, "d": 0.85, "i": 120.0}
+SETS = [NOM, {"c": 1.08, "g": 1.25, "s": 2.5, "p": 0.54, "x": 140.0, "y": 120.0, "d": 1.1, "i": 180.0},
+        {"c": 1.1, "g": 2.1, "s": 5.2, "p": 0.55, "x": 165.0, "y": 140.0, "d": 0.7, "i": 80.0}]
 
 
 def V(n, a=0, b=None, s=1):
@@ -198,18 +211,22 @@ def build(cfg):
         if sem is None:
             sem = ("d%d" % nd[0], 16)
             nd[0] += 1
-        add(q, "dma", (out, a, acc), [out], ins, (1000, 0, "c") if q == "g" else (0, 1, "i"), {"sem": sem[0], "val": sem[1], "lat": t})
+        add(q, "dma", (out, a, acc), [out], ins, (1000, 0, "c") if q == "g" else (0, 1, "i"),
+            {"sem": sem[0], "val": sem[1], "lat": t - 1900})
 
-    def send(dst, src, sem, gone, t):
-        sid = add("g", "send", (dst, src, sem, t, gone), [], [src], (400, 0, "c"), {"lat": 2500})
-        add("r", "recv", (), [dst], [], (0, 0, "c"), {"sem": sem, "val": ENG, "from": sid})
-        add("r", "recv", (), [(gone, 0, 1, 1)], [], (0, 0, "c"), {"sem": gone, "val": ENG, "from": sid})
+    def send(dst, src, sem, gone, t, more=0):
+        srcs = list(src) if isview(src[0]) else [src]
+        ne = ENG if t >= 0 else FENG
+        sid = add("g", "send", (dst, src, sem, t, gone), [], srcs, (400, 0, "c"), {"lat": 600 + more})
+        add("r", "recv", (), [dst], [], (0, 0, "c"), {"sem": sem, "val": ne, "from": sid})
+        add("r", "recv", (), [(gone, 0, 1, 1)], srcs, (0, 0, "c"), {"sem": gone, "val": ne, "from": sid})
 
     rot = [0]
 
     def bank():
         rot[0] += 1
-        return "p%d" % (2 + rot[0] % 2)
+        some = cfg["bk3"] if tag[0][:2] == "D3" else cfg["bk"]
+        return "p" + some[rot[0] % len(some)]
 
     pcs = [[pieces(x) for x in y] for y in cfg["pc"]]
     relu = [any(p[2] == "r" for t in range(RO) for p in pcs[t][st]) for st in range(2)]
@@ -219,6 +236,8 @@ def build(cfg):
     def chunks(t, st):
         cuts = (0,) + tuple(cfg["cut"][t][st]) + (NL[t],)
         return [(cuts[c], cuts[c + 1]) for c in range(len(cuts) - 1)]
+
+    XO = (0, 2560, 6656, 6656 + 2560) if cfg["x23"] else (0, 2560, 6656, 10752)
 
     def xl(t, a, b, s=1):
         return V("kk", QL[t] + a, QL[t] + b, s)
@@ -231,6 +250,8 @@ def build(cfg):
     dma("s", V("yb"), V("ys", 0, 640), 5600)
     dma("s", xl(2, 0, S), V("xs", 2 * S, 3 * S), 5800)
     dma("s", xl(3, 0, S), V("xs", 3 * S, 4 * S), 5900)
+    if cfg["x23"]:
+        dma("s", V("xb"), V("xs", 2 * S, 4 * S), 6000)
     for o in ops:
         o["x"]["load"] = True
     iota(C("pi", 0), [[0, 1]], 0, 1)
@@ -238,7 +259,6 @@ def build(cfg):
     asel(V("iw"), V("ones"), [[1, 160]], AL.is_equal, -16, -1)
     asel(V("bt"), V("ones", 0, 128), [[-16, 8], [0, 16]], AL.is_ge, 0, 1)
     asel(V("bo"), V("bt"), [[16, 8], [0, 16]], AL.is_ge, 15, -1)
-    iota(V("i16"), [[1, 16]], 0, 0)
     iota(V("cix"), [[15, 16], [1, 16]], 0, 0)
     iota(V("iob"), [[1, 256]], 0, 0)
     ts(C("pi", 1), C("pi", 0), 15, AL.bitwise_and)
@@ -250,18 +270,25 @@ def build(cfg):
     else:
         cp(kc, C("pi", 1))
     act(k64, kc, AF.Identity, -960.0, 64.0)
-    ts(V("rm"), V("i16"), kc, AL.is_equal)
+    if not cfg["seld"] or cfg["ctm"] != "d":
+        iota(V("i16"), [[1, 16]], 0, 0)
+        ts(V("rm"), V("i16"), kc, AL.is_equal)
     ms(V("w0"), 0.0)
     act(V("w0", 15, 143, 16), V("bo", 0, 128, 16), AF.Copy)
-    if relu[0] or cfg["fixr"]:
+    fold = any(p[2] in "fF" for t in range(RO) for p in pcs[t][0])
+    if relu[0] or cfg["fixr"] or fold:
         ts(V("wn1"), V("w0"), -32768.0, AL.mult)
+    if fold:
+        act(V("wp1"), V("w0"), AF.Copy, 0.0, 32768.0)
+        act(V("wp2"), V("w0"), AF.Copy, 0.0, 65536.0)
+        act(V("nb1"), V("bo"), AF.Copy, 0.0, -32768.0)
     if relu[1]:
         ts(V("wn2"), V("w0"), -65536.0, AL.mult)
     if relue:
         ts(V("nbo"), V("bo"), -65536.0, AL.mult)
     i32 = V("iw", 16, 144)
     for j, (w, val) in enumerate((("iy", 0.25), ("iq", -0.25), ("nib", -1.0), ("ib", 1.0))):
-        if w == "iy" and cfg["acm"] != "t":
+        if w == "iy" and cfg["acm"] == "v":
             continue
         if j < cfg["ig"]:
             asel(V(w), V("bt"), [[1, 128]], AL.is_gt, -200, 0)
@@ -278,17 +305,15 @@ def build(cfg):
         wid = max(b - a for t in range(RO - st) for a, b in chunks(t, st))
         ms(V(w, 0, wid), val)
         ms(V(w, 0, wid, 16), first)
-    if cfg["eg"]:
-        iota(V("zb"), [[0, 256]], 0, 0)
+    ms(V("zb"), 0.0)
     zero = V("ac", 0, HD)
     if cfg["zv"]:
         ms(zero, 0.0)
     else:
         iota(zero, [[0, HD]], 0, 0)
     if cfg["seld"]:
-        ms(V("eq", 0, 512), 0.0)
         for j in range(4):
-            dma("s", V("sel", 512 * j, 512 * j + 512), V("eq", 0, 512), 2300, None, False, ("wz", 64))
+            dma("s", V("sel", 512 * j, 512 * j + 512), V("zb"), 2300, None, False, ("wz", 64))
     for r in range(16):
         if cfg["seld"]:
             dma("s", P(V("sel", 128 * r, 128 * r + 128), r), P(V("bo"), r), 2000, None, False, ("ws", 256))
@@ -303,25 +328,26 @@ def build(cfg):
     ops[-1]["x"]["from"] = len(ops) - 2
     ts(V("ewd"), V("bo"), C("pw", 0), AL.mult)
     asel(V("lt"), V("bo"), [[1, 128]], AL.is_gt, 0, -1)
-    ET = (16, 36, 68)
+    ET = (16, 56, 120)
     iota(V("lc", 0, 16), [[16, 16]], 1, 0)
     for t in range(3):
         nb = NL[t] // 16
-        iota(V("lc", ET[t], ET[t] + 2 * nb), [[-QL[t], 2], [16, nb]], QL[t] - 896, 0)
-    act(V("lc", 0, 100), V("lc", 0, 100), AF.Identity, kc)
+        iota(V("lc", ET[t], ET[t] + 4 * nb), [[-QL[t], 2], [16, nb], [0, 2]], QL[t] - 896, 0)
+    act(V("lc"), V("lc"), AF.Identity, kc)
     act(V("lx", 16, 32), V("lc", 0, 16), AF.Identity, 4096.0, -1.0)
     act(V("cst", 0, 10), V("lc", 0, 10), AF.Identity, 160.0, -1.0)
     for t in range(3):
         if not cfg["fixt"]:
             asel(V("wr", 144 * t, 144 * t + 144), V("w0"), [[-1, 144]], AL.is_equal, 7 - t, 1)
-        iota(V("iof", 256 * t, 256 * t + NL[t]), [[1, NL[t]]], QL[t], 0)
-        ctv = V("ct", 256 * t, 256 * t + NL[t])
+        mct = NL[t] if t < 2 else S
+        iota(V("iof", 256 * t, 256 * t + mct), [[1, mct]], QL[t], 0)
+        ctv = V("ct", 256 * t, 256 * t + mct)
         if cfg["ctm"] == "d":
-            dma("s", ctv, V("ac", 0, NL[t]), 2300)
-            dma("s", P(ctv, 8 + t), P(V("iof", 256 * t, 256 * t + NL[t]), 8 + t), 2200)
+            dma("s", ctv, V("ac", 0, mct), 2300)
+            dma("s", P(ctv, 8 + t), P(V("iof", 256 * t, 256 * t + mct), 8 + t), 2200)
         else:
-            act(ctv, V("iof", 256 * t, 256 * t + NL[t]), AF.Identity, 0.0, C("rm", 8 + t))
-    iota(V("ce", S, HD), [[0, H]], 0, 0)
+            act(ctv, V("iof", 256 * t, 256 * t + mct), AF.Identity, 0.0, C("rm", 8 + t))
+    dma("s", V("ce", S, HD), V("zb", 0, H), 2100)
     for t in range(2):
         iota(V("gx%d" % t, S, HD), [[0, H]], 16, 0)
         dma("s", V("ga%d" % t, S, HD), V("ac", 0, H), 2200)
@@ -335,21 +361,32 @@ def build(cfg):
             act(o, a, AF.Copy)
         else:
             cp(o, a)
-    cp(V("stu"), V("sti"))
-    cp(V("qg0", 10, 16), V("sti", 10, 16))
+    cp(V("qg0"), V("sti"))
     ts(V("stm"), V("sti"), -896.0, AL.add)
     cp(V("nn", HD, HD + 1024), V("nbi"))
     cp(V("ll", 0, 1024), V("dli"))
     dma("g", V("ac", HD, LO[0]), V("aa", 0, 3072), 5000, V("kk", 0, 1024))
     ops[-1]["x"]["load"] = True
-    if cfg["acm"] != "t":
+    if cfg["acm"] == "v":
         act(V("y4"), V("yb", 0, 480), AF.Copy, 0.0, 0.25)
     if any(cfg["scan"]):
         iota(V("smask"), [[0, 512]], 1, 0)
         asel(V("smask"), V("smask"), [[0, 32], [1, 16]], AL.not_equal, 0, 0)
-    for t in (1, 2, 3):
+    for k in range(16 if cfg["x23"] else 0):
+        gcp(V("xe", XO[3] - 2560 + k, XO[3] + 2560, 16), V("xb"))
+    for t in (1,) if cfg["x23"] else (1, 2, 3):
         for k in range(16 if xen[t] else 0):
-            gcp(V("xe", 2560 * t + k, 2560 * t + 16 * xen[t], 16), xl(t, 0, xen[t]))
+            gcp(V("xe", XO[t] + k, XO[t] + 16 * min(xen[t], S), 16), xl(t, 0, min(xen[t], S)))
+
+    def folds(t):
+        out = []
+        for a, b, mode in pcs[t][0]:
+            if mode in "fF":
+                if out and out[-1][1] == a and b - out[-1][0] <= cfg["fmax"]:
+                    out[-1][1] = b
+                else:
+                    out.append([a, b, len(out)])
+        return out
 
     def dist(t, st, pc, table, offs, ab, rl):
         a, b, mode = pc
@@ -371,14 +408,27 @@ def build(cfg):
                     mm(o, V("nib"), xl(t, a, b), False, True)
                 act(V(ab, 16 * a + k0 * m, 16 * a + (k0 + kb) * m), V(p, 0, kb * m), AF.Abs, 0.0, sc)
             return
-        d, xe = V(ab, 16 * a, 16 * b), V("xe", 2560 * t + 16 * a, 2560 * t + 16 * b)
-        if mode == "a":
+        d, xe = V(ab, 16 * a, 16 * b), V("xe", XO[t] + 16 * a, XO[t] + 16 * b)
+        if mode in "fF":
+            (act if mode == "f" else cp)(*((d, X(table, V(offs, a, b))) + ((AF.Copy,) if mode == "f" else ())))
+            run = [r for r in folds(t) if r[0] <= a < r[1]][0]
+            if b == run[1]:
+                lo, hi, j = 2560 * (t - 1) + 16 * run[0], 2560 * (t - 1) + 16 * run[1], "%d%d" % (t, run[2])
+                raw = V(ab, 16 * run[0], 16 * run[1])
+                more = cfg["flat"] * (run[1] - run[0])
+                send(V("bn", lo, hi), (raw, V("xe", 2560 + lo, 2560 + hi)), "fa" + j, "fb" + j, -1, more)
+                send(V("mx", lo, hi), V("bn", lo, hi), "fc" + j, "fd" + j, -1, more)
+        elif mode == "m":
+            act(d, X(table, V(offs, a, b)), AF.Copy, 0.0, -1.0)
+            dma("g", d, xe, 2100 + 14 * (b - a), None, True)
+            act(d, d, AF.Abs, 0.0, sc)
+        elif mode == "a":
             gr = V("graw", 16 * a, 16 * b)
             act(gr, X(table, V(offs, a, b)), AF.Copy)
             for a0 in range(a, b, 32):
                 p = bank()
                 mm(V(p), V("ib"), V("graw", 16 * a0, 16 * a0 + 512), True, False)
-                mm(V(p), V("nib"), V("xe", 2560 * t + 16 * a0, 2560 * t + 16 * a0 + 512), False, True)
+                mm(V(p), V("nib"), V("xe", XO[t] + 16 * a0, XO[t] + 16 * a0 + 512), False, True)
                 act(V(ab, 16 * a0, 16 * a0 + 512), V(p), AF.Abs, 0.0, sc)
         else:
             tt(d, X(table, V(offs, a, b)), xe, AL.subtract)
@@ -390,7 +440,7 @@ def build(cfg):
     def key(p, t, st, c0, c1, ab, rl, num, fix=-1, d0=0):
         runs = []
         for a, b, mode in pcs[t][st]:
-            mode = "e" if mode in "va" else mode
+            mode = "e" if mode in "vam" else mode.lower()
             lo, hi = max(a, c0), min(b, c1)
             if lo >= hi:
                 continue
@@ -401,10 +451,20 @@ def build(cfg):
         todo = []
         for lo, hi, mode, a, b in runs:
             o = V(p, lo - c0, hi - c0)
+            if mode == "f":
+                todo.append((o, "nb1", 15, xl(t, lo, hi)))
+                todo.append((o, "wp1", fix, xl(t, lo, hi)))
             for k in range(16):
                 if k == fix and lo < d0:
                     continue
-                if mode == "k":
+                if mode == "f":
+                    todo.append((o, "wn1", k, V(ab, 16 * lo + k, 16 * hi, 16)))
+            for k in range(16):
+                if k == fix and lo < d0:
+                    continue
+                if mode == "f":
+                    todo.append((o, "wp2", k, V("mx", 2560 * (t - 1) + 16 * lo + k, 2560 * (t - 1) + 16 * hi, 16)))
+                elif mode == "k":
                     e0 = 16 * a + k * (b - a) - a
                     todo.append((o, "w0", k, V(ab, e0 + lo, e0 + hi)))
                 elif mode == "r":
@@ -419,7 +479,7 @@ def build(cfg):
                 todo.append((V(p, 0, e1 - c0), "w0", fix, V("rfx", c0, e1)))
             else:
                 todo.append((V(p, 0, e1 - c0), "w0", fix, V("dfx", c0, e1)))
-        first = [x for x in todo if x[3][0] in ("ab1", "rl1") and fix >= 0 and x[0][2] + c0 <= d0]
+        first = [x for x in todo if x[3][0] in ("ab1", "rl1", "mx", "kk") and fix >= 0 and x[0][2] + c0 <= d0]
         if first and c1 <= d0 and (len(runs) == 1 or cfg["eg"]):
             rest = [x for x in todo if x not in first]
             if len(runs) > 1:
@@ -436,33 +496,62 @@ def build(cfg):
             o, wn, k, r = todo[j]
             mm(o, V(wn, 15 - k, 143 - k), r, False, j == len(todo) - 1)
 
-    def swap(out, o0, src, s0, n, step, sfx):
+    def swap(out, o0, src, s0, n, step, sfx, wide=1):
         for c1 in range(2):
             u = ("u0", "u1")[c1] + sfx
-            o = V(out, o0 + c1, o0 + n, 2)
+            o = V(out, o0 + c1 * wide, o0 + n * wide, 2 * wide)
             for s in range(2):
                 off = 16 + 16 * (c1 - s)
                 mm(o, V(u, off, off + 128), V(src, s0 + s * step, s0 + n * step, 2 * step), s == 0, s == 1)
+
+    def flags(o0, nb):
+        mm(V("p7", o0, o0 + 4 * nb, 2), V("ib"), V("zb", 0, 2 * nb))
+        swap("p7", o0 + 1, "nz", 0, nb, 1, "b", 2)
+        swap("p7", o0 + 1 + 2 * nb, "nz", 0, nb, 1, "b", 2)
 
     def pstage(t):
         tag[0] = "P%d" % t
         ab, rl = "ab2%d" % (t % 2), "rl2%d" % (t % 2)
         last = t == RO - 1
         acw = V("ac", HD, LO[t])
-        viat = cfg["acm"] == "t"
+        viat = cfg["acm"] in "th"
+        withy = cfg["acm"] == "y" and not last
+        if withy:
+            mm(V("p6", 0, S), V("iy"), V("yb", S * t, S * t + S), True, False)
         idm = i32 if viat else V("iq")
         po = V("pout", S * t, S * t + S)
         pe = S
-        if cfg["pm"][t] == "d":
+        mode = cfg["pm"][t]
+        if mode == "c":
+            todo = []
+            for j in range(16):
+                for a, b, md in pcs[t][1]:
+                    lo, hi = max(16 * a, S * j), min(16 * b, S * j + S)
+                    if lo < hi and md == "r":
+                        todo.append((j, lo, hi, "wn2", ab))
+                    if lo < hi:
+                        todo.append((j, lo, hi, "w0", rl if md == "r" else ab))
+            mm(V("p4", 0, S), V("ib"), V("zb", 0, S), True, False)
+            for x in todo:
+                j, lo, hi, w, src = x
+                mm(V("p4", lo - S * j, hi - S * j), V(w, 15 - j, 143 - j), V(src, lo, hi), False, x is todo[-1])
+            act(V("wc"), V("p4", 0, S), AF.Exp, 0.0, -2.0 ** -22)
+        if mode == "d":
             act(V("wc"), V("wq"), AF.Exp, MAGIC2 * 2.0 ** -22, -2.0 ** -22)
-            if cfg["wd"]:
+        if mode != "e":
+            for j in range(4):
+                dma("s", ("wd", j, j + 1, 1), V("wc"), 2200 + 100 * j, None, False, ("wa%d" % t, 64))
+            for h in range(2):
                 for j in range(4):
-                    dma("s", ("wd", j, j + 1, 1), V("wc"), 2200 + 100 * j, None, False, ("wa%d" % t, 64))
-                for j in range(4):
-                    dma("s", P(V("wt"), j, 4), ("wd", 0, 4, 1), 2400 + 550 * j, None, False, ("wb%d" % t, 64))
-            for j in range(0 if cfg["wd"] else 16):
-                f = 4 * (j % 4) + j // 4
-                dma("s", P(V("wt"), f), V("wc"), 2400 + 600 * j, None, False, ("wb%d" % t, 256))
+                    dma("s", P(V("wt", 1280 * h, 1280 * h + 1280), j, 4), ("wd", 0, 4, 1, h), 2200 + 1100 * h + 200 * j, None,
+                        False, ("w%s%d" % ("bc"[h], t), 64))
+        if mode == "c":
+            for a, b in ((0, 64), (64, 128), (128, S)) if cfg["bigp"] else [(a, a + 32) for a in range(0, S, 32)]:
+                tt(V("prod", 16 * a, 16 * b), X(acw, V("liu%d" % t, a, b)), V("wt", 16 * a, 16 * b), AL.mult)
+            for a, b in ((0, cfg["pgrp"]), (cfg["pgrp"], S)):
+                for k in range(16):
+                    mm(V("p6", a, b), idm, V("prod", 16 * a + k, 16 * b, 16), k == 0, k == 15)
+        elif mode == "d":
             tr(V("lz"), V("lih", 0, S))
             for bb in range(5):
                 for c1 in range(2):
@@ -473,24 +562,26 @@ def build(cfg):
             ts(V("lk"), V("p4", 0, S), 2048.0 - HD, AL.add)
             ch = cfg["ch"][t]
             seg = 16 // ch
-            pp = min(cfg["pp"], seg)
-            for k in range(0, 16, pp):
+            k = 0
+            for pp in cfg["pk"] if ch == 1 else [min(cfg["pp"], seg)] * (16 // min(cfg["pp"], seg)):
                 tt(V("prod", S * k, S * (k + pp)), X(acw, V("lk", 10 * k, 10 * (k + pp))), V("wt", S * k, S * (k + pp)), AL.mult)
-                if (k + pp) % seg == 0 and k + pp > seg:
-                    dma("g", V("prod", 0, S * seg), V("prod", S * (k + pp - seg), S * (k + pp)), 2200 + 250 * seg, None, True)
+                k += pp
+                if k % seg == 0 and k > seg:
+                    dma("g", V("prod", 0, S * seg), V("prod", S * (k - seg), S * k), 2200 + 250 * seg, None, True)
             for _ in range(cfg["lev"][t]):
                 seg //= 2
                 dma("g", V("prod", 0, S * seg), V("prod", S * seg, 2 * S * seg), 2200 + 250 * seg, None, True)
             for k in range(seg):
-                mm(V("p6", 0, S), idm, V("prod", S * k, S * k + S), k == 0, k == seg - 1)
+                mm(V("p6", 0, S), idm, V("prod", S * k, S * k + S), k == 0 and not withy, k == seg - 1)
         else:
             for a in range(0, S, 32):
+                pb = V("p" + cfg["bke"][a // 32 % len(cfg["bke"])]) if last else V("p4")
                 if [p for p in pcs[t][1] if p[0] <= a < p[1]][0][2] == "r":
-                    mm(V("p4"), V("nbo"), V(ab, 16 * a, 16 * a + 512), True, False)
-                    mm(V("p4"), V("bo"), V(rl, 16 * a, 16 * a + 512), False, True)
+                    mm(pb, V("nbo"), V(ab, 16 * a, 16 * a + 512), True, False)
+                    mm(pb, V("bo"), V(rl, 16 * a, 16 * a + 512), False, True)
                 else:
-                    mm(V("p4"), V("bo"), V(ab, 16 * a, 16 * a + 512))
-                act(V("wt", 16 * a, 16 * a + 512), V("p4"), AF.Exp, 0.0, -2.0 ** -22)
+                    mm(pb, V("bo"), V(ab, 16 * a, 16 * a + 512))
+                act(V("wt", 16 * a, 16 * a + 512), pb, AF.Exp, 0.0, -2.0 ** -22)
                 if cfg["bigp"] and a in (0, 64):
                     continue
                 a0 = a - 32 if cfg["bigp"] and a in (32, 96) else a
@@ -502,28 +593,41 @@ def build(cfg):
                 if b > a:
                     for k in range(16):
                         mm(V("p6", a, b), idm, V("prod", 16 * a + k, 16 * b, 16), k == 0, k == 15)
+        old = X(V("ac", 0, LO[t]), V("tu%d" % t, 2 * (NL[t] // 16), 2 * (NL[t] // 16) + 10))
+        new = V("ac", LO[t], LO[t] + S)
+        if not viat and not last:
+            if withy:
+                act(V("uu"), old, AF.Copy)
+            else:
+                tt(V("uu"), old, V("y4", S * t, S * t + S), AL.add)
+            tt(new, V("uu"), V("p6", 0, S), AL.add)
         if pe > 0:
             act(V("pout", S * t, S * t + pe), V("p6", 0, pe), AF.Copy, 0.0, 1.0 if viat else -4.0)
         if last and 0 < pe < S:
             dma("s", V("yp", S * t, S * t + pe), V("pout", S * t, S * t + pe), 2000)
         for a in range(pe, S, 32):
             scan(V("wt", 16 * a, 16 * a + 512), V("smask"), V("prod", 16 * a, 16 * a + 512), AL.mult, AL.add)
-            cp(V("pout", S * t + a, S * t + a + 32), V("wt", 16 * a + 15, 16 * a + 512, 16))
+            if cfg["pouta"]:
+                act(V("pout", S * t + a, S * t + a + 32), V("wt", 16 * a + 15, 16 * a + 512, 16), AF.Copy)
+            else:
+                cp(V("pout", S * t + a, S * t + a + 32), V("wt", 16 * a + 15, 16 * a + 512, 16))
         o0 = pe if last and pe < S else 0
         dma("s", V("yp", S * t + o0, S * t + S), V("pout", S * t + o0, S * t + S), 2000)
+        if withy:
+            ops[-1]["w"].append(("out%d" % t, 0, 1, 1))
+            dma("g", V("yp", S * t, S * t + S), V("yb", S * t, S * t + S), 2200, ("out%d" % t, 0, 1, 1), True)
         if last:
             return
-        old = X(V("ac", 0, LO[t]), V("tu%d" % t, 2 * (NL[t] // 16), 2 * (NL[t] // 16) + 10))
-        new = V("ac", LO[t], LO[t] + S)
         if viat:
             act(V("uu"), old, AF.Copy)
             mm(V("p6", 256, 256 + S), V("iy"), V("yb", S * t, S * t + S), True, False)
-            mm(V("p6", 256, 256 + S), i32, V("uu"), False, False)
+            if cfg["acm"] == "t":
+                mm(V("p6", 256, 256 + S), i32, V("uu"), False, False)
             mm(V("p6", 256, 256 + S), V("iq"), po, False, True)
-            act(new, V("p6", 256, 256 + S), AF.Copy)
-        else:
-            tt(V("uu"), old, V("y4", S * t, S * t + S), AL.add)
-            tt(new, V("uu"), V("p6", 0, S), AL.add)
+            if cfg["acm"] == "t":
+                act(new, V("p6", 256, 256 + S), AF.Copy)
+            else:
+                tt(new, V("uu"), V("p6", 256, 256 + S), AL.add)
         if t < 2:
             cp(X(V("ga%d" % t), V("pos%d" % t, 0, 10)), new)
             a0 = LO[t + 1] + S
@@ -557,6 +661,13 @@ def build(cfg):
                 b = min(b, d0)
                 if a >= b:
                     continue
+                if cfg["fixa"][t]:
+                    act(V("rfx", a, b), X(kkw, V("fx", a // 16, b // 16)), AF.Copy)
+                    p = V(bank(), 0, b - a)
+                    mm(p, V("nib"), xl(t, a, b), True, False)
+                    mm(p, V("ib"), V("rfx", a, b), False, True)
+                    act(V("dfx", a, b), p, AF.Abs, 0.0, 32768.0)
+                    continue
                 tt(V("dfx", a, b), X(kkw, V("fx", a // 16, b // 16)), xl(t, a, b), AL.subtract)
                 if cfg["fixr"]:
                     ts(V("rfx", a, b), V("dfx", a, b), 0.0, AL.max, 65536.0, AL.mult)
@@ -567,7 +678,7 @@ def build(cfg):
             e0 = max(c0, d0)
             tag[0] = "Q%d%d" % (t, c)
             if c1 > e0:
-                cl = ("stu", "qg0", "qg1")[t]
+                cl = ("qg0", "qg0", "qg1")[t]
                 cp(V("candu", e0, c1), X(V("nbi") if t == 0 else V("nn", HD, HD + QL[t - 1]), V(cl, e0 // 16, c1 // 16)))
                 for pc in pcs[t][0]:
                     if e0 <= pc[0] < c1:
@@ -610,7 +721,9 @@ def build(cfg):
             continue
         nnq = V("nn", HD + QL[t], HD + QL[t] + n)
         act(V("lik", 0, n), X(llw, V(qg, 0, nb)), AF.Copy)
-        act(nnq, X(nnw, V(qg, 0, nb)), AF.Copy)
+        if t == 2:
+            nnq = V("nn", HD + QL[t], HD + QL[t] + S)
+        act(nnq, X(nnw, V(qg, 0, cnt(nnq) // 16)), AF.Copy)
         d1 = ahead(t + 1)
         tag[0] = "E%d" % t
         if cfg["cfrom"]:
@@ -640,7 +753,7 @@ def build(cfg):
         act(V("winr", 0, n), V("p5", 256, 256 + n), AF.Sign, 0.0, -1.0)
         for r in range(16):
             mm(V("p5", 0, nb), V("w0", 15 - r, 143 - r), V("winr", r, n, 16), r == 0, r == 15)
-        et, et0 = V("lc", ET[t], ET[t] + 2 * nb), V("lc", ET[t], ET[t] + nb)
+        et0 = V("lc", ET[t] + 1, ET[t] + 2 * nb, 2)
         qf = V("qf", 0, nb)
         if t == 1:
             for r in range(16):
@@ -661,14 +774,13 @@ def build(cfg):
         act(V("sm", 64 + nb, 64 + 2 * nb), sm(1), AF.Identity, float(QL[t] + HD), -1.0)
         tt(sm(2, 2), sm(1, 2), sm(0, 2), AL.mult)
         tt(et0, et0, sm(2), AL.subtract)
-        tt(sm(3, 2), sm(2, 2), V("qf", nb, 3 * nb), AL.mult)
+        tt(V("lc", ET[t], ET[t] + 4 * nb, 2), sm(2, 2), V("qf", nb, 3 * nb), AL.mult)
         th = 37 * 65536.0 - 63488.0
         if t < 2:
             tag[0] = "G%d" % t
             ts(V("nz", 0, 10), V("sc2", 15, S, 16), th, AL.is_ge)
-            swap("p7", 96, "nz", 0, 10, 1, "b")
-            swap("p7", 106, "nz", 0, 10, 1, "b")
-            tt(V("nw", 0, 20), V("sm", 22, 42), V("p7", 96, 116), AL.mult)
+            flags(320, 10)
+            tt(V("nw", 0, 20), V("sm", 22, 42), V("p7", 321, 360, 2), AL.mult)
             mm(V("p7", 176, 186), V("ib"), V("cst", 0, 10), True, False)
             mm(V("p7", 176, 186), V("ib"), V("nw", 0, 10), False, False)
             mm(V("p7", 176, 186), V("lt"), V("nw", 10, 20), False, False)
@@ -678,6 +790,10 @@ def build(cfg):
             gx = "gx%d" % t
             cp(X(V(gx), V("pos%d" % t, 0, 10)), xt)
             send(xl(t + 1, S, HD), V(gx, S, HD), "rx%d" % t, "tx%d" % t, t)
+            tag[0] = "X%d" % t
+            g0 = min([p[0] for st in range(2) for p in pcs[t + 1][st] if p[2] != "k" and p[0] >= S] + [HD])
+            for k in range(16 if g0 < HD else 0):
+                gcp(V("xe", XO[t + 1] + 16 * g0 + k, XO[t + 1] + 16 * xen[t + 1], 16), xl(t + 1, g0, xen[t + 1]))
             tag[0] = "H%d" % t
             for pc in pcs[t + 1][0]:
                 if S < pc[1] <= d1:
@@ -687,13 +803,14 @@ def build(cfg):
         z0 = 10 if t < 2 else 0
         if nb > z0:
             ts(V("nz", z0, nb), V("sc2", 16 * z0 + 15, n, 16), th, AL.is_ge)
-            swap("p7", 128, "nz", 0, nb, 1, "b")
-            swap("p7", 128 + nb, "nz", 0, nb, 1, "b")
-        nu = V("p7", 128, 128 + 2 * nb) if nb > z0 else V("p7", 96, 116)
-        tt(sm(4, 2), sm(3, 2), nu, AL.mult)
-        tt(sm(4, 2), sm(4, 2), et, AL.add)
-        ts(V(tu, 0, 2 * nb), sm(4, 2), 896.0, AL.add)
-        tt(X(V("nn", 0, HD + QL[t]), V(tu, nb, 2 * nb)), nnq, V("ct", 256 * t, 256 * t + n), AL.max)
+            flags(256, nb)
+        n0 = 256 if nb > z0 else 320
+        nu = V("p7", n0 + 1, n0 + 4 * nb, 2)
+        scan(V("sm", 160, 160 + 4 * nb), V("p7", n0, n0 + 4 * nb), V("lc", ET[t], ET[t] + 4 * nb), AL.mult, AL.add)
+        ts(V(tu, 0, 2 * nb), V("sm", 161, 160 + 4 * nb, 2), 896.0, AL.add)
+        m = n if t < 2 else S
+        tt(X(V("nn", 0, HD + QL[t]), V(tu, nb, nb + m // 16)), V("nn", HD + QL[t], HD + QL[t] + m),
+           V("ct", 256 * t, 256 * t + m), AL.max)
         if t < 2:
             dma("s", P(nnq, t), P(V("qrf", 0, n), t), 2200)
         swap("p5", 0, "sc2", 15, 2 * nb, 16, "")
@@ -762,6 +879,10 @@ def cost(o, m):
     return o["m"][0] + o["m"][1] * m[o["m"][2]]
 
 
+def late(o, m):
+    return 1900.0 * m["d"] + o["x"]["lat"] if "lat" in o["x"] else 0.0
+
+
 def gap(o, q, i, m):
     if q["e"] == o["e"]:
         return 0.0 if o["e"] == "t" or i not in q["h"] else m["y"]
@@ -803,14 +924,14 @@ def schedule(full, cfg, m):
         for j in ops[i]["s"]:
             succ[j].append(i)
     cs = [cost(o, m) for o in ops]
-    tl = [o["x"].get("lat", 0.0) * m["d"] for o in ops]
+    tl = [late(o, m) for o in ops]
     pr = [0.0] * n
     for i in range(n - 1, -1, -1):
         pr[i] = cs[i] + tl[i] + max([m["x"] + pr[j] for j in succ[i]] + [0.0])
     fw = [[(j, tl[i] + gap(ops[i], ops[j], i, m)) for j in succ[i]] for i in range(n)]
     bw = [[(j, tl[j] + gap(ops[j], ops[i], j, m)) for j in ops[i]["s"]] for i in range(n)]
     eng = [o["e"] for o in ops]
-    tabs = [([cost(o, q) for o in ops], [o["x"].get("lat", 0.0) * q["d"] for o in ops],
+    tabs = [([cost(o, q) for o in ops], [late(o, q) for o in ops],
              [[(j, gap(ops[j], ops[i], j, q)) for j in ops[i]["s"]] for i in range(n)]) for q in SETS]
 
     def value(seq):
@@ -866,29 +987,46 @@ def schedule(full, cfg, m):
                     pool.setdefault(eng[j], []).append(j)
         return seq, st
 
-    def timing(seq, tab):
+    names = sorted(set(eng))
+    en = [names.index(e) for e in eng]
+    sinks = [i for i in range(n) if not succ[i]]
+
+    def timing(seq, tab, a=0, old=None):
         c, lat, pre = tab
-        free, last, fin, par, end, top = {}, {}, [0.0] * n, [-1] * n, 0.0, -1
-        for i in seq:
-            e = eng[i]
-            s, p = free.get(e, 0.0), last.get(e, -1)
+        free, last = [0.0] * len(names), [-1] * len(names)
+        if old is None:
+            fin, par = [0.0] * n, [-1] * n
+        else:
+            fin, par = old[3][:], old[1][:]
+            k, miss = a - 1, len(names)
+            while k >= 0 and miss:
+                i = seq[k]
+                if last[en[i]] < 0:
+                    last[en[i]], free[en[i]] = i, fin[i] - lat[i]
+                    miss -= 1
+                k -= 1
+        for i in seq[a:]:
+            e = en[i]
+            s, p = free[e], last[e]
             for j, w in pre[i]:
                 if fin[j] + w > s:
                     s, p = fin[j] + w, j
-            free[e], last[e], par[i] = s + c[i], i, p
-            fin[i] = s + c[i] + lat[i]
-            if fin[i] > end:
-                end, top = fin[i], i
-        return end, par, top
+            s += c[i]
+            free[e], last[e], par[i] = s, i, p
+            fin[i] = s + lat[i]
+        top = max(sinks, key=lambda i: fin[i])
+        return fin[top] + cfg["wmean"] * sum(fin) / n, par, top, fin
 
-    def polish(seq):
+    def polish(seq, steps, heat):
         prs = [set(o["s"]) for o in ops]
         res = [timing(seq, tab) for tab in tabs]
         val = sum(r[0] for r in res)
         keep = (val, seq)
-        for it in range(cfg["sa"]):
-            temp = cfg["temp"] * (1.0 - it / cfg["sa"])
-            _, par, i = res[rs.randint(len(res))]
+        for it in range(steps):
+            temp = heat * (1.0 - it / steps)
+            _, par, i, _ = res[rs.randint(len(res))]
+            if rs.uniform() < cfg["pany"]:
+                i = rs.randint(n)
             cand = []
             while i >= 0:
                 p = par[i]
@@ -896,7 +1034,7 @@ def schedule(full, cfg, m):
                     cand.append((p, i))
                 i = p
             if not cand:
-                break
+                continue
             p, i = cand[rs.randint(len(cand))]
             a, b = seq.index(p), seq.index(i)
             e = eng[i]
@@ -928,15 +1066,20 @@ def schedule(full, cfg, m):
                 new = seq[:a] + [j for j in seq[a:b + 1] if j not in ms] + move + seq[b + 1:]
             if new == seq:
                 continue
-            r2 = [timing(new, tab) for tab in tabs]
+            lim = -temp * math.log(1.0 - rs.uniform())
+            r2 = [timing(new, tabs[0], a, res[0])]
+            if r2[0][0] - res[0][0] > lim + cfg["slack"]:
+                continue
+            r2 += [timing(new, tabs[k], a, res[k]) for k in range(1, len(tabs))]
             v2 = sum(r[0] for r in r2)
-            if v2 <= val - temp * math.log(1.0 - rs.uniform()):
+            if v2 <= val + lim:
                 seq, res, val = new, r2, v2
                 if val < keep[0]:
                     keep = (val, seq)
         return keep[1]
 
     tags = sorted(set(o["g"] for o in ops))
+    pr0 = list(pr)
     rs = np.random.RandomState(cfg["seed"])
     best = None
     for _ in range(cfg["iters"] + 1):
@@ -947,9 +1090,37 @@ def schedule(full, cfg, m):
         z = rs.standard_normal(n) * cfg["noise"]
         back = sweep([st[i] + cs[i] + float(z[i]) for i in range(n)], bw, fw, tl)[1]
         pr = [back[i] + cs[i] for i in range(n)]
-    if cfg["boost"]:
-        seq, st = sweep([-best[2][i] + cfg["boost"].get(ops[i]["g"], 0.0) for i in range(n)], fw, bw, [0.0] * n)
-        best = (value(seq), seq, st)
+    if cfg.get("warm"):
+        pw = []
+        for i in range(n):
+            z = cfg["warm"].get(full[ops[i]["sub"][0]]["sig"])
+            pw.append(z if z is not None else max([pw[j] + cs[j] for j in ops[i]["s"]] + [0.0]))
+        for i in range(n):
+            pw[i] = max([pw[i]] + [pw[j] + 1e-3 for j in ops[i]["s"]])
+        seq = sorted(range(n), key=lambda i: pw[i])
+        fin = timing(seq, tabs[0])[3]
+        st = [fin[i] - cs[i] - tl[i] for i in range(n)]
+        val = value(seq)
+        if val < best[0]:
+            best = (val, seq, st)
+    if cfg["phs"]:
+        shift = {z: cfg["boost"].get(z, 0.0) for z in tags}
+        now = None
+        main = [z for z in tags if z[0] in "FQDEWGHLP" and z[1:].isdigit()]
+        for it in range(cfg["phs"]):
+            new = dict(shift)
+            for _ in range(1 + rs.randint(2) if it else 0):
+                some = main if rs.uniform() < 0.8 else tags
+                new[some[rs.randint(len(some))]] += float(rs.standard_normal()) * (500.0, 2000.0, 5000.0)[rs.randint(3)]
+            seq, st = sweep([pr0[i] + new[ops[i]["g"]] for i in range(n)], fw, bw, [0.0] * n)
+            val = value(seq)
+            if now is None or val <= now - cfg["ptemp"] * (1.0 - it / cfg["phs"]) * math.log(1.0 - rs.uniform()):
+                now, shift = val, new
+            if val < best[0]:
+                best = (val, seq, st)
+        if "out" in cfg:
+            cfg["out"].update(shift)
+            cfg["out"]["_v"] = now
     for _ in range(cfg["ils"]):
         t0, wd, sg = rs.uniform(0, 85000), rs.uniform(3000, 15000), (200.0, 600.0, 1500.0)[rs.randint(3)]
         z = rs.standard_normal(n) * sg
@@ -965,7 +1136,8 @@ def schedule(full, cfg, m):
         val = value(seq)
         if val <= best[0]:
             best = (val, seq, st)
-    seq = polish(best[1]) if cfg["sa"] else best[1]
+    seq = polish(best[1], cfg["sa"], cfg["temp"])
+    seq = polish(seq, cfg["sa2"], cfg["temp2"])
     return [j for i in seq for j in ops[i]["sub"]]
 
 
@@ -977,7 +1149,7 @@ def replay(ops, seq, m):
         for j in o["s"]:
             s = max(s, fin[j] + gap(ops[j], o, j, m))
         free[o["e"]] = s + cost(o, m)
-        fin[i] = free[o["e"]] + o["x"].get("lat", 0.0) * m["d"]
+        fin[i] = free[o["e"]] + late(o, m)
         end = max(end, fin[i])
     return end
 
@@ -985,35 +1157,49 @@ def replay(ops, seq, m):
 def plan(cfg):
     ops = graph(cfg)
     order = {}
-    for i in schedule(ops, cfg, NOM):
+    seq = schedule(ops, cfg, NOM)
+    for i in seq:
         order.setdefault(ops[i]["e"], []).append(i)
     place = {}
     for e in order:
         for k in range(len(order[e])):
             place[order[e][k]] = k
     marked = {}
-    for e in order:
-        got = {}
-        for i in order[e]:
-            o = ops[i]
-            need = {}
-            own = []
-            for j in o["d"]:
-                q = ops[j]
-                if "sem" in q["x"]:
-                    if ("x", q["x"]["sem"]) not in got:
-                        got[("x", q["x"]["sem"])] = True
-                        own.append(j)
-                elif not (e == "t" and q["e"] == "t"):
-                    need[q["e"]] = max(need.get(q["e"], -1), place[j])
-            o["wo"] = own
-            o["wq"] = []
-            for f in need:
-                if need[f] > got.get(f, -1):
-                    got[f] = need[f]
-                    j = order[f][need[f]]
-                    marked[j] = True
-                    o["wq"].append(j)
+    gots = {e: {} for e in order}
+    knew = {}
+
+    def learn(got, j):
+        if cfg["prune"]:
+            for f, z in knew[j].items():
+                got[f] = max(got.get(f, -1), z)
+
+    for i in seq:
+        o = ops[i]
+        e = o["e"]
+        got = gots[e]
+        need = {}
+        o["wo"], o["wq"] = [], []
+        for j in o["d"]:
+            q = ops[j]
+            if "sem" not in q["x"] and not (e == "t" and q["e"] == "t"):
+                need[q["e"]] = max(need.get(q["e"], -1), place[j])
+        last = [order[f][need[f]] for f in need if need[f] > got.get(f, -1)]
+        for j in sorted(last, key=lambda j: -knew[j].get("n", 0)):
+            f = ops[j]["e"]
+            if place[j] > got.get(f, -1):
+                got[f] = place[j]
+                marked[j] = True
+                o["wq"].append(j)
+                learn(got, j)
+        for j in o["d"]:
+            q = ops[j]
+            if "sem" in q["x"] and q["x"]["sem"] not in got:
+                got[q["x"]["sem"]] = 0
+                o["wo"].append(j)
+                if q["k"] == "dma":
+                    learn(got, j)
+        got["n"] = max(got.get("n", 0), len(knew))
+        knew[i] = dict(got)
     for e in order:
         c = 0
         for i in order[e]:
@@ -1043,7 +1229,7 @@ def rank_program(g, core, T, topo):
         if v[0] == "ind":
             return ap(v[1]).indirect(ap(v[2]))
         if v[0] == "wd":
-            return T.wd[:, v[1], :] if v[2] - v[1] == 1 else T.wd[:]
+            return T.wd[:, v[1], :] if len(v) == 4 else T.wd[:, :, 1280 * v[4]:1280 * v[4] + 1280]
         if len(v) > 4:
             return T[v[0]][v[4][0]:v[4][1]:v[4][2], v[1]:v[2]]
         if v[3] == 1:
@@ -1059,6 +1245,18 @@ def rank_program(g, core, T, topo):
             for j in o["wq"]:
                 q.wait_ge(T.sem[QSEM[ops[j]["e"]]], ops[j]["n"])
             k = o["k"]
+            if k == "send" and o["a"][3] < 0:
+                near = [c for c in topo.cores_of(core) if topo.die(c) == topo.die(core)]
+                dst = near[near.index(core) ^ 1]
+                rid, pid, _ = topo.addr(dst)
+                mask = sum(1 << x for x in topo.engines(core, dst)[slice(*CFG["feng"])])
+                if isview(o["a"][1][0]):
+                    g.remote_dma_fused([RemoteDMATransfer(dst_ids=[DstId(rid=rid, pnc=pid)], dma_engine_mask=mask,
+                                                          remote_sem=T.sem[o["a"][2]], srcs=[ap(v) for v in o["a"][1]],
+                                                          dsts=[ap(o["a"][0])], alu_op=2)], local_sem=T.sem[o["a"][4]])
+                else:
+                    g.remote_dma(ap(o["a"][0]), ap(o["a"][1]), T.sem[o["a"][2]], T.sem[o["a"][4]], pid, rid, mask)
+                continue
             if k == "send":
                 dst = T.cores[(rank + 1 + o["a"][3] % (nr - 1)) % nr]
                 rid, pid, _ = topo.addr(dst)
@@ -1097,6 +1295,6 @@ def rank_program(g, core, T, topo):
                 ins.then_inc(T.sem[QSEM[e]], 1)
     for o in ops:
         if o["k"] == "send":
-            g.wait_ge(T.sem[o["a"][4]], ENG)
+            g.wait_ge(T.sem[o["a"][4]], ENG if o["a"][3] >= 0 else FENG)
         if o["k"] == "dma" and o["a"][0][0] == "yp":
             g.sync.wait_ge(T.sem[o["x"]["sem"]], 16)

import math
import numpy as np
from concourse.bass import DstId, RemoteDMATransfer
from concourse.mybir import AluOpType, ActivationFunctionType

AL = AluOpType
AF = ActivationFunctionType
S, H, RO = 160, 96, 4
HD = 256
QL = (1024, 1184, 1440, 1696)
LO = (3328, 3488, 3744, 4000)
NL = (160, 256, 256, 160)
XO = (0, 2560, 6656, 10752)
MAGIC = 1.5 * 2.0 ** 34
MAGIC2 = 1.5 * 2.0 ** 39
F, B, I, U, HF = "float32", "bfloat16", "int32", "uint16", "float16"
CFG = {
    "cut": ((96,), (128,), (128,), (128,)),
    "pc": (("a32 v64 v64", "v64 v32 v32 a32"), ("v64 v64 a32 k96", "v64 v32 a32 v32 k96"),
           ("v64 a32 v64 k96", "v64 v64 a32 k96"), ("a32 v64 v32 a32", "v64 a32 a32 a32")),
    "pm": "ddee", "ch": (4, 4, 1, 1), "lev": (0, 0, 0, 0), "pp": 4, "wdep": 1, "acm": "t", "ctm": "d", "cfrom": 1,
    "scan": (0, 0, 0, 3),
    "pgrp": 160, "seed": 768, "noise": 200.0, "xe0": 6, "look": 0.3, "iters": 6, "selv": 8, "sela": 0,
    "bigp": 0, "gp": 48, "ils": 1000, "ug": 4, "ig": 0, "xeg": 0, "fixr": 0, "zv": 0, "seld": 0, "tmax": 1200,
    "sa2": 0, "temp2": 50.0, "phs": 0, "ptemp": 500.0, "wmean": 0.0, "pany": 0.0, "slack": 150.0, "boost": {}, "ptag": 0.3, "sa": 0, "temp": 300.0,
}

CFG.update({
    "cut": (((96,), (96,)), ((160,), (160,)), ((160,), (160,)), ((128,), (128,))), "eg": 1, "fixt": 1, "wd": 1,
    "kv": ((0, 0), (0, 0), (0, 0), (0, 0)), "eng": (0, 16, 2), "bk": "23", "bk3": "23", "bke": "45", "prune": 1, "x23": 0, "fixa": (0, 0, 0, 0), "pouta": 1, "pk": (5, 5, 4, 2),
    "feng": (0, 16, 1), "fmax": 96, "flat": 14.0, "fsplit": (0, 1, 1, 0), "pm": "ddde", "ch": (2, 2, 1, 1), "wdep": 0, "xe0": 11, "acm": "v", "seld": 1,
    "zv": 1, "pgrp": 96, "ils": 600, "ptag": 0.5, "sa": 8000, "temp": 200.0, "seed": 2,
    "pc": (("a32 v64 v32 a32", "v64 a32 v32 a32"), ("v64 v32 a32 a32 k96", "v64 a32 a32 v32 k96"),
           ("v64 a32 v64 k96", "v64 a32 a32 a32 k96"), ("a32 v64 a32 a32", "v32 a32 a32 a32 a32")),
})

CFG.update({
    "zv": 0, "fsplit": (0, 1, 0, 1), "ils": 60, "sa": 1500, "temp": 60.0, "seed": 127, "noise": 600.0, "iters": 12,
    "sa2": 30000, "temp2": 60.0,
    "ug": 2, "fixa": (0, 0, 0, 1), "gp": 32, "fsplit": (0, 1, 1, 0), "seed": 214, "sa2": 25000,
    "pc": (("a32 v64 v32 a32", "v32 v32 a32 v32 a32"), ("v64 v32 a32 v32 k96", "v64 a32 a32 v32 k96"),
           ("v64 m64 v32 k96", "v64 m64 a32 k96"), ("v64 m96", "v32 a32 a32 a32 a32")),
})

SB = {
    "sti": (16, I), "nbi": (1024, I), "dli": (1024, I), "nn": (HD + 1696, F), "ll": (1696, F), "kk": (1856, B),
    "ce": (4000, B), "ac": (4000, F), "yb": (640, B), "y4": (480, B), "pout": (640, F),
    "ones": (160, F), "iw": (160, F), "u0": (160, F), "u1": (160, F), "u0b": (160, B), "u1b": (160, B),
    "ib": (128, B), "nib": (128, B), "iq": (128, F), "iy": (128, B), "bo": (128, B), "bt": (128, B), "w0": (144, B),
    "wn1": (144, B), "wn2": (144, B), "nbo": (128, B),
    "sel": (2048, B), "lt": (128, B), "ewd": (128, B), "smask": (512, F),
    "pi": (8, I), "col": (32, F), "pw": (8, B), "rm": (16, F), "i16": (16, F),
    "iob": (256, B), "iof": (768, F), "cix": (256, B), "thr": (256, B), "rm1": (256, F), "rm2": (256, F), "rmx": (256, F),
    "lc": (184, F), "lx": (32, F), "stm": (16, F), "stu": (16, U), "cst": (16, B), "zb": (512, B), "xb": (320, B), "cz": (256, HF),
    "candu": (256, U), "c16": (256, HF), "lih": (256, HF), "qrf": (256, F), "ct": (768, F),
    "ab1": (4096, B), "ab20": (4096, B), "ab21": (4096, B), "graw": (4096, B), "wt": (2560, F), "prod": (2560, F),
    "rl1": (4096, B), "rl20": (4096, B), "rl21": (4096, B), "lik": (256, F), "sq": (256, B),
    "tk": (256, F), "tk2": (256, F), "sc": (256, F), "sc2": (512, F), "hz": (16, F), "qz": (32, HF), "qf": (48, F),
    "qh": (16, HF), "qr": (256, HF), "vd": (96, B), "wq": (160, F), "wc": (160, F), "lz": (160, HF), "lk": (160, U),
    "eq": (4096, B), "winr": (256, B), "sm": (256, F), "mi": (32, I), "kab": (32, I), "ti": (16, I), "rr": (16, F),
    "ks": (16, B), "nw": (32, B), "zz": (256, F), "uu": (160, F), "xe": (13312, B), "nz": (16, B),
    "wr": (432, B), "fx": (16, U), "dfx": (256, B), "rfx": (256, B),
}
for _t in range(4):
    SB["qg%d" % _t] = (16, U)
    SB["liu%d" % _t] = (256, U)
for _t in range(3):
    SB["tu%d" % _t] = (48, U)
for _t in range(2):
    SB["gx%d" % _t] = (320, B)
    SB["ga%d" % _t] = (320, F)
    SB["pos%d" % _t] = (16, U)
SCRATCH = {}
for _n in SB:
    SCRATCH[_n] = ("sbuf", [128, SB[_n][0]], SB[_n][1])
for _t in range(8):
    SCRATCH["p%d" % _t] = ("psum", [128, 512], F)
SCRATCH["wd"] = ("dram", [8, 4, 2560], F)
NDMA = 48
SEMAPHORES = (["sv", "sa", "sp", "sg", "rx0", "rx1", "ra0", "ra1", "tx0", "tx1", "ta0", "ta1", "wz", "ws"]
              + ["w%s%d" % (_a, _t) for _a in "abc" for _t in range(3)] + ["d%d" % _t for _t in range(NDMA)])
DRAM = ("kq", "cc", "aa", "xs", "ys", "nb", "dl", "st", "yp")
SEMAPHORES += ["f%s%d%d" % (_a, _t, _j) for _a in "abcd" for _t in (1, 2, 3) for _j in range(3)]
ENG = len(range(*CFG["eng"]))
FENG = len(range(*CFG["feng"]))

NOM = {"c": 0.86, "g": 1.34, "s": 3.2, "p": 0.43, "x": 165.0, "y": 140.0, "d": 0.85, "i": 120.0}
SETS = [NOM, {"c": 1.08, "g": 1.25, "s": 2.5, "p": 0.54, "x": 140.0, "y": 120.0, "d": 1.1, "i": 180.0},
        {"c": 1.1, "g": 2.1, "s": 5.2, "p": 0.55, "x": 165.0, "y": 140.0, "d": 0.7, "i": 80.0}]


def V(n, a=0, b=None, s=1):
    if b is None:
        b = SB[n][0] if n in SB else 512
    return (n, a, b, s)


def C(n, a):
    return (n, a, a + 1, 1)


def P(v, r, step=16):
    return v + ((r, 128, step),)


def X(w, o):
    return ("ind", w, o)


def cnt(v):
    if v[0] == "ind":
        return 16 * cnt(v[2])
    return len(range(v[1], v[2], v[3]))


def isview(v):
    return isinstance(v, tuple)


def psum(v):
    return v[0][0] == "p" and v[0][1:].isdigit()


def two(v):
    return v[0] in SB and SB[v[0]][1] in (B, U, HF)


def meet(a, b):
    if a[0] != b[0] or a[1] >= b[2] or b[1] >= a[2]:
        return False
    if a[3] == b[3] and a[3] > 1 and (a[1] - b[1]) % a[3] != 0:
        return False
    if len(a) > 4 and len(b) > 4 and a[4] != b[4]:
        return False
    return True


def pieces(text):
    out, a = [], 0
    for w in text.split():
        out.append((a, a + int(w[1:]), w[0]))
        a += int(w[1:])
    return out


def build(cfg):
    ops = []
    tag = [""]

    def add(eng, kind, args, outs, ins, cost, extra=None):
        rd, wr = [], []
        for v in ins:
            if isview(v):
                rd.extend([v[1], v[2]] if v[0] == "ind" else [v])
        for v in outs:
            if v[0] == "ind":
                wr.append(v[1])
                rd.append(v[2])
            else:
                wr.append(v)
        ops.append({"e": eng, "k": kind, "a": args, "r": rd, "w": wr, "m": cost, "x": extra or {},
                    "g": tag[0] or (wr[0][0] + str(wr[0][1] // 2560) if wr else "")})
        return len(ops) - 1

    def vcost(out, a, f):
        n = cnt(out)
        if out[0] == "ind":
            return (50, n, "s")
        if a[0] == "ind":
            return (50, n, "g")
        return (30, max(64, n * f), "c")

    def cp(out, a):
        add("v", "cp", (out, a), [out], [a], vcost(out, a, 0.5 if two(out) and two(a) else 1))

    def tt(out, a, b, op):
        add("v", "tt", (out, a, b, op), [out], [a, b], vcost(out, a, 1 if psum(a) or psum(b) else 2))

    def ts(out, a, s1, o1, s2=None, o2=None):
        add("v", "ts", (out, a, s1, s2, o1, o2), [out], [a, s1, s2], vcost(out, a, 0.5 if two(out) and two(a) else 1))

    def ms(out, c):
        add("v", "ms", (out, c), [out], [], vcost(out, out, 0.5 if two(out) else 1))

    def scan(out, d0, d1, o0, o1):
        add("v", "scan", (out, d0, d1, 0.0, o0, o1), [out], [d0, d1], vcost(out, d0, 1))

    def tr(out, a):
        add("v", "tr", (out, a), [out], [a], vcost(out, a, 0.5 if two(out) else 1))

    def act(out, a, f, bias=0.0, scale=1.0, more=0):
        c = (65, cnt(out), "g") if a[0] == "ind" else (50 + more, max(64, cnt(out)), "c")
        add("a", "act", (out, a, f, bias, scale), [out], [a, bias, scale], c)

    def mm(out, l, r, st=True, sp=True):
        add("t", "mm", (out, l, r, st, sp), [out], [l, r], (8, max(64, cnt(r)) * (4 if SB[r[0]][1] == F else 1), "p"))

    def iota(out, pat, base, cm):
        add("g", "iota", (out, pat, base, cm), [out], [], (0, 156 + 2 * cnt(out), "c"))

    def asel(out, a, pat, op, base, cm, fill=0.0):
        add("g", "asel", (out, a, pat, op, fill, base, cm), [out], [a], (0, 205 + 2 * cnt(out), "c"))

    def gcp(out, a):
        asel(out, a, [[0, cnt(out)]], AL.is_ge, 0, 0)

    nd = [0]

    def dma(q, out, a, t, after=None, acc=False, sem=None):
        ins = [a] + ([after] if after else []) + ([out] if acc else [])
        if sem is None:
            sem = ("d%d" % nd[0], 16)
            nd[0] += 1
        add(q, "dma", (out, a, acc), [out], ins, (1000, 0, "c") if q == "g" else (0, 1, "i"),
            {"sem": sem[0], "val": sem[1], "lat": t - 1900})

    def send(dst, src, sem, gone, t, more=0):
        srcs = list(src) if isview(src[0]) else [src]
        ne = ENG if t >= 0 else FENG
        sid = add("g", "send", (dst, src, sem, t, gone), [], srcs, (400, 0, "c"), {"lat": 600 + more})
        add("r", "recv", (), [dst], [], (0, 0, "c"), {"sem": sem, "val": ne, "from": sid})
        add("r", "recv", (), [(gone, 0, 1, 1)], srcs, (0, 0, "c"), {"sem": gone, "val": ne, "from": sid})

    rot = [0]

    def bank():
        rot[0] += 1
        some = cfg["bk3"] if tag[0][:2] == "D3" else cfg["bk"]
        return "p" + some[rot[0] % len(some)]

    pcs = [[pieces(x) for x in y] for y in cfg["pc"]]
    relu = [any(p[2] == "r" for t in range(RO) for p in pcs[t][st]) for st in range(2)]
    relue = any(p[2] == "r" for t in range(RO) for p in pcs[t][1] if cfg["pm"][t] == "e")
    xen = [max([p[1] for st in range(2) for p in pcs[t][st] if p[2] != "k"] + [0]) for t in range(RO)]

    def chunks(t, st):
        cuts = (0,) + tuple(cfg["cut"][t][st]) + (NL[t],)
        return [(cuts[c], cuts[c + 1]) for c in range(len(cuts) - 1)]

    XO = (0, 2560, 6656, 6656 + 2560) if cfg["x23"] else (0, 2560, 6656, 10752)

    def xl(t, a, b, s=1):
        return V("kk", QL[t] + a, QL[t] + b, s)
    dma("a", xl(0, 0, 2 * S), V("xs", 0, 2 * S), 2100)
    dma("s", V("sti"), V("st", 0, 16), 2000)
    dma("s", V("nbi"), V("nb", 0, 1024), 2900)
    dma("s", V("kk", 0, 1024), V("kq", 0, 1024), 3300)
    dma("s", V("dli"), V("dl", 0, 1024), 4100)
    dma("s", V("ce", HD, LO[0]), V("cc", 0, 3072), 5300)
    dma("s", V("yb"), V("ys", 0, 640), 5600)
    dma("s", xl(2, 0, S), V("xs", 2 * S, 3 * S), 5800)
    dma("s", xl(3, 0, S), V("xs", 3 * S, 4 * S), 5900)
    if cfg["x23"]:
        dma("s", V("xb"), V("xs", 2 * S, 4 * S), 6000)
    for o in ops:
        o["x"]["load"] = True
    iota(C("pi", 0), [[0, 1]], 0, 1)
    ms(V("ones"), 1.0)
    asel(V("iw"), V("ones"), [[1, 160]], AL.is_equal, -16, -1)
    asel(V("bt"), V("ones", 0, 128), [[-16, 8], [0, 16]], AL.is_ge, 0, 1)
    asel(V("bo"), V("bt"), [[16, 8], [0, 16]], AL.is_ge, 15, -1)
    iota(V("cix"), [[15, 16], [1, 16]], 0, 0)
    iota(V("iob"), [[1, 256]], 0, 0)
    ts(C("pi", 1), C("pi", 0), 15, AL.bitwise_and)
    kc, odd, even, k64 = (C("col", j) for j in range(4))
    if cfg["ug"] < 4:
        ts(C("pi", 2), C("pi", 0), 4, AL.arith_shift_right, 1, AL.bitwise_and)
        cp(V("col", 0, 2), V("pi", 1, 3))
        act(even, odd, AF.Identity, 1.0, -1.0)
    else:
        cp(kc, C("pi", 1))
    act(k64, kc, AF.Identity, -960.0, 64.0)
    if not cfg["seld"] or cfg["ctm"] != "d":
        iota(V("i16"), [[1, 16]], 0, 0)
        ts(V("rm"), V("i16"), kc, AL.is_equal)
    ms(V("w0"), 0.0)
    act(V("w0", 15, 143, 16), V("bo", 0, 128, 16), AF.Copy)
    fold = any(p[2] in "fF" for t in range(RO) for p in pcs[t][0])
    if relu[0] or cfg["fixr"] or fold:
        ts(V("wn1"), V("w0"), -32768.0, AL.mult)
    if fold:
        act(V("wp1"), V("w0"), AF.Copy, 0.0, 32768.0)
        act(V("wp2"), V("w0"), AF.Copy, 0.0, 65536.0)
        act(V("nb1"), V("bo"), AF.Copy, 0.0, -32768.0)
    if relu[1]:
        ts(V("wn2"), V("w0"), -65536.0, AL.mult)
    if relue:
        ts(V("nbo"), V("bo"), -65536.0, AL.mult)
    i32 = V("iw", 16, 144)
    for j, (w, val) in enumerate((("iy", 0.25), ("iq", -0.25), ("nib", -1.0), ("ib", 1.0))):
        if w == "iy" and cfg["acm"] == "v":
            continue
        if j < cfg["ig"]:
            asel(V(w), V("bt"), [[1, 128]], AL.is_gt, -200, 0)
            asel(V(w), V(w), [[1, 128]], AL.not_equal, 0, -1, val)
        else:
            act(V(w), i32, AF.Copy, 0.0, val)
    for j, (w, par) in enumerate((("u0", 1), ("u1", 0), ("u0b", 1), ("u1b", 0))):
        if j < cfg["ug"]:
            asel(V(w), V("iw"), [[0, 5], [1, 2], [0, 16]], AL.is_equal, -par, 0)
        else:
            act(V(w), V("iw"), AF.Identity, 0.0, even if par else odd)
    for w, val, first in (("rm1", -2048.0, 3.0e7), ("rm2", -4096.0, 3.0e7), ("rmx", 4096.0, -3.0e7)):
        st = 0 if w == "rm1" else 1
        wid = max(b - a for t in range(RO - st) for a, b in chunks(t, st))
        ms(V(w, 0, wid), val)
        ms(V(w, 0, wid, 16), first)
    ms(V("zb"), 0.0)
    zero = V("ac", 0, HD)
    if cfg["zv"]:
        ms(zero, 0.0)
    else:
        iota(zero, [[0, HD]], 0, 0)
    if cfg["seld"]:
        for j in range(4):
            dma("s", V("sel", 512 * j, 512 * j + 512), V("zb"), 2300, None, False, ("wz", 64))
    for r in range(16):
        if cfg["seld"]:
            dma("s", P(V("sel", 128 * r, 128 * r + 128), r), P(V("bo"), r), 2000, None, False, ("ws", 256))
        elif r < cfg["selv"]:
            ts(V("sel", 128 * r, 128 * r + 128), V("bo"), C("rm", r), AL.mult)
        elif r < cfg["selv"] + cfg["sela"]:
            act(V("sel", 128 * r, 128 * r + 128), V("bo"), AF.Identity, 0.0, C("rm", r))
        else:
            asel(V("sel", 128 * r, 128 * r + 128), V("ones", 0, 128), [[-16, 8], [0, 16]], AL.is_equal, -r, 1)
    act(C("pw", 0), kc, AF.Exp, 21 * math.log(2.0), -math.log(2.0), 1600)
    act(V("thr"), V("cix"), AF.Exp, 121 * math.log(2.0), -math.log(2.0))
    ops[-1]["x"]["from"] = len(ops) - 2
    ts(V("ewd"), V("bo"), C("pw", 0), AL.mult)
    asel(V("lt"), V("bo"), [[1, 128]], AL.is_gt, 0, -1)
    ET = (16, 56, 120)
    iota(V("lc", 0, 16), [[16, 16]], 1, 0)
    for t in range(3):
        nb = NL[t] // 16
        iota(V("lc", ET[t], ET[t] + 4 * nb), [[-QL[t], 2], [16, nb], [0, 2]], QL[t] - 896, 0)
    act(V("lc"), V("lc"), AF.Identity, kc)
    act(V("lx", 16, 32), V("lc", 0, 16), AF.Identity, 4096.0, -1.0)
    act(V("cst", 0, 10), V("lc", 0, 10), AF.Identity, 160.0, -1.0)
    for t in range(3):
        if not cfg["fixt"]:
            asel(V("wr", 144 * t, 144 * t + 144), V("w0"), [[-1, 144]], AL.is_equal, 7 - t, 1)
        mct = NL[t] if t < 2 else S
        iota(V("iof", 256 * t, 256 * t + mct), [[1, mct]], QL[t], 0)
        ctv = V("ct", 256 * t, 256 * t + mct)
        if cfg["ctm"] == "d":
            dma("s", ctv, V("ac", 0, mct), 2300)
            dma("s", P(ctv, 8 + t), P(V("iof", 256 * t, 256 * t + mct), 8 + t), 2200)
        else:
            act(ctv, V("iof", 256 * t, 256 * t + mct), AF.Identity, 0.0, C("rm", 8 + t))
    dma("s", V("ce", S, HD), V("zb", 0, H), 2100)
    for t in range(2):
        iota(V("gx%d" % t, S, HD), [[0, H]], 16, 0)
        dma("s", V("ga%d" % t, S, HD), V("ac", 0, H), 2200)
    for a in range(1024, QL[3], HD):
        dma("s", V("ll", a, min(a + HD, QL[3])), V("ac", 0, min(HD, QL[3] - a)), 2300)
    for k in range(16):
        o, a = V("xe", k, 16 * xen[0], 16), xl(0, 0, xen[0])
        if k >= 16 - cfg["xeg"]:
            gcp(o, a)
        elif k >= cfg["xe0"]:
            act(o, a, AF.Copy)
        else:
            cp(o, a)
    cp(V("qg0"), V("sti"))
    ts(V("stm"), V("sti"), -896.0, AL.add)
    cp(V("nn", HD, HD + 1024), V("nbi"))
    cp(V("ll", 0, 1024), V("dli"))
    dma("g", V("ac", HD, LO[0]), V("aa", 0, 3072), 5000, V("kk", 0, 1024))
    ops[-1]["x"]["load"] = True
    if cfg["acm"] == "v":
        act(V("y4"), V("yb", 0, 480), AF.Copy, 0.0, 0.25)
    if any(cfg["scan"]):
        iota(V("smask"), [[0, 512]], 1, 0)
        asel(V("smask"), V("smask"), [[0, 32], [1, 16]], AL.not_equal, 0, 0)
    for k in range(16 if cfg["x23"] else 0):
        gcp(V("xe", XO[3] - 2560 + k, XO[3] + 2560, 16), V("xb"))
    for t in (1,) if cfg["x23"] else (1, 2, 3):
        for k in range(16 if xen[t] else 0):
            gcp(V("xe", XO[t] + k, XO[t] + 16 * min(xen[t], S), 16), xl(t, 0, min(xen[t], S)))

    def folds(t):
        out = []
        for a, b, mode in pcs[t][0]:
            if mode in "fF":
                if out and out[-1][1] == a and b - out[-1][0] <= cfg["fmax"]:
                    out[-1][1] = b
                else:
                    out.append([a, b, len(out)])
        return out

    def dist(t, st, pc, table, offs, ab, rl):
        a, b, mode = pc
        sc = 32768.0 * (st + 1)
        if mode == "k":
            m = b - a
            for a0 in range(a, b, cfg["gp"]):
                b0 = min(b, a0 + cfg["gp"])
                if (a0 - a) // cfg["gp"] < cfg["kv"][t][st]:
                    cp(V("graw", 16 * a0, 16 * b0), X(table, V(offs, a0, b0)))
                else:
                    act(V("graw", 16 * a0, 16 * b0), X(table, V(offs, a0, b0)), AF.Copy)
            kb = min(16, 1 << int(math.log2(512 // m)))
            for k0 in range(0, 16, kb):
                p = bank()
                for k in range(k0, k0 + kb):
                    o = V(p, (k - k0) * m, (k - k0 + 1) * m)
                    mm(o, V("ib"), V("graw", 16 * a + k, 16 * b, 16), True, False)
                    mm(o, V("nib"), xl(t, a, b), False, True)
                act(V(ab, 16 * a + k0 * m, 16 * a + (k0 + kb) * m), V(p, 0, kb * m), AF.Abs, 0.0, sc)
            return
        d, xe = V(ab, 16 * a, 16 * b), V("xe", XO[t] + 16 * a, XO[t] + 16 * b)
        if mode in "fF":
            (act if mode == "f" else cp)(*((d, X(table, V(offs, a, b))) + ((AF.Copy,) if mode == "f" else ())))
            run = [r for r in folds(t) if r[0] <= a < r[1]][0]
            if b == run[1]:
                lo, hi, j = 2560 * (t - 1) + 16 * run[0], 2560 * (t - 1) + 16 * run[1], "%d%d" % (t, run[2])
                raw = V(ab, 16 * run[0], 16 * run[1])
                more = cfg["flat"] * (run[1] - run[0])
                send(V("bn", lo, hi), (raw, V("xe", 2560 + lo, 2560 + hi)), "fa" + j, "fb" + j, -1, more)
                send(V("mx", lo, hi), V("bn", lo, hi), "fc" + j, "fd" + j, -1, more)
        elif mode == "m":
            act(d, X(table, V(offs, a, b)), AF.Copy, 0.0, -1.0)
            dma("g", d, xe, 2100 + 14 * (b - a), None, True)
            act(d, d, AF.Abs, 0.0, sc)
        elif mode == "a":
            gr = V("graw", 16 * a, 16 * b)
            act(gr, X(table, V(offs, a, b)), AF.Copy)
            for a0 in range(a, b, 32):
                p = bank()
                mm(V(p), V("ib"), V("graw", 16 * a0, 16 * a0 + 512), True, False)
                mm(V(p), V("nib"), V("xe", XO[t] + 16 * a0, XO[t] + 16 * a0 + 512), False, True)
                act(V(ab, 16 * a0, 16 * a0 + 512), V(p), AF.Abs, 0.0, sc)
        else:
            tt(d, X(table, V(offs, a, b)), xe, AL.subtract)
            if mode == "r":
                ts(V(rl, 16 * a, 16 * b), d, 0.0, AL.max, 2 * sc, AL.mult)
            else:
                act(d, d, AF.Abs, 0.0, sc)

    def key(p, t, st, c0, c1, ab, rl, num, fix=-1, d0=0):
        runs = []
        for a, b, mode in pcs[t][st]:
            mode = "e" if mode in "vam" else mode.lower()
            lo, hi = max(a, c0), min(b, c1)
            if lo >= hi:
                continue
            if runs and mode != "k" and runs[-1][2] == mode and (runs[-1][0] < d0) == (lo < d0):
                runs[-1] = (runs[-1][0], hi, mode, a, b)
            else:
                runs.append((lo, hi, mode, a, b))
        todo = []
        for lo, hi, mode, a, b in runs:
            o = V(p, lo - c0, hi - c0)
            if mode == "f":
                todo.append((o, "nb1", 15, xl(t, lo, hi)))
                todo.append((o, "wp1", fix, xl(t, lo, hi)))
            for k in range(16):
                if k == fix and lo < d0:
                    continue
                if mode == "f":
                    todo.append((o, "wn1", k, V(ab, 16 * lo + k, 16 * hi, 16)))
            for k in range(16):
                if k == fix and lo < d0:
                    continue
                if mode == "f":
                    todo.append((o, "wp2", k, V("mx", 2560 * (t - 1) + 16 * lo + k, 2560 * (t - 1) + 16 * hi, 16)))
                elif mode == "k":
                    e0 = 16 * a + k * (b - a) - a
                    todo.append((o, "w0", k, V(ab, e0 + lo, e0 + hi)))
                elif mode == "r":
                    todo.append((o, "wn%d" % (st + 1), k, V(ab, 16 * lo + k, 16 * hi, 16)))
                    todo.append((o, "w0", k, V(rl, 16 * lo + k, 16 * hi, 16)))
                else:
                    todo.append((o, "w0", k, V(ab, 16 * lo + k, 16 * hi, 16)))
        if fix >= 0 and min(c1, d0) > c0:
            e1 = min(c1, d0)
            if cfg["fixr"]:
                todo.append((V(p, 0, e1 - c0), "wn1", fix, V("dfx", c0, e1)))
                todo.append((V(p, 0, e1 - c0), "w0", fix, V("rfx", c0, e1)))
            else:
                todo.append((V(p, 0, e1 - c0), "w0", fix, V("dfx", c0, e1)))
        first = [x for x in todo if x[3][0] in ("ab1", "rl1", "mx", "kk") and fix >= 0 and x[0][2] + c0 <= d0]
        if first and c1 <= d0 and (len(runs) == 1 or cfg["eg"]):
            rest = [x for x in todo if x not in first]
            if len(runs) > 1:
                mm(V(p, 0, c1 - c0), V("ib"), V("zb", 0, c1 - c0), True, False)
            for j in range(len(first)):
                o, wn, k, r = first[j]
                mm(o, V(wn, 15 - k, 143 - k), r, j == 0 and len(runs) == 1, False)
            for o, wn, k, r in rest:
                mm(o, V(wn, 15 - k, 143 - k), r, False, False)
            mm(V(p, 0, c1 - c0), V("ib"), V(num, c0, c1), False, True)
            return
        mm(V(p, 0, c1 - c0), V("ib"), V(num, c0, c1), True, False)
        for j in range(len(todo)):
            o, wn, k, r = todo[j]
            mm(o, V(wn, 15 - k, 143 - k), r, False, j == len(todo) - 1)

    def swap(out, o0, src, s0, n, step, sfx, wide=1):
        for c1 in range(2):
            u = ("u0", "u1")[c1] + sfx
            o = V(out, o0 + c1 * wide, o0 + n * wide, 2 * wide)
            for s in range(2):
                off = 16 + 16 * (c1 - s)
                mm(o, V(u, off, off + 128), V(src, s0 + s * step, s0 + n * step, 2 * step), s == 0, s == 1)

    def flags(o0, nb):
        mm(V("p7", o0, o0 + 4 * nb, 2), V("ib"), V("zb", 0, 2 * nb))
        swap("p7", o0 + 1, "nz", 0, nb, 1, "b", 2)
        swap("p7", o0 + 1 + 2 * nb, "nz", 0, nb, 1, "b", 2)

    def pstage(t):
        tag[0] = "P%d" % t
        ab, rl = "ab2%d" % (t % 2), "rl2%d" % (t % 2)
        last = t == RO - 1
        acw = V("ac", HD, LO[t])
        viat = cfg["acm"] in "th"
        withy = cfg["acm"] == "y" and not last
        if withy:
            mm(V("p6", 0, S), V("iy"), V("yb", S * t, S * t + S), True, False)
        idm = i32 if viat else V("iq")
        po = V("pout", S * t, S * t + S)
        pe = S
        mode = cfg["pm"][t]
        if mode == "c":
            todo = []
            for j in range(16):
                for a, b, md in pcs[t][1]:
                    lo, hi = max(16 * a, S * j), min(16 * b, S * j + S)
                    if lo < hi and md == "r":
                        todo.append((j, lo, hi, "wn2", ab))
                    if lo < hi:
                        todo.append((j, lo, hi, "w0", rl if md == "r" else ab))
            mm(V("p4", 0, S), V("ib"), V("zb", 0, S), True, False)
            for x in todo:
                j, lo, hi, w, src = x
                mm(V("p4", lo - S * j, hi - S * j), V(w, 15 - j, 143 - j), V(src, lo, hi), False, x is todo[-1])
            act(V("wc"), V("p4", 0, S), AF.Exp, 0.0, -2.0 ** -22)
        if mode == "d":
            act(V("wc"), V("wq"), AF.Exp, MAGIC2 * 2.0 ** -22, -2.0 ** -22)
        if mode != "e":
            for j in range(4):
                dma("s", ("wd", j, j + 1, 1), V("wc"), 2200 + 100 * j, None, False, ("wa%d" % t, 64))
            for h in range(2):
                for j in range(4):
                    dma("s", P(V("wt", 1280 * h, 1280 * h + 1280), j, 4), ("wd", 0, 4, 1, h), 2200 + 1100 * h + 200 * j, None,
                        False, ("w%s%d" % ("bc"[h], t), 64))
        if mode == "c":
            for a, b in ((0, 64), (64, 128), (128, S)) if cfg["bigp"] else [(a, a + 32) for a in range(0, S, 32)]:
                tt(V("prod", 16 * a, 16 * b), X(acw, V("liu%d" % t, a, b)), V("wt", 16 * a, 16 * b), AL.mult)
            for a, b in ((0, cfg["pgrp"]), (cfg["pgrp"], S)):
                for k in range(16):
                    mm(V("p6", a, b), idm, V("prod", 16 * a + k, 16 * b, 16), k == 0, k == 15)
        elif mode == "d":
            tr(V("lz"), V("lih", 0, S))
            for bb in range(5):
                for c1 in range(2):
                    for s in range(2):
                        off = 16 + 16 * (c1 - s)
                        mm(V("p4", 2 * bb + c1, S, 10), V(("u0b", "u1b")[c1], off, off + 128),
                           V("lz", 32 * bb + 16 * s, 32 * bb + 16 * s + 16), s == 0, s == 1)
            ts(V("lk"), V("p4", 0, S), 2048.0 - HD, AL.add)
            ch = cfg["ch"][t]
            seg = 16 // ch
            k = 0
            for pp in cfg["pk"] if ch == 1 else [min(cfg["pp"], seg)] * (16 // min(cfg["pp"], seg)):
                tt(V("prod", S * k, S * (k + pp)), X(acw, V("lk", 10 * k, 10 * (k + pp))), V("wt", S * k, S * (k + pp)), AL.mult)
                k += pp
                if k % seg == 0 and k > seg:
                    dma("g", V("prod", 0, S * seg), V("prod", S * (k - seg), S * k), 2200 + 250 * seg, None, True)
            for _ in range(cfg["lev"][t]):
                seg //= 2
                dma("g", V("prod", 0, S * seg), V("prod", S * seg, 2 * S * seg), 2200 + 250 * seg, None, True)
            for k in range(seg):
                mm(V("p6", 0, S), idm, V("prod", S * k, S * k + S), k == 0 and not withy, k == seg - 1)
        else:
            for a in range(0, S, 32):
                pb = V("p" + cfg["bke"][a // 32 % len(cfg["bke"])]) if last else V("p4")
                if [p for p in pcs[t][1] if p[0] <= a < p[1]][0][2] == "r":
                    mm(pb, V("nbo"), V(ab, 16 * a, 16 * a + 512), True, False)
                    mm(pb, V("bo"), V(rl, 16 * a, 16 * a + 512), False, True)
                else:
                    mm(pb, V("bo"), V(ab, 16 * a, 16 * a + 512))
                act(V("wt", 16 * a, 16 * a + 512), pb, AF.Exp, 0.0, -2.0 ** -22)
                if cfg["bigp"] and a in (0, 64):
                    continue
                a0 = a - 32 if cfg["bigp"] and a in (32, 96) else a
                tt(V("prod", 16 * a0, 16 * a + 512), X(acw, V("liu%d" % t, a0, a + 32)),
                   V("wt", 16 * a0, 16 * a + 512), AL.mult)
            pe = S - 32 * cfg["scan"][t]
            grp = [(0, cfg["pgrp"]), (cfg["pgrp"], pe)] if pe > cfg["pgrp"] else [(0, pe)]
            for a, b in grp:
                if b > a:
                    for k in range(16):
                        mm(V("p6", a, b), idm, V("prod", 16 * a + k, 16 * b, 16), k == 0, k == 15)
        old = X(V("ac", 0, LO[t]), V("tu%d" % t, 2 * (NL[t] // 16), 2 * (NL[t] // 16) + 10))
        new = V("ac", LO[t], LO[t] + S)
        if not viat and not last:
            if withy:
                act(V("uu"), old, AF.Copy)
            else:
                tt(V("uu"), old, V("y4", S * t, S * t + S), AL.add)
            tt(new, V("uu"), V("p6", 0, S), AL.add)
        if pe > 0:
            act(V("pout", S * t, S * t + pe), V("p6", 0, pe), AF.Copy, 0.0, 1.0 if viat else -4.0)
        if last and 0 < pe < S:
            dma("s", V("yp", S * t, S * t + pe), V("pout", S * t, S * t + pe), 2000)
        for a in range(pe, S, 32):
            scan(V("wt", 16 * a, 16 * a + 512), V("smask"), V("prod", 16 * a, 16 * a + 512), AL.mult, AL.add)
            if cfg["pouta"]:
                act(V("pout", S * t + a, S * t + a + 32), V("wt", 16 * a + 15, 16 * a + 512, 16), AF.Copy)
            else:
                cp(V("pout", S * t + a, S * t + a + 32), V("wt", 16 * a + 15, 16 * a + 512, 16))
        o0 = pe if last and pe < S else 0
        dma("s", V("yp", S * t + o0, S * t + S), V("pout", S * t + o0, S * t + S), 2000)
        if withy:
            ops[-1]["w"].append(("out%d" % t, 0, 1, 1))
            dma("g", V("yp", S * t, S * t + S), V("yb", S * t, S * t + S), 2200, ("out%d" % t, 0, 1, 1), True)
        if last:
            return
        if viat:
            act(V("uu"), old, AF.Copy)
            mm(V("p6", 256, 256 + S), V("iy"), V("yb", S * t, S * t + S), True, False)
            if cfg["acm"] == "t":
                mm(V("p6", 256, 256 + S), i32, V("uu"), False, False)
            mm(V("p6", 256, 256 + S), V("iq"), po, False, True)
            if cfg["acm"] == "t":
                act(new, V("p6", 256, 256 + S), AF.Copy)
            else:
                tt(new, V("uu"), V("p6", 256, 256 + S), AL.add)
        if t < 2:
            cp(X(V("ga%d" % t), V("pos%d" % t, 0, 10)), new)
            a0 = LO[t + 1] + S
            send(V("ac", a0, a0 + H), V("ga%d" % t, S, HD), "ra%d" % t, "ta%d" % t, t)

    def ahead(t):
        return (NL[t] if cfg["eg"] else S) if t > 0 else 0

    for t in range(RO):
        n, nb = NL[t], NL[t] // 16
        last = t == RO - 1
        qg, liu, ab2, rl2 = "qg%d" % t, "liu%d" % t, "ab2%d" % (t % 2), "rl2%d" % (t % 2)
        nnw, llw = V("nn", HD, HD + QL[t]), V("ll", 0, QL[t])
        kkw = V("kk", 0, QL[t])
        xt = xl(t, 0, S)
        if not last:
            dma("s", V("ce", 0, S), xt, 2300)
            if n > S:
                dma("s", V("ce", S, HD), xl(t, S, n), 2200)
        d0 = ahead(t)
        tag[0] = "F%d" % t
        if d0:
            ts(V("c16", 0, d0), X(V("nn", HD, HD + QL[t - 1]), V("qg%d" % (t - 1), 0, d0 // 16)), -896.0, AL.add)
            if cfg["fixt"]:
                tr(V("cz", 0, d0), V("c16", 0, d0))
                swap("p7", 192, "cz", 7 + t, d0 // 16, 16, "b")
            for r in range(0 if cfg["fixt"] else 16):
                mm(V("p7", 192, 192 + d0 // 16), V("wr", 144 * t - 129 - r, 144 * t - 1 - r), V("c16", r, d0, 16), r == 0, r == 15)
            ts(V("fx", 0, d0 // 16), V("p7", 192, 192 + d0 // 16), 896.0, AL.add)
            for a, b in chunks(t, 0) if cfg["fsplit"][t] else [(0, d0)]:
                b = min(b, d0)
                if a >= b:
                    continue
                if cfg["fixa"][t]:
                    act(V("rfx", a, b), X(kkw, V("fx", a // 16, b // 16)), AF.Copy)
                    p = V(bank(), 0, b - a)
                    mm(p, V("nib"), xl(t, a, b), True, False)
                    mm(p, V("ib"), V("rfx", a, b), False, True)
                    act(V("dfx", a, b), p, AF.Abs, 0.0, 32768.0)
                    continue
                tt(V("dfx", a, b), X(kkw, V("fx", a // 16, b // 16)), xl(t, a, b), AL.subtract)
                if cfg["fixr"]:
                    ts(V("rfx", a, b), V("dfx", a, b), 0.0, AL.max, 65536.0, AL.mult)
                else:
                    act(V("dfx", a, b), V("dfx", a, b), AF.Abs, 0.0, 32768.0)
        for c, (c0, c1) in enumerate(chunks(t, 0)):
            b0, bn = c0 // 16, (c1 - c0) // 16
            e0 = max(c0, d0)
            tag[0] = "Q%d%d" % (t, c)
            if c1 > e0:
                cl = ("qg0", "qg0", "qg1")[t]
                cp(V("candu", e0, c1), X(V("nbi") if t == 0 else V("nn", HD, HD + QL[t - 1]), V(cl, e0 // 16, c1 // 16)))
                for pc in pcs[t][0]:
                    if e0 <= pc[0] < c1:
                        dist(t, 0, pc, kkw, "candu", "ab1", "rl1")
                ts(V("c16", e0, c1), V("candu", e0, c1), -896.0, AL.add)
            p = "p%d" % (c % 2)
            key(p, t, 0, c0, c1, "ab1", "rl1", "c16", 7 + t if d0 else -1, d0)
            tr(V("tk", c0, c1), V(p, 0, c1 - c0))
            scan(V("sc", c0, c1), V("rm1", 0, c1 - c0), V("tk", c0, c1), AL.add, AL.min)
            mn = V("sc", c0 + 15, c1, 16)
            ts(V("hz", b0, b0 + bn), mn, MAGIC, AL.add, MAGIC, AL.subtract)
            tt(V("qz", b0, b0 + bn), mn, V("hz", b0, b0 + bn), AL.subtract)
            swap("p7", b0, "qz", b0, bn, 1, "b")
            ts(V(qg, b0, b0 + bn), V("p7", b0, b0 + bn), 896.0, AL.add)
        if not last:
            cp(V("qh", 0, nb), V("p7", 0, nb))
            ts(V("qz", 16, 16 + nb), V("hz", 0, nb), 52 * 32768.0 + 1024, AL.is_ge)
            swap("p7", nb, "qz", 16, nb, 1, "b")
            swap("p7", 2 * nb, "qz", 16, nb, 1, "b")
            act(V("qf", 0, 3 * nb), V("p7", 0, 3 * nb), AF.Copy)
        for c, (c0, c1) in enumerate(chunks(t, 1)):
            b0, bn = c0 // 16, (c1 - c0) // 16
            tag[0] = "D%d%d" % (t, c)
            cp(V(liu, c0, c1), X(llw if t else V("dli"), V(qg, b0, b0 + bn)))
            for pc in pcs[t][1]:
                if c0 <= pc[0] < c1:
                    dist(t, 1, pc, V("ce", HD, LO[t]), liu, ab2, rl2)
            if last:
                continue
            ts(V("lih", c0, c1), V(liu, c0, c1), HD - 2048.0, AL.add)
            p = "p%d" % ((c + len(chunks(t, 0))) % 2)
            key(p, t, 1, c0, c1, ab2, rl2, "lih")
            tr(V("tk2", c0, c1), V(p, 0, c1 - c0))
            if cfg["pm"][t] == "d" and c0 < S:
                act(V("wq", c0, min(c1, S)), V(p, 0, min(c1, S) - c0), AF.Identity, MAGIC2)
            scan(V("sc2", c0, c1), V("rm2", 0, c1 - c0), V("tk2", c0, c1), AL.add, AL.min)
            scan(V("sc2", n + c0, n + c1), V("rmx", 0, c1 - c0), V("tk2", c0, c1), AL.add, AL.max)
        if last:
            pstage(t)
            continue
        nnq = V("nn", HD + QL[t], HD + QL[t] + n)
        act(V("lik", 0, n), X(llw, V(qg, 0, nb)), AF.Copy)
        if t == 2:
            nnq = V("nn", HD + QL[t], HD + QL[t] + S)
        act(nnq, X(nnw, V(qg, 0, cnt(nnq) // 16)), AF.Copy)
        d1 = ahead(t + 1)
        tag[0] = "E%d" % t
        if cfg["cfrom"]:
            cp(V("candu", 0, S), V("nn", HD + QL[t], HD + QL[t] + S))
        else:
            cp(V("candu", 0, S), X(nnw, V(qg, 0, 10)))
        for pc in pcs[t + 1][0]:
            if pc[1] <= S:
                dist(t + 1, 0, pc, kkw, "candu", "ab1", "rl1")

        def sm(j, w=1):
            return V("sm", 32 * j + 32, 32 * j + 32 + w * nb)
        tag[0] = "W%d" % t
        for r in range(16):
            mm(V("p5", r, n, 16), V("sel", 128 * r, 128 * r + 128), V("qh", 0, nb))
        cp(V("qr", 0, n), V("p5", 0, n))
        if t < 2:
            act(V("qrf", 0, n), V("p5", 0, n), AF.Identity, 896.0)
        mm(V("p5", 256, 256 + n), V("nib"), V("thr", 0, n), True, False)
        if n > S:
            act(V("vd"), xl(t, S, n), AF.Relu, -15.0 / 16, 1.0 / 16)
            mm(V("p5", 256 + S, 256 + n), V("bo"), V("vd"), False, False)
        for b in range(nb):
            e0 = 256 * b
            ts(V("eq", e0, e0 + n - 16 * b), V("qr", 16 * b, n), C("qf", b), AL.is_equal, 2.0 ** (99 - 15 * b), AL.mult)
            mm(V("p5", 256 + 16 * b, 256 + n), V("ewd"), V("eq", e0, e0 + n - 16 * b), False, b == nb - 1)
        act(V("winr", 0, n), V("p5", 256, 256 + n), AF.Sign, 0.0, -1.0)
        for r in range(16):
            mm(V("p5", 0, nb), V("w0", 15 - r, 143 - r), V("winr", r, n, 16), r == 0, r == 15)
        et0 = V("lc", ET[t] + 1, ET[t] + 2 * nb, 2)
        qf = V("qf", 0, nb)
        if t == 1:
            for r in range(16):
                mm(V("p5", 32, 38), V("w0", 15 - r, 143 - r), V("vd", r, H, 16), r == 0, r == 15)
        for j in range(2):
            act(V("sm", 32 + j * nb, 32 + (j + 1) * nb), V("p5", 0, nb), AF.Relu, 0.0, 1.0 / 16)
        if t == 1:
            w = V("sm", 240, 246)
            tt(w, V("qf", 10, 16), V("stm", 10, 16), AL.subtract)
            tt(w, w, V("p5", 32, 38), AL.mult)
            tt(w, V("qf", 10, 16), w, AL.subtract)
            ts(V(qg, 10, 16), w, 896.0, AL.add)
        if t < 2:
            tt(V("sm", 22, 32), V("sm", 32, 42), V("lc", 0, 10), AL.mult)
            if d1 > S:
                cp(V("candu", S, HD), X(nnw, V(qg, 10, 16)))
        tt(sm(1), et0, qf, AL.subtract)
        act(V("sm", 64 + nb, 64 + 2 * nb), sm(1), AF.Identity, float(QL[t] + HD), -1.0)
        tt(sm(2, 2), sm(1, 2), sm(0, 2), AL.mult)
        tt(et0, et0, sm(2), AL.subtract)
        tt(V("lc", ET[t], ET[t] + 4 * nb, 2), sm(2, 2), V("qf", nb, 3 * nb), AL.mult)
        th = 37 * 65536.0 - 63488.0
        if t < 2:
            tag[0] = "G%d" % t
            ts(V("nz", 0, 10), V("sc2", 15, S, 16), th, AL.is_ge)
            flags(320, 10)
            tt(V("nw", 0, 20), V("sm", 22, 42), V("p7", 321, 360, 2), AL.mult)
            mm(V("p7", 176, 186), V("ib"), V("cst", 0, 10), True, False)
            mm(V("p7", 176, 186), V("ib"), V("nw", 0, 10), False, False)
            mm(V("p7", 176, 186), V("lt"), V("nw", 10, 20), False, False)
            for s in range(1, 10):
                mm(V("p7", 176 + s, 186), V("bo"), V("nw", 10, 20 - s), False, s == 9)
            ts(V("pos%d" % t, 0, 10), V("p7", 176, 186), 0.0, AL.add)
            gx = "gx%d" % t
            cp(X(V(gx), V("pos%d" % t, 0, 10)), xt)
            send(xl(t + 1, S, HD), V(gx, S, HD), "rx%d" % t, "tx%d" % t, t)
            tag[0] = "X%d" % t
            g0 = min([p[0] for st in range(2) for p in pcs[t + 1][st] if p[2] != "k" and p[0] >= S] + [HD])
            for k in range(16 if g0 < HD else 0):
                gcp(V("xe", XO[t + 1] + 16 * g0 + k, XO[t + 1] + 16 * xen[t + 1], 16), xl(t + 1, g0, xen[t + 1]))
            tag[0] = "H%d" % t
            for pc in pcs[t + 1][0]:
                if S < pc[1] <= d1:
                    dist(t + 1, 0, pc, kkw, "candu", "ab1", "rl1")
        tag[0] = "L%d" % t
        tu = "tu%d" % t
        z0 = 10 if t < 2 else 0
        if nb > z0:
            ts(V("nz", z0, nb), V("sc2", 16 * z0 + 15, n, 16), th, AL.is_ge)
            flags(256, nb)
        n0 = 256 if nb > z0 else 320
        nu = V("p7", n0 + 1, n0 + 4 * nb, 2)
        scan(V("sm", 160, 160 + 4 * nb), V("p7", n0, n0 + 4 * nb), V("lc", ET[t], ET[t] + 4 * nb), AL.mult, AL.add)
        ts(V(tu, 0, 2 * nb), V("sm", 161, 160 + 4 * nb, 2), 896.0, AL.add)
        m = n if t < 2 else S
        tt(X(V("nn", 0, HD + QL[t]), V(tu, nb, nb + m // 16)), V("nn", HD + QL[t], HD + QL[t] + m),
           V("ct", 256 * t, 256 * t + m), AL.max)
        if t < 2:
            dma("s", P(nnq, t), P(V("qrf", 0, n), t), 2200)
        swap("p5", 0, "sc2", 15, 2 * nb, 16, "")
        act(V("rr", 0, nb), V("p5", 0, nb), AF.Relu, th - 1.0, -1.0)
        act(V("lx", 16 - nb, 16), V("p5", nb, 2 * nb), AF.Identity, 2048.0)
        tt(V("mi", 0, 2 * nb), V("lx", 16 - nb, 16 + nb), nu, AL.mult)
        tt(V("mi", nb, 2 * nb), V("mi", nb, 2 * nb), V("rr", 0, nb), AL.add)
        ts(V("ti", 0, nb), V("mi", nb, 2 * nb), 4095, AL.bitwise_and)
        ts(V(tu, 2 * nb, 3 * nb), V("ti", 0, nb), -1.0, AL.mult, 4095.0, AL.add)
        ts(V("kab", 0, 2 * nb), V("mi", 0, 2 * nb), 12, AL.arith_shift_right, 15, AL.bitwise_and)
        tt(V("ks", 0, nb), V("kab", 0, nb), V("kab", nb, 2 * nb), AL.add)
        for r in range(16):
            mm(V("p5", r, n, 16), V("sel", 128 * r, 128 * r + 128), V("ks", 0, nb))
        act(V("sq", 0, n), V("p5", 0, n), AF.Square, k64, 64.0)
        mm(V("p5", 256, 256 + n), V("ib"), V("iob", 0, n), True, False)
        mm(V("p5", 256, 256 + n), V("nib"), V("sq", 0, n), False, True)
        act(V("zz", 0, n), V("p5", 256, 256 + n), AF.Identity, float(LO[t] - HD))
        tt(X(V("ll", 0, QL[t] + n), V(tu, 0, nb)), V("zz", 0, n), V("lik", 0, n), AL.max)
        act(V("ce", LO[t], LO[t] + n), X(V("ce", 0, LO[t]), V(tu, 2 * nb, 3 * nb)), AF.Copy)
        pstage(t)
    return ops


def graph(cfg):
    ops = build(cfg)
    n = len(ops)
    seen = {}
    before = {}
    for i in range(n):
        o = ops[i]
        deps = {}
        acc = [(v, False) for v in o["r"] if v[0] not in DRAM] + [(v, True) for v in o["w"] if v[0] not in DRAM]
        for v, w in acc:
            lst = seen.setdefault(v[0], [])
            if psum(v):
                if lst and ops[lst[0][0]]["e"] != o["e"]:
                    before[v[0]] = [e[0] for e in lst]
                    lst[:] = []
                for j in before.get(v[0], ()):
                    deps[j] = True
            for j, u, uw in lst:
                if (w or uw) and meet(u, v):
                    deps[j] = True
        for v, w in acc:
            lst = seen[v[0]]
            if w and v[3] == 1 and len(v) == 4 and not psum(v):
                lst[:] = [e for e in lst if not (e[1][1] >= v[1] and e[1][2] <= v[2])]
            lst.append((i, v, w))
        deps.pop(i, None)
        o["d"] = sorted(deps)
        o["s"] = list(o["d"]) + ([o["x"]["from"]] if "from" in o["x"] else [])
    lastmm = {}
    for i in range(n):
        o = ops[i]
        if o["k"] == "mm":
            b = o["w"][0][0]
            if b in lastmm:
                o["s"].append(lastmm[b])
            lastmm[b] = i
        o["s"] = sorted(set(o["s"]))
        o["h"] = set(o["d"])
    return ops


def cost(o, m):
    return o["m"][0] + o["m"][1] * m[o["m"][2]]


def late(o, m):
    return 1900.0 * m["d"] + o["x"]["lat"] if "lat" in o["x"] else 0.0


def gap(o, q, i, m):
    if q["e"] == o["e"]:
        return 0.0 if o["e"] == "t" or i not in q["h"] else m["y"]
    return m["x"]


def schedule(full, cfg, m):
    ops, of, last = [], [], {}
    for i in range(len(full)):
        o = full[i]
        if o["k"] == "mm":
            b = o["w"][0][0]
            ext = set(j for j in o["s"] if full[j]["e"] != "t")
            z = last.get(b)
            if (z is not None and full[i - 1]["k"] == "mm" and of[i - 1] == z and ext <= ops[z]["ext"]
                    and ops[z]["m"][1] < cfg["tmax"]):
                q = ops[z]
                q["m"] = (q["m"][0] + o["m"][0], q["m"][1] + o["m"][1], "p")
                q["sub"].append(i)
                q["s"] = sorted(set(q["s"]) | set(of[j] for j in o["s"] if of[j] != z))
                of.append(z)
                continue
            last[b] = len(ops)
        of.append(len(ops))
        ops.append({"e": o["e"], "k": o["k"], "m": o["m"], "x": o["x"], "g": o["g"], "sub": [i], "s": sorted(set(of[j] for j in o["s"])),
                    "h": set(of[j] for j in o["h"]), "ext": set(j for j in o["s"] if full[j]["e"] != "t")})
    n = len(ops)
    anc = []
    for i in range(n):
        far = 0
        for j in ops[i]["s"]:
            far |= anc[j]
        ops[i]["s"] = [j for j in ops[i]["s"] if not far >> j & 1]
        for j in ops[i]["s"]:
            far |= 1 << j
        anc.append(far)
    succ = [[] for _ in range(n)]
    for i in range(n):
        for j in ops[i]["s"]:
            succ[j].append(i)
    cs = [cost(o, m) for o in ops]
    tl = [late(o, m) for o in ops]
    pr = [0.0] * n
    for i in range(n - 1, -1, -1):
        pr[i] = cs[i] + tl[i] + max([m["x"] + pr[j] for j in succ[i]] + [0.0])
    fw = [[(j, tl[i] + gap(ops[i], ops[j], i, m)) for j in succ[i]] for i in range(n)]
    bw = [[(j, tl[j] + gap(ops[j], ops[i], j, m)) for j in ops[i]["s"]] for i in range(n)]
    eng = [o["e"] for o in ops]
    tabs = [([cost(o, q) for o in ops], [late(o, q) for o in ops],
             [[(j, gap(ops[j], ops[i], j, q)) for j in ops[i]["s"]] for i in range(n)]) for q in SETS]

    def value(seq):
        tot = 0.0
        for c, lat, pre in tabs:
            free, fin, end = {}, [0.0] * n, 0.0
            for i in seq:
                s = free.get(eng[i], 0.0)
                for j, w in pre[i]:
                    if fin[j] + w > s:
                        s = fin[j] + w
                free[eng[i]] = s + c[i]
                fin[i] = s + c[i] + lat[i]
                if fin[i] > end:
                    end = fin[i]
            tot += end
        return tot

    def sweep(pri, nxt, prv, first):
        left = [len(x) for x in prv]
        ready = list(first)
        if nxt is fw:
            pri = [1e9 - i if "load" in ops[i]["x"] else pri[i] for i in range(n)]
        pool = {}
        for i in range(n):
            if left[i] == 0:
                pool.setdefault(eng[i], []).append(i)
        free, seq, st = {}, [], [0.0] * n
        for _ in range(n):
            best = None
            for e in pool:
                if pool[e]:
                    t0 = max(free.get(e, 0.0), min([ready[i] for i in pool[e]]))
                    if best is None or t0 < best[0]:
                        best = (t0, e)
            t0, e = best
            top = i = -1
            for j in pool[e]:
                if top < 0 or pri[j] > pri[top]:
                    top = j
                if ready[j] <= t0 + 1e-6 and (i < 0 or pri[j] > pri[i]):
                    i = j
            if top != i and ready[top] - t0 < cfg["look"] * cs[i]:
                i = top
            st[i] = max(free.get(e, 0.0), ready[i])
            pool[e].remove(i)
            free[e] = st[i] + cs[i]
            seq.append(i)
            for j, lat in nxt[i]:
                ready[j] = max(ready[j], free[e] + lat)
                left[j] -= 1
                if left[j] == 0:
                    pool.setdefault(eng[j], []).append(j)
        return seq, st

    names = sorted(set(eng))
    en = [names.index(e) for e in eng]
    sinks = [i for i in range(n) if not succ[i]]

    def timing(seq, tab, a=0, old=None):
        c, lat, pre = tab
        free, last = [0.0] * len(names), [-1] * len(names)
        if old is None:
            fin, par = [0.0] * n, [-1] * n
        else:
            fin, par = old[3][:], old[1][:]
            k, miss = a - 1, len(names)
            while k >= 0 and miss:
                i = seq[k]
                if last[en[i]] < 0:
                    last[en[i]], free[en[i]] = i, fin[i] - lat[i]
                    miss -= 1
                k -= 1
        for i in seq[a:]:
            e = en[i]
            s, p = free[e], last[e]
            for j, w in pre[i]:
                if fin[j] + w > s:
                    s, p = fin[j] + w, j
            s += c[i]
            free[e], last[e], par[i] = s, i, p
            fin[i] = s + lat[i]
        top = max(sinks, key=lambda i: fin[i])
        return fin[top] + cfg["wmean"] * sum(fin) / n, par, top, fin

    def polish(seq, steps, heat):
        prs = [set(o["s"]) for o in ops]
        res = [timing(seq, tab) for tab in tabs]
        val = sum(r[0] for r in res)
        keep = (val, seq)
        for it in range(steps):
            temp = heat * (1.0 - it / steps)
            _, par, i, _ = res[rs.randint(len(res))]
            if rs.uniform() < cfg["pany"]:
                i = rs.randint(n)
            cand = []
            while i >= 0:
                p = par[i]
                if p >= 0 and eng[p] == eng[i] and p not in prs[i] and "load" not in ops[p]["x"]:
                    cand.append((p, i))
                i = p
            if not cand:
                continue
            p, i = cand[rs.randint(len(cand))]
            a, b = seq.index(p), seq.index(i)
            e = eng[i]
            hop = rs.randint(4)
            if rs.uniform() < 0.5:
                while hop and a > 0 and "load" not in ops[seq[a - 1]]["x"]:
                    a -= 1
                    hop -= eng[seq[a]] == e
                mark, engs, move = set(prs[i]), set(), [i]
                for k in range(b - 1, a - 1, -1):
                    j = seq[k]
                    if j in mark or eng[j] in engs:
                        move.append(j)
                        mark |= prs[j]
                        engs.add(eng[j])
                ms = set(move)
                new = seq[:a] + move[::-1] + [j for j in seq[a:b + 1] if j not in ms] + seq[b + 1:]
            else:
                while hop and b < n - 1:
                    b += 1
                    hop -= eng[seq[b]] == e
                ms, engs, move = {p}, set(), [p]
                for k in range(a + 1, b + 1):
                    j = seq[k]
                    if eng[j] in engs or not ms.isdisjoint(prs[j]):
                        move.append(j)
                        ms.add(j)
                        engs.add(eng[j])
                new = seq[:a] + [j for j in seq[a:b + 1] if j not in ms] + move + seq[b + 1:]
            if new == seq:
                continue
            lim = -temp * math.log(1.0 - rs.uniform())
            r2 = [timing(new, tabs[0], a, res[0])]
            if r2[0][0] - res[0][0] > lim + cfg["slack"]:
                continue
            r2 += [timing(new, tabs[k], a, res[k]) for k in range(1, len(tabs))]
            v2 = sum(r[0] for r in r2)
            if v2 <= val + lim:
                seq, res, val = new, r2, v2
                if val < keep[0]:
                    keep = (val, seq)
        return keep[1]

    tags = sorted(set(o["g"] for o in ops))
    pr0 = list(pr)
    rs = np.random.RandomState(cfg["seed"])
    best = None
    for _ in range(cfg["iters"] + 1):
        seq, st = sweep(pr, fw, bw, [0.0] * n)
        val = value(seq)
        if best is None or val < best[0]:
            best = (val, seq, st)
        z = rs.standard_normal(n) * cfg["noise"]
        back = sweep([st[i] + cs[i] + float(z[i]) for i in range(n)], bw, fw, tl)[1]
        pr = [back[i] + cs[i] for i in range(n)]
    if cfg.get("warm"):
        pw = []
        for i in range(n):
            z = cfg["warm"].get(full[ops[i]["sub"][0]]["sig"])
            pw.append(z if z is not None else max([pw[j] + cs[j] for j in ops[i]["s"]] + [0.0]))
        for i in range(n):
            pw[i] = max([pw[i]] + [pw[j] + 1e-3 for j in ops[i]["s"]])
        seq = sorted(range(n), key=lambda i: pw[i])
        fin = timing(seq, tabs[0])[3]
        st = [fin[i] - cs[i] - tl[i] for i in range(n)]
        val = value(seq)
        if val < best[0]:
            best = (val, seq, st)
    if cfg["phs"]:
        shift = {z: cfg["boost"].get(z, 0.0) for z in tags}
        now = None
        main = [z for z in tags if z[0] in "FQDEWGHLP" and z[1:].isdigit()]
        for it in range(cfg["phs"]):
            new = dict(shift)
            for _ in range(1 + rs.randint(2) if it else 0):
                some = main if rs.uniform() < 0.8 else tags
                new[some[rs.randint(len(some))]] += float(rs.standard_normal()) * (500.0, 2000.0, 5000.0)[rs.randint(3)]
            seq, st = sweep([pr0[i] + new[ops[i]["g"]] for i in range(n)], fw, bw, [0.0] * n)
            val = value(seq)
            if now is None or val <= now - cfg["ptemp"] * (1.0 - it / cfg["phs"]) * math.log(1.0 - rs.uniform()):
                now, shift = val, new
            if val < best[0]:
                best = (val, seq, st)
        if "out" in cfg:
            cfg["out"].update(shift)
            cfg["out"]["_v"] = now
    for _ in range(cfg["ils"]):
        t0, wd, sg = rs.uniform(0, 85000), rs.uniform(3000, 15000), (200.0, 600.0, 1500.0)[rs.randint(3)]
        z = rs.standard_normal(n) * sg
        keep = rs.uniform(size=n) < rs.uniform(0.1, 1.0)
        pri = [-best[2][i] + (float(z[i]) if keep[i] and t0 <= best[2][i] < t0 + wd else 0.0) for i in range(n)]
        if rs.uniform() < cfg["ptag"]:
            mv = {tags[rs.randint(len(tags))]: float(rs.standard_normal()) * 5000.0 for _ in range(1 + rs.randint(2))}
            pri = [-best[2][i] + mv.get(ops[i]["g"], 0.0) for i in range(n)]
        seq, st = sweep(pri, fw, bw, [0.0] * n)
        if rs.uniform() < 0.3:
            back = sweep([st[i] + cs[i] for i in range(n)], bw, fw, tl)[1]
            seq, st = sweep([back[i] + cs[i] for i in range(n)], fw, bw, [0.0] * n)
        val = value(seq)
        if val <= best[0]:
            best = (val, seq, st)
    seq = polish(best[1], cfg["sa"], cfg["temp"])
    seq = polish(seq, cfg["sa2"], cfg["temp2"])
    return [j for i in seq for j in ops[i]["sub"]]


def replay(ops, seq, m):
    free, fin, end = {}, {}, 0.0
    for i in seq:
        o = ops[i]
        s = free.get(o["e"], 0.0)
        for j in o["s"]:
            s = max(s, fin[j] + gap(ops[j], o, j, m))
        free[o["e"]] = s + cost(o, m)
        fin[i] = free[o["e"]] + late(o, m)
        end = max(end, fin[i])
    return end


def plan(cfg):
    ops = graph(cfg)
    order = {}
    seq = schedule(ops, cfg, NOM)
    for i in seq:
        order.setdefault(ops[i]["e"], []).append(i)
    place = {}
    for e in order:
        for k in range(len(order[e])):
            place[order[e][k]] = k
    marked = {}
    gots = {e: {} for e in order}
    knew = {}

    def learn(got, j):
        if cfg["prune"]:
            for f, z in knew[j].items():
                got[f] = max(got.get(f, -1), z)

    for i in seq:
        o = ops[i]
        e = o["e"]
        got = gots[e]
        need = {}
        o["wo"], o["wq"] = [], []
        for j in o["d"]:
            q = ops[j]
            if "sem" not in q["x"] and not (e == "t" and q["e"] == "t"):
                need[q["e"]] = max(need.get(q["e"], -1), place[j])
        last = [order[f][need[f]] for f in need if need[f] > got.get(f, -1)]
        for j in sorted(last, key=lambda j: -knew[j].get("n", 0)):
            f = ops[j]["e"]
            if place[j] > got.get(f, -1):
                got[f] = place[j]
                marked[j] = True
                o["wq"].append(j)
                learn(got, j)
        for j in o["d"]:
            q = ops[j]
            if "sem" in q["x"] and q["x"]["sem"] not in got:
                got[q["x"]["sem"]] = 0
                o["wo"].append(j)
                if q["k"] == "dma":
                    learn(got, j)
        got["n"] = max(got.get("n", 0), len(knew))
        knew[i] = dict(got)
    for e in order:
        c = 0
        for i in order[e]:
            if i in marked:
                c += 1
                ops[i]["n"] = c
    return ops, order


PLAN = []
QSEM = {"v": "sv", "a": "sa", "t": "sp", "g": "sg"}


def rank_program(g, core, T, topo):
    rank = T.rank_of(core)
    if rank is None:
        return
    if not PLAN:
        PLAN.append(plan(CFG))
    ops, order = PLAN[0]
    nr = len(T.cores)
    qs = {"v": g.vector, "a": g.scalar, "t": g.tensor, "g": g, "s": g.sync}

    def ap(v):
        if not isview(v):
            return v
        if v[0] == "ind":
            return ap(v[1]).indirect(ap(v[2]))
        if v[0] == "wd":
            return T.wd[:, v[1], :] if len(v) == 4 else T.wd[:, :, 1280 * v[4]:1280 * v[4] + 1280]
        if len(v) > 4:
            return T[v[0]][v[4][0]:v[4][1]:v[4][2], v[1]:v[2]]
        if v[3] == 1:
            return T[v[0]][:, v[1]:v[2]]
        return T[v[0]][:, v[1]:v[1] + (cnt(v) - 1) * v[3] + 1:v[3]]

    for e in ("s", "g", "v", "a", "t"):
        q = qs[e]
        for i in order[e]:
            o = ops[i]
            for j in o["wo"]:
                q.wait_ge(T.sem[ops[j]["x"]["sem"]], ops[j]["x"]["val"])
            for j in o["wq"]:
                q.wait_ge(T.sem[QSEM[ops[j]["e"]]], ops[j]["n"])
            k = o["k"]
            if k == "send" and o["a"][3] < 0:
                near = [c for c in topo.cores_of(core) if topo.die(c) == topo.die(core)]
                dst = near[near.index(core) ^ 1]
                rid, pid, _ = topo.addr(dst)
                mask = sum(1 << x for x in topo.engines(core, dst)[slice(*CFG["feng"])])
                if isview(o["a"][1][0]):
                    g.remote_dma_fused([RemoteDMATransfer(dst_ids=[DstId(rid=rid, pnc=pid)], dma_engine_mask=mask,
                                                          remote_sem=T.sem[o["a"][2]], srcs=[ap(v) for v in o["a"][1]],
                                                          dsts=[ap(o["a"][0])], alu_op=2)], local_sem=T.sem[o["a"][4]])
                else:
                    g.remote_dma(ap(o["a"][0]), ap(o["a"][1]), T.sem[o["a"][2]], T.sem[o["a"][4]], pid, rid, mask)
                continue
            if k == "send":
                dst = T.cores[(rank + 1 + o["a"][3] % (nr - 1)) % nr]
                rid, pid, _ = topo.addr(dst)
                mask = sum(1 << x for x in topo.engines(core, dst)[slice(*CFG["eng"])])
                g.remote_dma(ap(o["a"][0]), ap(o["a"][1]), T.sem[o["a"][2]], T.sem[o["a"][4]], pid, rid, mask)
                continue
            a = [ap(v) for v in o["a"]]
            if k == "dma":
                ins = q.dma_start(a[0], a[1], accum_op=AL.add) if a[2] else q.dma_start(a[0], a[1])
                ins.then_inc(T.sem[o["x"]["sem"]], 16)
                continue
            if k == "cp":
                ins = q.tensor_copy(a[0], a[1])
            elif k == "tt":
                ins = q.tensor_tensor(a[0], a[1], a[2], a[3])
            elif k == "ts":
                ins = q.tensor_scalar(a[0], a[1], a[2], None, a[4]) if a[5] is None else q.tensor_scalar(*a)
            elif k == "ms":
                ins = q.memset(a[0], a[1])
            elif k == "scan":
                ins = q.tensor_tensor_scan(*a)
            elif k == "tr":
                ins = q.transpose(a[0], a[1])
            elif k == "act":
                ins = q.activation(a[0], a[1], a[2], bias=a[3], scale=a[4])
            elif k == "mm":
                ins = q.matmul(*a)
            elif k == "iota":
                if SB[o["a"][0][0]][1] == I:
                    ins = q.iota(*a)
                else:
                    ins = q.iota(*a, allow_small_or_imprecise_dtypes=True)
            else:
                ins = q.affine_select(*a)
            if "n" in o:
                ins.then_inc(T.sem[QSEM[e]], 1)
    for o in ops:
        if o["k"] == "send":
            g.wait_ge(T.sem[o["a"][4]], ENG if o["a"][3] >= 0 else FENG)
        if o["k"] == "dma" and o["a"][0][0] == "yp":
            g.sync.wait_ge(T.sem[o["x"]["sem"]], 16)
